import numpy as np, ml_dtypes
CORES = [48,51,52,55]
N = 4
BF = ml_dtypes.bfloat16
W, K, E, TH, ST, RO = 8192, 256, 32, 9, 1, 6
def subset(rng, cnt):
    a = 2 * rng.integers(0, 8, cnt.shape) + 1; o = rng.integers(0, 16, cnt.shape)
    return (((a * np.arange(16)[:, None] + o) & 15) < cnt).astype(np.int16)
def parts(rng):
    x = rng.integers(0, 256, (N, 8, 1, W), dtype=np.int16) + rng.integers(-12, 13, (N, 8, 16, W), dtype=np.int16)
    x = np.where(rng.random((N, 8, 1, W)) < 0.125, rng.integers(0, 256, (N, 8, 16, W), dtype=np.int16), np.clip(x, 0, 255))
    stk = rng.integers(0, W, (N, 8, 16, K)); bas = rng.integers(0, W, (N, 8, 16, K)); con = rng.integers(0, W, (N, 8, 16, K)); ln = rng.integers(1, 16, (N, 8, K))
    lv = (255.0 * (1.0 - rng.random((N, 8, 1, K)) ** 2)).astype(np.int64)
    z = np.clip(lv + rng.integers(-12, 13, (N, 8, 16, K)), 0, 255); w = rng.integers(1, 258, (N, 8, 16, 1))
    return x, stk, bas, con, ln, z, w
def pack(x, stk, bas, con, ln, z, w):
    def t(a, n): return np.ascontiguousarray(np.reshape(a, (N, 128, n)))
    return {"xt": t(x, W).astype(np.float32).astype(BF), "stk": t(stk, K).astype(np.int32), "bas": t(bas, K).astype(np.int32), "con": t(con, K).astype(np.int32),
            "ln": np.ascontiguousarray(ln).astype(np.int32), "z": t(z, K).astype(np.float32).astype(BF), "w": t(w, 1).astype(np.int32)}
def setup_inputs(rng):
    return pack(*parts(rng))
def setup_inputs_spread(rng):
    x, stk, bas, con, ln, z, w = parts(rng)
    x = (np.exp2(8.0 * rng.random((N, 8, 1, W), dtype=np.float32)) * rng.random((N, 8, 16, W), dtype=np.float32)).astype(np.int16)
    x = np.minimum(x, 255) * (rng.random((N, 8, 1, W)) > 0.0625)
    z = np.minimum((np.exp2(8.0 * rng.random((N, 8, 1, K))) * rng.random((N, 8, 16, K))).astype(np.int64), 255)
    def skew(lo, n, shape):
        e = rng.choice(np.array([0.25, 1.0, 4.0]), (N, 8) + (1,) * (len(shape) - 2))
        return np.minimum(lo + (n * rng.random(shape) ** e).astype(np.int64), lo + n - 1)
    stk = skew(0, W, (N, 8, 16, K)); bas = skew(0, W, (N, 8, 16, K)); con = skew(0, W, (N, 8, 16, K)); ln = skew(1, 15, (N, 8, K))
    w = np.minimum(np.exp2(8.01 * rng.random((N, 8, 16, 1))).astype(np.int64), 257)
    return pack(x, stk, bas, con, ln, z, w)
def endnames(rng):
    a = (W - 1) * rng.integers(0, 2, (N, 8, 16, K))
    s = (W - 1) * ((np.arange(16)[:, None] >= rng.integers(0, 17, (N, 8, 1, K))).astype(np.int64) ^ rng.integers(0, 2, (N, 8, 1, K)))
    ty = rng.random((N, 8, 1, K))
    return np.where(ty < 0.4, a, np.where(ty < 0.75, s, rng.integers(0, W, (N, 8, 16, K))))
def setup_inputs_ends(rng):
    cnt = rng.choice(np.array([0, 1, TH - 2, TH - 1, TH, 12, 16]), (N, 8, 1, W)); cnt[1] = np.minimum(cnt[1], TH - 2)
    x = 255 * subset(rng, cnt)
    zc = rng.choice(np.array([0, 1, 3, TH - 1, TH, 12]), (N, 8, 1, K)); zc[0] = rng.choice(np.array([TH, 12, 15]), (8, 1, K)); zc[1] = 1
    z = 255 * (1 - subset(rng, zc)); stk = endnames(rng); bas = endnames(rng); con = endnames(rng)
    for k in (0, K // 2, K - 1): z[1, 0, :, k] = 0
    ln = 1 + 14 * rng.integers(0, 2, (N, 8, K)); w = 1 + 256 * rng.integers(0, 2, (N, 8, 16, 1)); q = N - 1
    w[q, 7] = 257; w[q, 0] = 1; w[q, 6, 0] = 257; x[q, 6:8, :, 0] = 0; x[q, 7, :, W - 1] = 255; x[q, 6, :, W - 1] = 0; x[q, 6, 0, W - 1] = 255
    for k in (0, K - 1): stk[q, 7, :, k] = 0; stk[q, 7, 15, k] = W - 1
    for k in (1, K - 2): stk[q, 7, :, k] = W - 1
    for k in (2, K - 3): stk[q, 7, :, k] = 0; stk[q, 7, 0, k] = W - 1
    for k in (0, 1, 2, K - 3, K - 2, K - 1): z[q, 7, :, k] = 255
    for k in (2, K - 1): stk[q, 6, :, k] = W - 1; z[q, 6, :12, k] = 0; z[q, 6, 12:, k] = 255
    return pack(x, stk, bas, con, ln, z, w)
def setup_inputs_corners(rng):
    x, stk, bas, con, ln, z, w = parts(rng)
    cnt = rng.choice(np.array([0, TH - 1, TH, 16]), (N, 8, 1, W))
    over = rng.integers(0, 2, (N, 8, 1, W), dtype=np.int16) * rng.integers(0, 56, (N, 8, 16, W), dtype=np.int16)
    x = np.where(subset(rng, cnt) > 0, 200 + over, rng.integers(0, 200, (N, 8, 16, W), dtype=np.int16))
    z[:] = np.where(rng.random((N, 8, 1, K)) < 0.125, 201, 200); i = np.arange(16)[:, None]
    for q in range(N):
        for g in range(8):
            hot = np.flatnonzero(cnt[q, g, 0] >= TH); cold = np.flatnonzero(cnt[q, g, 0] < TH)
            row = rng.integers(1, 17, K); row[0] = 1; row[1] = 16; row[2] = 14; row[K - 1] = 15; row[K - 2] = 16
            hn = hot[rng.integers(0, len(hot), (16, K))]; cn = cold[rng.integers(0, len(cold), (16, K))]
            stk[q, g] = np.where(i == row, hn, np.where(i > row, stk[q, g], np.where((i == 0) & (rng.random((1, K)) < 0.5), hn, cn)))
    ln = rng.choice(np.array([1, 2, 14, 15]), (N, 8, K))
    for q in range(N): ln[q, q % 8] = 15; ln[q, (q + 1) % 8] = 1
    four = np.arange(K) % 4; stk[:, 3] = stk[:, 3][..., four]; z[:, 3] = z[:, 3][..., four]
    bas[:, 4] = (W - 1) * rng.integers(0, 2, (N, 16, K)); con[:, 2] = (W - 1) * rng.integers(0, 2, (N, 16, K))
    stk[:, 5] = stk[:, 5, :1].copy(); stk[:, 6] = E * np.arange(K) + rng.integers(0, E, (N, 16, K)); bas[:, 6] = E * np.arange(K) + rng.integers(0, E, (N, 16, K))
    w[0] = 1; w[N - 1] = 257
    return pack(x, stk, bas, con, ln, z, w)
def setup_inputs_long(rng):
    x, stk, bas, con, ln, z, w = parts(rng)
    x = np.where(rng.random((N, 8, 1, W)) < 0.06, rng.integers(250, 254, (N, 8, 16, W), dtype=np.int16), np.minimum(x, 249))
    ty = rng.random((N, 8, 1, K)); z = np.where(ty < 0.4, 250, np.where(ty < 0.8, 254, z)); ln = np.maximum(ln, rng.integers(1, 16, (N, 8, K)))
    return pack(x, stk, bas, con, ln, z, w)
def setup_inputs_alike(rng):
    x, stk, bas, con, ln, z, w = parts(rng); ga, gb, gc = [int(g) for g in rng.permutation(8)[:3]]; o = int(rng.integers(0, N))
    for a in (stk, bas, con):
        a[:, gb] = np.where(rng.random((N, 16, K)) < 0.5, E * rng.integers(K - 16, K, (N, 16, K)) + E - 1, a[:, gb])
    w[:, gb] = E * rng.integers(1, 256 // E + 1, (N, 16, 1)); w[:, gb, 0] = 1 + 256 * rng.integers(0, 2, (N, 1))
    for i in range(N):
        q = (o + i * ST) % N; lo, hi = ((32, 63), (96, 127), (192, 254), (96, 127), (0, 255))[min(i, 4)]
        if i < 4:
            x[q] = rng.integers(lo, hi + 1, (8, 16, W)); z[q] = 255 if i == 1 else 0
        if i == 2:
            m = np.zeros(8 * K, dtype=bool); m[rng.permutation(8 * K)[:K * int(rng.integers(0, 8)) + int(rng.integers(1, K))]] = True
            z[q] = np.where(m.reshape(8, 1, K), 255, 0)
        for g, v in ((ga, int(rng.integers(1, 4))), (gc, 0)):
            one = rng.integers(lo, hi - 2, 16); one[15] += (v - int(np.sum(one))) % 4
            x[q, g] = one[:, None]
        x[q, gb, 0] = (hi + 1) // E * E - 1
    return pack(x, stk, bas, con, ln, z, w)
def check_inputs(d):
    bad = []
    for k, lo, hi in (("xt", 0, 255), ("stk", 0, W - 1), ("bas", 0, W - 1), ("con", 0, W - 1), ("ln", 1, 15), ("z", 0, 255), ("w", 1, 257)):
        v = np.asarray(d[k]).astype(np.float32)
        if not (np.min(v) >= lo and np.max(v) <= hi and np.all(v == np.floor(v))): bad.append("range of " + k)
    return bad
def reference(xt, stk, bas, con, ln, z, w):
    X = xt.astype(np.float32).astype(np.int32).reshape(N, 8, 16, W); Z = z.astype(np.float32).astype(np.int64).reshape(N, 8, 16, K); wt = w.astype(np.int64).reshape(N, 8, 16, 1)
    S = stk.astype(np.int64).reshape(N, 8, 16, K); B = bas.astype(np.int64).reshape(N, 8, 16, K); C = con.astype(np.int64).reshape(N, 8, 16, K); n = ln.astype(np.int64).reshape(N, 8, K)
    A = [0] * N; p = np.arange(16)[None, :, None]
    for t in range(RO):
        for q in range(N):
            b = (q - t * ST) % N
            s, zz = S[b].copy(), Z[b].copy()
            R = np.take_along_axis(X[q], s.reshape(8, 1, 16 * K), 2).reshape(8, 16, 16, K).astype(np.int64)
            votes = np.add.reduce((R >= zz[:, :, None, :]).astype(np.int64), axis=1)
            hit = votes >= TH; hit[:, 0] = False
            found = np.maximum.accumulate(hit.astype(np.int64), axis=1)
            handled = found[:, 15] == 1; h = 16 - np.add.reduce(found, axis=1)
            M = np.max(np.where(found[:, None] == 1, 0, R), axis=2)
            u = np.add.reduce(wt[q] * M, axis=1) & 4095
            xh = np.take_along_axis(R, np.minimum(h, 15)[:, None, None, :], 2)[:, :, 0]
            v = np.add.reduce(xh, axis=1) & 3
            j = (((u * u) >> 5) + u + A[q]) & (K - 1)
            paste = handled & (v > 0)
            m = np.where(paste, np.take_along_axis(n[q], j, 1), 0)
            src = p + (np.where(paste, h + 1, h) - m)[:, None, :]
            low = np.take_along_axis(s, np.clip(src, 0, 15), 1); piece = np.take_along_axis(C[q], j[:, None, :], 2)
            new = np.where(p < m[:, None, :], piece, np.where(src <= 15, low, B[b]))
            S[b] = np.where(handled[:, None, :], new, s)
            Z[b] = np.where(handled[:, None, :], np.abs(xh - zz), M)
            C[q] = np.where(paste[:, None, :] & (p < h[:, None, :]), s, C[q])
            n[q] = np.where(paste, h, n[q])
            A[q] = int(np.sum(np.where(handled, 0, 1)))
            if t < RO - 1:
                col = (E * np.arange(K) + (u & (E - 1)))[:, None, :]
                np.put_along_axis(X[q], col, ((np.take_along_axis(X[q], col, 2) + M) >> 1).astype(np.int32), 2)
    last = [(q - (RO - 1) * ST) % N for q in range(N)]
    return {"ys": S[last].reshape(N, 128, K).astype(np.float32), "yc": C.reshape(N, 128, K).astype(np.float32), "yn": n.astype(np.float32), "yz": Z[last].reshape(N, 128, K).astype(np.float32).astype(BF)}

@@ -1,0 +1,525 @@
+import math
+from concourse.bass import DstId, RemoteDMATransfer
+from concourse.mybir import AluOpType as OP, AxisListType, ActivationFunctionType as AF
+
+RO = 6
+CH, L = 2, 128
+K = CH * L
+NDP = 4
+PXN = 32
+PIECES = [(0, 64, "A"), (64, 32, "V"), (96, 32, "V"), (128, 64, "A"), (192, 64, "A")]
+CHUNKS = [(0, 128, 0), (128, 64, 0), (192, 64, 0)]
+SIGNQ = 1
+DELTA = 300.0
+
+SCRATCH = {
+    "XT": ("sbuf", [128, 8192], "bfloat16"), "PC": ("sbuf", [128, 2048], "float32"),
+    "NB0": ("sbuf", [128, 256], "bfloat16"), "NB1": ("sbuf", [128, 256], "bfloat16"),
+    "EALL": ("sbuf", [128, 2048], "bfloat16"), "RALL": ("sbuf", [128, 2048], "bfloat16"), "RESET": ("sbuf", [128, 2048], "bfloat16"),
+    "BO": ("sbuf", [128, 128], "bfloat16"), "IDM": ("sbuf", [128, 128], "bfloat16"), "NID": ("sbuf", [128, 128], "bfloat16"),
+    "ONES": ("sbuf", [128, 256], "bfloat16"), "DIAG": ("sbuf", [128, 256], "bfloat16"), "WALL": ("sbuf", [128, 2048], "float16"),
+    "ACT": ("sbuf", [128, 16], "float32"), "KF": ("sbuf", [128, 16], "float32"), "T1": ("sbuf", [128, 16], "bfloat16"), "T2": ("sbuf", [128, 32], "bfloat16"),
+    "NV": ("sbuf", [128, 128], "float32"), "SEL": ("sbuf", [128, 128], "bfloat16"),
+    "IO1": ("sbuf", [128, 2048], "bfloat16"), "IO2": ("sbuf", [128, 128], "bfloat16"), "IO3": ("sbuf", [128, 256], "bfloat16"),
+    "IO4": ("sbuf", [128, 128], "bfloat16"), "IO5": ("sbuf", [128, 128], "int32"), "RL1": ("sbuf", [128, 128], "int32"),
+    "RL2": ("sbuf", [128, 128], "int32"), "RLU": ("sbuf", [128, 128], "uint16"), "K0": ("sbuf", [128, 16], "int32"),
+    "KT": ("sbuf", [128, 16], "int32"), "KM": ("sbuf", [128, 16], "int32"), "K32": ("sbuf", [128, 16], "int32"),
+    "PI": ("sbuf", [128, 8], "int32"), "PF": ("sbuf", [128, 24], "float32"), "F4": ("sbuf", [128, 16], "float32"),
+    "Z0": ("sbuf", [128, 16], "float32"), "PWS": ("sbuf", [128, 16], "float32"), "PWM": ("sbuf", [128, 16], "float32"),
+    "PW": ("sbuf", [128, 1], "float32"), "WI": ("sbuf", [128, 8], "int32"), "WF": ("sbuf", [128, 8], "float32"),
+    "LNI": ("sbuf", [128, 256], "int32"), "LNB": ("sbuf", [128, 256], "bfloat16"), "PCM": ("sbuf", [128, 256], "bfloat16"),
+    "STI": ("sbuf", [128, 256], "int32"), "BAI": ("sbuf", [128, 256], "int32"), "COI": ("sbuf", [128, 256], "int32"),
+    "HD": ("sbuf", [128, 16], "bfloat16"), "AR": ("sbuf", [128, 1], "float32"), "AC": ("sbuf", [128, 1], "float32"),
+    "FI": ("sbuf", [128, 256], "int32"), "FJ": ("sbuf", [128, 256], "int32"), "FC": ("sbuf", [128, 256], "float32"),
+    "FN": ("sbuf", [128, 256], "int32"), "FM": ("sbuf", [128, 256], "int32"), "FL": ("sbuf", [128, 256], "float32"),
+    "ER": ("dram", [8, 32, 256], "float32"), "YSF": ("sbuf", [128, 256], "float32"),
+    "RP": ("sbuf", [128, 8192], "bfloat16"),
+    "GE": ("sbuf", [128, 4096], "bfloat16"), "WR": ("sbuf", [128, 4096], "float32"), "HP": ("sbuf", [128, 256], "bfloat16"),
+    "ZH": ("sbuf", [128, 256], "bfloat16"), "DA": ("sbuf", [128, 512], "float32"), "DB": ("sbuf", [128, 512], "float32"),
+    "SM": ("sbuf", [128, 512], "int32"), "SF": ("sbuf", [128, 32], "float32"), "LU": ("sbuf", [128, 128], "uint16"),
+    "ME": ("sbuf", [128, 256], "bfloat16"), "YE": ("sbuf", [128, 256], "bfloat16"), "XS": ("sbuf", [128, 256], "int32"),
+    "XD": ("sbuf", [128, 256], "int32"), "AB": ("sbuf", [128, 256], "float32"), "AD": ("sbuf", [128, 256], "float32"),
+    "QQ": ("sbuf", [128, 256], "int32"), "SI": ("sbuf", [128, 256], "int32"), "S8": ("sbuf", [128, 256], "float32"),
+    "MD": ("sbuf", [128, 256], "bfloat16"), "ML": ("sbuf", [128, 256], "bfloat16"), "PL": ("sbuf", [128, 256], "float32"),
+    "pz": ("psum", [128, 512], "float32"), "pva": ("psum", [128, 512], "float32"), "pvb": ("psum", [128, 512], "float32"),
+    "pu": ("psum", [128, 512], "float32"), "pm": ("psum", [128, 512], "float32"), "pr0": ("psum", [128, 512], "float32"),
+    "pr1": ("psum", [128, 512], "float32"), "pr2": ("psum", [128, 512], "float32"),
+}
+for _d in range(4):
+    SCRATCH["BB%d" % _d] = ("sbuf", [128, 256], "float32")
+for _n, _ty in (("U", "uint16"), ("Z", "bfloat16"), ("H", "bfloat16"), ("L", "bfloat16")):
+    SCRATCH["S" + _n] = ("sbuf", [128, RO * 256], _ty)
+    SCRATCH["O" + _n] = ("sbuf", [128, 2 * 256], _ty)
+
+SEMAPHORES = ["cV", "cA", "cT", "cG", "loc"] + ["lo%d" % i for i in range(20)] + ["dm%d" % i for i in range(24)] + ["bs%d" % d for d in (1, 2, 3)] + \
+             ["ar%d%d%s" % (t, c, s) for t in range(1, RO) for c in range(CH) for s in "ab"]
+
+ORDER = {}
+BONUS = {"IO": -2000.0, "HP": 8000.0, "XS": -20000.0, "OL": -8000.0, "pa": -2000.0, "SU": -2000.0, "pr": -20000.0, "NB": -20000.0, "pm": 8000.0,
+         "uv": -8000.0, "e": -20000.0, "HI": 2000.0, "XT": -20000.0, "pz": -20000.0}
+CYC = 0.83 * 1.2
+G_R = 1.55
+
+
+def make_order(ops, deps, log=None):
+    n = len(ops)
+    succ = [[] for _ in range(n)]
+    for i in range(n):
+        for j in deps[i]:
+            succ[j].append(i)
+    prio = [0.0] * n
+    for i in range(n - 1, -1, -1):
+        op = ops[i]
+        prio[i] = op["cost"] + max([op["lat"] + prio[x] for x in succ[i]] + [0.0])
+    for i in range(n):
+        prio[i] += max([BONUS.get(w.split(":")[0].rstrip("0123456789"), 0.0) for w in ops[i]["w"]] + [-9e9]) if ops[i]["w"] else 0.0
+    left = [len(deps[i]) for i in range(n)]
+    est = [0.0] * n
+    qs = ["V", "A", "T", "S", "G"]
+    ready = {q: [] for q in qs}
+    for i in range(n):
+        if left[i] == 0:
+            ready[ops[i]["q"]].append(i)
+    qt = {q: 0.0 for q in qs}
+    order = []
+    while len(order) < n:
+        best = None
+        for q in qs:
+            if not ready[q]:
+                continue
+            m0 = max(qt[q], min([est[i] for i in ready[q]]))
+            if best is None or m0 < best[0]:
+                best = (m0, q)
+        m0, q = best
+        i = max([x for x in ready[q] if est[x] <= m0 + DELTA], key=lambda x: (prio[x], -x))
+        st = max(qt[q], est[i])
+        ready[q].remove(i)
+        qt[q] = st + ops[i]["cost"]
+        order.append(i)
+        if log is not None:
+            log.append((i, st))
+        for x in succ[i]:
+            cross = ops[x]["q"] != q or deps[x][i]
+            est[x] = max(est[x], qt[q] + (ops[i]["lat"] if cross else 0.0))
+            left[x] -= 1
+            if left[x] == 0:
+                ready[ops[x]["q"]].append(x)
+    return order, max(qt.values())
+
+
+def rank_program(g, core, T, topo):
+    rank = T.rank_of(core)
+    if rank is None:
+        return
+    n_ranks = len(T.cores)
+    ops = []
+    eng = {"V": g.vector, "A": g.scalar, "T": g.tensor, "S": g.sync, "G": g}
+
+    def add(q, fns, reads, writes, cost, lat=60.0, kind="c", sem=None, amount=0, banks=()):
+        ops.append({"q": q, "fns": fns if isinstance(fns, list) else [fns], "r": list(reads), "w": list(writes), "cost": cost,
+                    "lat": lat, "kind": kind, "sem": sem, "amount": amount, "banks": list(banks)})
+
+    def vc(n, rate=1.0):
+        return max(64.0, n * rate) * CYC
+
+    def isps(keys):
+        return sorted(set(k.split(":")[0] for k in keys if k.startswith("p")))
+
+    def V(fn, reads, writes, n, rate=1.0):
+        add("V", fn, reads, writes, vc(n, rate), banks=isps(list(reads) + list(writes)))
+
+    def A(fn, reads, writes, n, rate=1.0, extra=0.0):
+        add("A", fn, reads, writes, vc(n, rate) + extra, banks=isps(list(reads) + list(writes)))
+
+    def P(fns, reads, writes, cyc):
+        add("T", fns, reads, writes, cyc * 0.8, banks=isps(list(reads) + list(writes)))
+
+    def G(fn, reads, writes, n):
+        add("G", fn, reads, writes, 130 + 2 * n * CYC)
+
+    ndma = [0]
+
+    def D(q, fn, reads, writes, lat=2500.0):
+        add(q, fn, reads, writes, 60.0, lat, "d", "dm%d" % ndma[0], 16)
+        ndma[0] += 1
+
+    def DS(fns, reads, writes, lat):
+        add("S", fns, reads, writes, 60.0 * len(fns), lat, "d", "dm%d" % ndma[0], 16 * len(fns))
+        ndma[0] += 1
+
+    v, s, te = g.vector, g.scalar, g.tensor
+
+    def tt(o, a, b, op):
+        return lambda: v.tensor_tensor(out=o, in0=a, in1=b, op=op)
+
+    def ts(o, a, s1, op0, s2=None, op1=None):
+        if op1 is None:
+            return lambda: v.tensor_scalar(out=o, in0=a, scalar1=s1, scalar2=None, op0=op0)
+        return lambda: v.tensor_scalar(out=o, in0=a, scalar1=s1, scalar2=s2, op0=op0, op1=op1)
+
+    def cp(o, a):
+        return lambda: v.tensor_copy(out=o, in_=a)
+
+    def scan(o, d0, d1, op1, ini=0.0):
+        return lambda: v.tensor_tensor_scan(out=o, data0=d0, data1=d1, initial=ini, op0=OP.mult, op1=op1)
+
+    def act(o, a, f, bias=0.0):
+        return lambda: s.activation(out=o, in_=a, func=f, bias=bias)
+
+    def mm(o, lh, rh, st, sp):
+        return lambda: te.matmul(out=o, lhsT=lh, rhs=rh, start=st, stop=sp)
+
+    def ms(o, x):
+        return lambda: v.memset(o, x)
+
+    def io(o, pat, ch, flag=True, base=0):
+        if flag:
+            return lambda: g.iota(o, pattern=pat, base=base, channel_multiplier=ch, allow_small_or_imprecise_dtypes=True)
+        return lambda: g.iota(o, pattern=pat, base=base, channel_multiplier=ch)
+
+    def dma(q, o, a):
+        return lambda: eng[q].dma_start(out=o, in_=a)
+
+    V(ms(T.PF[:, 9:10], 0.5), [], ["PF9"], 1)
+    V(ms(T.PF[:, 10:11], 64.0), [], ["PF10"], 1)
+    V(ms(T.PF[:, 11:12], 8.5), [], ["PF11"], 1)
+    V(ms(T.PF[:, 12:13], 2040.0 - 0.4375), [], ["PF12"], 1)
+    for t in range(RO):
+        V(ms(T.PF[:, 16 + t:17 + t], 8192.0 * (t + 2)), [], ["PF%d" % (16 + t)], 1)
+
+    D("S", dma("S", T.XT[:], T.xt[:]), [], ["XT"], 9000.0)
+    D("A", dma("A", T.STI[:], T.stk[:]), [], ["STI"])
+    D("A", dma("A", T.SZ[:, 0:256], T.z[:]), [], ["ZZ0:0", "ZZ0:1"])
+    D("S", dma("S", T.WI[:, 0:1], T.w[:]), [], ["WI"])
+    D("S", dma("S", T.BAI[:], T.bas[:]), [], ["BAI"])
+    D("A", dma("A", T.LNI[0:8, :], T.ln[:]), [], ["LNI"])
+    D("S", dma("S", T.COI[:], T.con[:]), [], ["COI"])
+
+    G(io(T.PI[:, 0:1], [[0, 1]], 1, False), [], ["PI0"], 1)
+    V(ts(T.PI[:, 1:2], T.PI[:, 0:1], 15, OP.bitwise_and), ["PI0"], ["PI1"], 1)
+    V(ts(T.PI[:, 2:3], T.PI[:, 0:1], 112, OP.bitwise_and), ["PI0"], ["PI2"], 1)
+    V(cp(T.PF[:, 0:3], T.PI[:, 0:3]), ["PI0", "PI1", "PI2"], ["PF0"], 3)
+    pf, pmf, p16 = T.PF[:, 0:1], T.PF[:, 1:2], T.PF[:, 2:3]
+    V(ts(T.PF[:, 3:4], pmf, -1.0, OP.mult, 16.0, OP.add), ["PF0"], ["PF3"], 1)
+    V(ts(T.PF[:, 4:5], pmf, -1.0, OP.mult, 15.0, OP.add), ["PF0"], ["PF4"], 1)
+    V(ts(T.PF[:, 5:6], pf, 16.0, OP.mult), ["PF0"], ["PF5"], 1)
+    V(ts(T.PF[:, 6:7], pmf, 256.0, OP.mult), ["PF0"], ["PF6"], 1)
+    V(ts(T.PF[:, 7:8], pmf, 15.5 - 4 * SIGNQ, OP.is_gt, -7.5, OP.mult), ["PF0"], ["PF7"], 1)
+    V(ts(T.PF[:, 8:9], T.PF[:, 7:8], 8.5, OP.add), ["PF7"], ["PF8"], 1)
+    G(io(T.IO4[:], [[1, 128]], 0), [], ["IO4"], 128)
+    G(io(T.RL1[:], [[1, 16], [0, 8]], 1, False), [], ["RL1"], 128)
+    G(io(T.IO5[:], [[0, 16], [16, 8]], 0, False), [], ["IO5"], 128)
+    G(io(T.IO3[:], [[0, 16], [1, 16]], 0), [], ["IO3"], 256)
+    G(io(T.IO1[:], [[-1, 16], [1, 128]], 0), [], ["IO1"], 2048)
+    G(io(T.IO2[:], [[16, 8], [0, 16]], 0), [], ["IO2"], 128)
+    G(io(T.K0[:], [[16, 16]], 0, False), [], ["K0"], 16)
+    G(io(T.NV[:], [[8192, 8], [256, 16]], 0, True, -256), [], ["NV"], 128)
+    V(ms(T.NV[:, 0:128:16], 0.0), [], ["NV"], 8)
+    V(ts(T.IDM[:], T.IO4[:], pf, OP.is_equal), ["IO4", "PF0"], ["IDM"], 128, .5)
+    V(ts(T.NID[:], T.IDM[:], -1.0, OP.mult), ["IDM"], ["NID"], 128, .5)
+    V(cp(T.SU[:, 0:K], T.STI[:]), ["STI"], ["SU0:0", "SU0:1"], K)
+    V(cp(T.SH[:, 0:K], T.STI[:]), ["STI"], ["HI0:0", "HI0:1"], K)
+    V(tt(T.SL[:, 0:K], T.STI[:], T.SH[:, 0:K], OP.subtract), ["STI", "HI0:0", "HI0:1"], ["LO0:0", "LO0:1"], K, 2)
+    V(ts(T.RL2[:], T.RL1[:], 15, OP.bitwise_and), ["RL1"], ["RL2"], 128)
+    V(tt(T.RL1[:], T.RL2[:], T.IO5[:], OP.add), ["RL2", "IO5"], ["RL1"], 128, 2)
+    V(cp(T.RLU[:], T.RL1[:]), ["RL1"], ["RLU"], 128)
+    A(act(T.RALL[:], T.IDM[:, 0:128].indirect(T.RLU[:, 0:128]), AF.Copy), ["IDM", "RLU"], ["RALL"], 2048, G_R)
+    V(ts(T.EALL[:], T.IO1[:], p16, OP.is_equal), ["IO1", "PF0"], ["EALL"], 2048, .5)
+    V(ms(T.RESET[:], 1.0), [], ["RESET"], 2048, .5)
+    V(ms(T.RESET[:, 0:2048:16], 0.0), [], ["RESET"], 128, .5)
+    V(ts(T.DIAG[:], T.IO3[:], pmf, OP.is_equal), ["IO3", "PF0"], ["DIAG"], 256, .5)
+    V(ts(T.T1[:], T.IO4[:, 0:16], pmf, OP.is_gt), ["IO4", "PF0"], ["T1"], 16)
+    V(ts(T.T2[:], T.IO4[:, 0:32], T.PF[:, 3:4], OP.is_ge), ["IO4", "PF3"], ["T2"], 32)
+    V(ms(T.T2[:, 16:32], 0.0), [], ["T2"], 16)
+    V(ts(T.BO[:], T.IO2[:], p16, OP.is_equal), ["IO2", "PF0"], ["BO"], 128, .5)
+    V(ms(T.ONES[:], 1.0), [], ["ONES"], 256, .5)
+    V(ts(T.KT[:], T.K0[:], pmf, OP.add), ["K0", "PF0"], ["KT"], 16)
+    V(ts(T.KM[:], T.KT[:], 16.0, OP.mult, 4095.0, OP.add), ["KT"], ["KM"], 16)
+    V(ts(T.K32[:], T.KT[:], 32.0, OP.mult), ["KT"], ["K32"], 16)
+    V(ts(T.KF[:], T.KT[:], -16.0 * math.log(4.0), OP.mult, -(4095.0 + 19.0) * math.log(4.0), OP.add), ["KT"], ["KF"], 16)
+    V(ms(T.F4[:], 4.0), [], ["F4"], 16)
+    V(ms(T.Z0[:], 0.0), [], ["Z0"], 16)
+    V(scan(T.PWS[:], T.F4[:], T.Z0[:], OP.add, 64.0), ["F4", "Z0"], ["PWS"], 16)
+    V(ms(T.PWS[:, 15:16], 0.0), [], ["PWS"], 1)
+    V(ts(T.PWM[:], T.IO4[:, 0:16], T.PF[:, 4:5], OP.is_equal), ["IO4", "PF4"], ["PWM"], 16)
+    V(tt(T.PWM[:], T.PWM[:], T.PWS[:], OP.mult), ["PWM", "PWS"], ["PWM"], 16)
+    V(lambda: v.tensor_reduce(out=T.PW[:], in_=T.PWM[:], axis=AxisListType.X, op=OP.add), ["PWM"], ["PW"], 16)
+    V(cp(T.WF[:, 0:1], T.WI[:, 0:1]), ["WI"], ["WF"], 1)
+    V(ts(T.WALL[:], T.EALL[:], T.WF[:, 0:1], OP.mult), ["EALL", "WF"], ["WALL"], 2048, .5)
+    V(ms(T.AC[:], -8.4375), [], ["AC"], 1)
+    V(ts(T.BB0[:], T.BAI[:], 8192.0, OP.add), ["BAI"], ["BB0"], 256)
+
+    def remote(pairs, dst, sem, lsem):
+        es = topo.engines(core, dst)
+        per = len(es) // len(pairs)
+        rid, pid, _ = topo.addr(dst)
+        tr = []
+        for i, (o, a) in enumerate(pairs):
+            m = sum(1 << e for e in es[i * per:(i + 1) * per])
+            tr.append(RemoteDMATransfer(dst_ids=[DstId(rid=rid, pnc=pid)], dma_engine_mask=m, remote_sem=T.sem[sem], srcs=[a], dsts=[o], alu_op=0))
+        return lambda: g.remote_dma_fused(tr, local_sem=T.sem[lsem])
+
+    n_eng = len(topo.engines(core, T.cores[(rank + 1) % n_ranks]))
+    for d in (1, 2, 3):
+        dst = T.cores[(rank + d) % n_ranks]
+        add("G", remote([(T["BB%d" % d][:], T.BB0[:])], dst, "bs%d" % d, "loc"), ["BB0"], ["BB%d" % d], 1000.0, 4000.0, "r", "bs%d" % d, n_eng)
+    V(cp(T.LNB[0:8, :], T.LNI[0:8, :]), ["LNI"], ["LNB"], 256)
+    V(ts(T.SEL[0:8, :], T.IO2[0:8, :], T.PF[0:8, 5:6], OP.is_equal, 256.0, OP.mult), ["IO2", "PF5"], ["SEL"], 128)
+    P([mm(T.pm[:, 0:256], T.SEL[0:8, :], T.LNB[0:8, :], True, True)], ["SEL", "LNB"], ["pm:0"], 256)
+    V(ts(T.NB0[:], T.pm[:, 0:256], 7936.0, OP.add), ["pm:0"], ["NB0"], 256)
+    V(ts(T.PCM[:], T.pm[:, 0:256], T.PF[:, 6:7], OP.is_gt), ["pm:0", "PF6"], ["PCM"], 256)
+    V(ms(T.PC[:, 0:256], 0.0), [], ["PC0"], 256)
+    V(ts(T.PL[:], T.COI[:], 8192.0, OP.add), ["COI"], ["PL"], 256)
+    V(tt(T.PC[:, 256:512], T.PL[:], T.PCM[:], OP.mult), ["PL", "PCM"], ["PC1"], 256, 2)
+    V(cp(T.pm[:, 256:512], T.PL[:]), ["PL"], ["pm:c"], 256)
+    CT = T.pm[:, 256:512]
+
+    rotn = [0]
+    nloc = [0]
+    nxt = T.cores[(rank + 1) % n_ranks]
+    SM, LU, DA, DB, RP, GE = T.SM, T.LU, T.DA, T.DB, T.RP, T.GE
+    pvs = [T.pva, T.pvb]
+
+    def sm(x, w=16):
+        return SM[:, x * 16:x * 16 + w]
+
+    def bank():
+        rotn[0] += 1
+        return "pr%d" % (rotn[0] % 3)
+
+    def send(pairs, t, c, part, reads, writes):
+        sem, ls = "ar%d%d%s" % (t, c, part), "lo%d" % nloc[0]
+        nloc[0] += 1
+        add("G", remote(pairs, nxt, sem, ls), reads, writes, 1000.0, 2300.0, "r", sem, n_eng)
+        ops[-1]["lsem"] = ls
+
+    for t in range(RO):
+        last = t == RO - 1
+        par = t % 2
+        NB, NN, nb, nn = T["NB%d" % par], T["NB%d" % (1 - par)], "NB%d" % par, "NB%d" % (1 - par)
+        BB, bbk = T["BB%d" % (t % 4)], "BB%d" % (t % 4)
+        r0, o0 = t * K, par * K
+        su, zz, hi, lo = [["%s%d:%d" % (x, t, c) for c in range(CH)] for x in ("SU", "ZZ", "HI", "LO")]
+        ZA = T.SZ[:, r0:r0 + K]
+        for c in range(CH):
+            P([mm(T.pz[:, c * L:c * L + L], T.IDM[:], T.SZ[:, r0 + c * L:r0 + c * L + L], True, True)], ["IDM", zz[c]], ["pz:z%d" % c], L)
+        for p0, pn, pq in PIECES:
+            a, rk = r0 + p0, ["R%d" % (x // 16) for x in range(p0, p0 + pn, 16)]
+            rd = ["XT", su[p0 // L]]
+            if pq == "A":
+                A(act(RP[:, 16 * p0:16 * (p0 + pn)], T.XT[:].indirect(T.SU[:, a:a + pn]), AF.Copy), rd, rk, pn * 16, G_R, 65.0)
+            else:
+                V(cp(RP[:, 16 * p0:16 * (p0 + pn)], T.XT[:].indirect(T.SU[:, a:a + pn])), rd, rk, pn * 16, G_R)
+        for c, (c0, cn, sq) in enumerate(CHUNKS):
+            h = c0 // L
+            Z = T.SZ[:, r0 + c0:r0 + c0 + cn]
+            Rk = ["R%d" % (x // 16) for x in range(c0, c0 + cn, 16)]
+            vrows, srows = list(range(1, 16 - 4 * sq)), list(range(16 - 4 * sq, 16))
+            for qd in range(sq):
+                bk = bank()
+                i0 = 16 - 4 * (qd + 1)
+                fns = []
+                for i in range(4):
+                    ob = T[bk][:, i * cn:(i + 1) * cn]
+                    fns += [mm(ob, T.IDM[:], RP[:, 16 * c0 + i0 + i:16 * (c0 + cn):16], True, False), mm(ob, T.NID[:], Z, False, True)]
+                P(fns, ["IDM", "NID", zz[h]] + Rk, [bk + ":s"], 8 * cn)
+                A(act(GE[:, 16 * c0 + i0 * cn:16 * c0 + (i0 + 4) * cn], T[bk][:, 0:4 * cn], AF.Sign, T.PF[:, 9:10]), [bk + ":s", "PF9"],
+                  ["GE%d:%d" % (i, c) for i in range(i0, i0 + 4)], 4 * cn)
+            for i in vrows:
+                V(tt(GE[:, 16 * c0 + i * cn:16 * c0 + (i + 1) * cn], RP[:, 16 * c0 + i:16 * (c0 + cn):16], T.pz[:, c0:c0 + cn], OP.is_ge),
+                  ["pz:z%d" % h] + Rk, ["GE%d:%d" % (i, c)], cn)
+            pv, kv = pvs[h], ("pva", "pvb")[h]
+            seq = vrows + srows
+            for x, i in enumerate(seq):
+                P([mm(pv[:, c0 - h * L:c0 - h * L + cn], T.EALL[:, i * 128:(i + 1) * 128], GE[:, 16 * c0 + i * cn:16 * c0 + (i + 1) * cn], x == 0, x == len(seq) - 1)],
+                  ["EALL", "GE%d:%d" % (i, c)], [kv + ":v"], cn)
+            for x0 in range(c0, c0 + cn, PXN):
+                V(scan(RP[:, 4096 + 16 * x0:4096 + 16 * (x0 + PXN)], T.RESET[:, 0:16 * PXN], RP[:, 16 * x0:16 * (x0 + PXN)], OP.max),
+                  ["R%d" % (x // 16) for x in range(x0, x0 + PXN, 16)] + ["RESET"], ["PX:%d" % x0], 16 * PXN, .5)
+            if c0 + cn == L or c0 + cn == K:
+                V(ts(T.HP[:, h * L:h * L + L], pv[:, 0:L], T.PF[:, 8:9] if sq else T.PF[:, 11:12], OP.is_ge, T.PW[:], OP.mult), [kv + ":v", "PW", "PF8", "PF11"], ["HP%d" % h], L)
+        allR = ["R%d" % x for x in range(16)] + ["PX:%d" % x for x in range(0, K, PXN)]
+        P([mm(T.pva[:, 3 * L:3 * L + 16], T.EALL[:, i * 128:(i + 1) * 128], T.HP[:, i:K:16], i == 0, i == 15) for i in range(16)],
+          ["EALL", "HP0", "HP1"], ["pva:l"], 16 * 64)
+        A(act(T.SF[:, 0:16], T.pva[:, 3 * L:3 * L + 16], AF.Ln, T.PF[:, 10:11]), ["pva:l", "PF10"], ["SF"], 16)
+        P([mm(T.pvb[:, L:L + K], T.BO[:], T.HP[:], True, True)], ["BO", "HP0", "HP1"], ["pvb:s"], K)
+        V(tt(T.ZH[:], ZA, T.pvb[:, L:L + K], OP.min), zz + ["pvb:s"], ["ZH"], K)
+        V(ts(sm(0), T.SF[:, 0:16], -1.0 / math.log(4.0), OP.mult, 19.0, OP.add), ["SF"], ["h"], 16)
+        V(tt(sm(2), sm(0), T.KM[:], OP.add), ["h", "KM"], ["lm"], 16)
+        V(tt(DB[:, 0:16], T.SF[:, 0:16], T.KF[:], OP.add), ["SF", "KF"], ["SFx"], 16)
+        V(ts(LU[:, 0:16], DB[:, 0:16], -1.0 / math.log(4.0), OP.mult, 0.25, OP.add), ["SFx"], ["LU0"], 16)
+        V(ts(sm(1), sm(0), 15.5, OP.is_lt, -4095.0, OP.mult), ["h"], ["e"], 16)
+        V(tt(sm(3), sm(2), sm(1), OP.add), ["lm", "e"], ["ly"], 16)
+        V(cp(LU[:, 16:32], sm(3)), ["ly"], ["LUy"], 16)
+        A(act(T.ME[:], RP[:].indirect(LU[:, 0:16]), AF.Copy), allR + ["LU0"], ["M"], K, G_R, 65.0)
+        A(act(T.YE[:], RP[:].indirect(LU[:, 16:32]), AF.Copy), allR + ["LUy"], ["Y"], K, G_R, 65.0)
+        P([mm(T.pu[:, 0:16], T.BO[:], T.ONES[:, 0:16], True, False)], ["BO", "ONES"], ["pu:u"], 64)
+        P([mm(T.pu[:, 0:16], T.WALL[:, i * 128:(i + 1) * 128], T.ME[:, i:K:16], False, i == 15) for i in range(16)], ["WALL", "M"], ["pu:u"], 16 * 64)
+        P([mm(T.pva[:, 400:416], T.EALL[:, i * 128:(i + 1) * 128], T.YE[:, i:K:16], i == 0, i == 15) for i in range(16)], ["EALL", "Y"], ["pva:y"], 16 * 64)
+        V(cp(sm(4), T.pu[:, 0:16]), ["pu:u"], ["uv"], 16)
+        V(ts(sm(6), sm(4), 4095, OP.bitwise_and), ["uv"], ["uvm"], 16)
+        V(cp(sm(5), T.pva[:, 400:416]), ["pva:y"], ["vy"], 16)
+        u, vv = sm(6), sm(5)
+        V(tt(T.SF[:, 16:32], u, u, OP.mult), ["uvm"], ["yq"], 16)
+        V(ts(sm(9), T.SF[:, 16:32], 1.0 / 32.0, OP.mult, T.AC[:], OP.add), ["yq", "AC"], ["jf"], 16)
+        V(ts(sm(8), u, 16.0, OP.add), ["uvm"], ["u32"], 16)
+        V(ts(sm(11), sm(8), 31, OP.bitwise_and), ["u32"], ["a31"], 16)
+        V(ts(sm(12), sm(9), 255, OP.bitwise_and), ["jf"], ["j"], 16)
+        V(tt(sm(13), sm(11), T.K32[:], OP.add), ["a31", "K32"], ["a"], 16)
+        V(cp(LU[:, 32:64], sm(12, 32)), ["j", "a"], ["LU1"], 32)
+        V(tt(T.MD[:], NB[:].indirect(LU[:, 32:48]), T.DIAG[:, 0:K], OP.mult), [nb, "LU1", "DIAG"], ["MD"], K, G_R)
+        V(ts(T.HD[:], sm(0), 15.5, OP.is_lt), ["h"], ["HD"], 16)
+        V(ts(sm(17), sm(0), 256.0, OP.mult), ["h"], ["h256"], 16)
+        V(tt(sm(18), sm(17), T.KT[:], OP.add), ["h256", "KT"], ["d0"], 16)
+        V(ts(sm(14), vv, 3, OP.bitwise_and), ["vy"], ["v3"], 16)
+        V(tt(sm(16), sm(14), T.HD[:], OP.min), ["v3", "HD"], ["pa"], 16)
+        V(tt(sm(27), sm(0), sm(16), OP.mult), ["h", "pa"], ["cd"], 16)
+        V(scan(T.ML[:], T.RESET[:, 0:K], T.MD[:], OP.add), ["RESET", "MD"], ["ML"], K, .5)
+        V(tt(sm(20), T.ML[:, 15:K:16], sm(16), OP.mult), ["ML", "pa"], ["mc"], 16)
+        V(tt(sm(21), sm(18), sm(20), OP.subtract), ["d0", "mc"], ["d"], 16)
+        V(ts(sm(22), sm(20), 5, OP.arith_shift_right, 0x700, OP.bitwise_and), ["mc"], ["ver"], 16)
+        V(ts(sm(24), sm(21), 4095, OP.bitwise_and), ["d"], ["lr"], 16)
+        V(ts(sm(25), sm(21), 8, OP.arith_shift_right, 31, OP.bitwise_and), ["d"], ["ls"], 16)
+        V(tt(sm(26), sm(22), sm(12), OP.add), ["ver", "j"], ["lp"], 16)
+        V(cp(LU[:, 64:128], sm(24, 64)), ["lr", "ls", "lp", "cd"], ["LU2"], 64)
+        P([mm(T.pz[:, K:2 * K], T.IDM[:], T.YE[:], True, False), mm(T.pz[:, K:2 * K], T.NID[:], T.ZH[:], False, True)], ["IDM", "NID", "Y", "ZH"], ["pz:d"], 2 * K)
+        OZ, oz = T.OZ[:, o0:o0 + K], "OZ%d" % par
+        A(act(OZ, T.pz[:, K:2 * K], AF.Abs), ["pz:d"], [oz], K)
+        for qd in range(8 - NDP):
+            bk = bank()
+            for i in range(2):
+                r = qd * 2 + i
+                ob, lh = T[bk][:, i * K:(i + 1) * K], T.RALL[:, r * 128:(r + 1) * 128]
+                P([mm(ob, lh, T.SH[:, r0:r0 + K], True, False), mm(ob, lh, T.SL[:, r0:r0 + K], False, True)], ["RALL"] + hi + lo, [bk + ":%d" % i], 2 * K)
+            if qd == 0:
+                A(act(T.S8[:], T[bk][:, 0:K], AF.Identity, T.PF[:, 16 + t:17 + t]), [bk + ":0", "PF%d" % (16 + t)], ["S8"], K)
+            A(act(T.WR[:, qd * 512:(qd + 1) * 512], T[bk][:], AF.Copy), [bk + ":0", bk + ":1"], ["WR%d" % qd], 512)
+        if NDP:
+            DS([dma("S", T.ER[:, 0:16, :], T.WR[:, 0:K]), dma("S", T.ER[:, 16:32, :], T.WR[:, 0:K])], ["WR0"], ["ER"], 2300.0)
+            DS([dma("S", T.WR[:, r * K:(r + 1) * K], T.ER[:, r:r + 16, :]) for r in range(16 - 2 * NDP, 16)], ["ER"], ["WR%d" % x for x in range(8 - NDP, 8)], 2000.0 + 500.0 * 2 * NDP)
+        V(tt(T.AB[:], T.T2[:].indirect(LU[:, 80:96]), BB[:], OP.mult), ["T2", bbk, "LU2"], ["AB"], K, G_R)
+        V(tt(T.AD[:], T.PC[:, 0:K * (t + 2)].indirect(LU[:, 96:112]), T.AB[:], OP.max), ["PC%d" % x for x in range(t + 2)] + ["AB", "LU2"], ["AD"], K, G_R)
+        V(tt(T.QQ[:], T.WR[:].indirect(LU[:, 64:80]), T.AD[:], OP.max), ["WR%d" % x for x in range(8)] + ["AD", "LU2"], ["Q"], K, G_R)
+        V(ts(T.SI[:], T.QQ[:], 8191, OP.bitwise_and), ["Q"], ["SI"], K)
+        if last:
+            V(cp(T.YSF[:], T.SI[:]), ["SI"], ["YSF"], K)
+            D("S", dma("S", T.ys[:], T.YSF[:]), ["YSF"], [])
+            D("S", dma("S", T.yz[:], OZ), [oz], [])
+        else:
+            ou = "OU%d" % par
+            V(cp(T.OU[:, o0:o0 + K], T.SI[:]), ["SI"], [ou], K)
+            send([(T.SU[:, r0 + K:r0 + 2 * K], T.OU[:, o0:o0 + K]), (T.SZ[:, r0 + K:r0 + 2 * K], OZ)], t + 1, 0, "a", [ou, oz],
+                 [x % (t + 1) for x in ("SU%d:0", "SU%d:1", "ZZ%d:0", "ZZ%d:1")])
+            oc, nc, px = slice(o0, o0 + K), slice(r0 + K, r0 + 2 * K), T.pva[:, L:L + K]
+            oh, ol = "OH%d" % par, "OL%d" % par
+            V(cp(px, T.SI[:]), ["SI"], ["pva:x"], K)
+            A(act(T.OH[:, oc], px, AF.Copy), ["pva:x"], [oh], K)
+            V(tt(T.OL[:, oc], px, T.OH[:, oc], OP.subtract), ["pva:x", oh], [ol], K)
+            send([(T.SH[:, nc], T.OH[:, oc]), (T.SL[:, nc], T.OL[:, oc])], t + 1, 0, "b", [oh, ol], [x % (t + 1) for x in ("HI%d:0", "HI%d:1", "LO%d:0", "LO%d:1")])
+            V(tt(T.XS[:], T.XT[:].indirect(LU[:, 48:64]), T.ME[:], OP.add), ["XT", "LU1", "M"], ["XS"], K, G_R)
+            V(ts(T.XD[:], T.XS[:], 1, OP.arith_shift_right), ["XS"], ["XD"], K)
+            V(cp(T.XT[:].indirect(LU[:, 48:64]), T.XD[:]), ["XD", "LU1"], ["XT"], K, 4)
+            P([mm(T.pm[:, 0:16], T.ONES[:, 0:128], T.HD[:], True, True)], ["ONES", "HD"], ["pm:a"], 64)
+            A(lambda: s.activation(out=T.ACT[:], in_=T.pm[:, 0:16], func=AF.Copy, accum_out=T.AR[:]), ["pm:a"], ["AR"], 16, 1.0, 140.0)
+            A(lambda: s.activation(out=T.AC[:], in_=T.AR[:], func=AF.Identity, bias=T.PF[:, 12:13], scale=-1.0), ["AR", "PF12"], ["AC"], 1)
+        pk, PD = ("PL", T.PL[:]) if last else ("PC%d" % (t + 2), T.PC[:, K * (t + 2):K * (t + 3)])
+        V(tt(PD, T.T1[:].indirect(LU[:, 112:128]), T.S8[:], OP.mult), ["T1", "S8", "LU2"], [pk], K, G_R)
+        V(tt(CT, CT, PD, OP.max), ["pm:c", pk], ["pm:c"], K)
+        V(tt(NN[:], T.NV[:, 16 * (t + 2):16 * (t + 3)].indirect(LU[:, 112:128]), NB[:], OP.max), ["NV", "LU2", nb], [nn], K, G_R)
+    NF, nf = T["NB%d" % (RO % 2)], "NB%d" % (RO % 2)
+    V(cp(T.FI[:], CT), ["pm:c"], ["FI"], K)
+    V(ts(T.FJ[:], T.FI[:], 8191, OP.bitwise_and), ["FI"], ["FJ"], K)
+    V(cp(T.FC[:], T.FJ[:]), ["FJ"], ["FC"], K)
+    D("S", dma("S", T.yc[:], T.FC[:]), ["FC"], [])
+    V(cp(T.FN[:], NF[:]), [nf], ["FN"], K)
+    V(ts(T.FM[:], T.FN[:], 8, OP.arith_shift_right, 31, OP.bitwise_and), ["FN"], ["FM"], K)
+    V(ts(T.FL[:], T.FM[:], 1.0, OP.add), ["FM"], ["FL"], K)
+    D("S", dma("S", T.yn[:], T.FL[0:128:16, :]), ["FL"], [])
+
+    lastw, readers, lastb = {}, {}, {}
+    N = len(ops)
+    deps = [dict() for _ in range(N)]
+
+    def dep(i, j, wait):
+        if i != j:
+            deps[i][j] = deps[i].get(j, False) or wait
+
+    for i in range(N):
+        op = ops[i]
+        for r in op["r"]:
+            if r in lastw:
+                dep(i, lastw[r], True)
+            readers.setdefault(r, []).append(i)
+        for w in op["w"]:
+            acc = op["q"] == "T" and w.startswith("pv")
+            if w in lastw:
+                dep(i, lastw[w], not (acc and ops[lastw[w]]["q"] == "T"))
+            for j in readers.get(w, []):
+                dep(i, j, True)
+            lastw[w] = i
+            readers[w] = []
+        for b in op["banks"]:
+            if b in lastb:
+                dep(i, lastb[b], ops[lastb[b]]["q"] != op["q"])
+            lastb[b] = i
+
+    if "order" not in ORDER:
+        ORDER["order"] = make_order(ops, deps)[0]
+    order = ORDER["order"]
+
+    CN = {"V": "cV", "A": "cA", "T": "cT", "G": "cG"}
+    count = {q: 0 for q in CN}
+    known = {q: {} for q in eng}
+    done, clock = {}, {}
+    locsum = 0
+    for i in order:
+        op = ops[i]
+        q = op["q"]
+        need = {}
+        for j, wait in deps[i].items():
+            if not wait:
+                continue
+            oj = ops[j]
+            if oj["kind"] == "r" and not any(w in op["r"] or w in op["w"] for w in oj["w"]):
+                sem, val, cl = oj["lsem"], oj["amount"], {}
+            else:
+                sem, val = done[j]
+                cl = clock[j] if oj["kind"] != "r" else {}
+            if known[q].get(sem, 0) >= val:
+                continue
+            if sem not in need or need[sem][0] < val:
+                need[sem] = (val, cl)
+        for sem in sorted(need):
+            val, cl = need[sem]
+            if any(o2 != sem and need[o2][1].get(sem, 0) >= val and not (cl.get(o2, 0) >= need[o2][0]) for o2 in need):
+                continue
+            eng[q].wait_ge(T.sem[sem], int(val))
+        for sem in need:
+            val, cl = need[sem]
+            known[q][sem] = max(known[q].get(sem, 0), val)
+            for s2 in cl:
+                known[q][s2] = max(known[q].get(s2, 0), cl[s2])
+        for f in op["fns"]:
+            ins = f()
+            if op["kind"] == "c":
+                ins.then_inc(T.sem[CN[q]], 1)
+                count[q] += 1
+            elif op["kind"] == "d":
+                ins.then_inc(T.sem[op["sem"]], 16)
+        if op["kind"] == "c":
+            done[i] = (CN[q], count[q])
+        else:
+            done[i] = (op["sem"], op["amount"])
+            if op["kind"] == "r" and "lsem" not in op:
+                locsum += n_eng
+        clock[i] = dict(known[q])
+        clock[i][done[i][0]] = max(clock[i].get(done[i][0], 0), done[i][1])
+    for q in CN:
+        if count[q]:
+            g.wait_ge(T.sem[CN[q]], count[q])
+    g.wait_ge(T.sem.loc, locsum)
+    for op in ops:
+        if op["kind"] in ("d", "r") and known["G"].get(op["sem"], 0) < op["amount"]:
+            g.wait_ge(T.sem[op["sem"]], op["amount"])
+        if "lsem" in op and known["G"].get(op["lsem"], 0) < n_eng:
+            g.wait_ge(T.sem[op["lsem"]], n_eng)

@@ -3,108 +3,120 @@ from concourse.bass import DstId, RemoteDMATransfer
 from concourse.mybir import AluOpType as OP, AxisListType, ActivationFunctionType as AF
 
 RO = 6
-CH, L = 2, 128
-K = CH * L
-NDP = 4
-PXN = 32
-PIECES = [(0, 64, "A"), (64, 32, "V"), (96, 32, "V"), (128, 64, "A"), (192, 64, "A")]
-CHUNKS = [(0, 128, 0), (128, 64, 0), (192, 64, 0)]
-SIGNQ = 1
-DELTA = 300.0
+NH, L = 2, 128
+K = NH * L
+CM = 16383
+PV = 65536.0
+DP = 3088
+RW = DP + 16 * L
+HC = float(DP - 1)
+INV = 272
+TAG = 16384.0
+P = {
+    "pieces": [[(0, 32, "A"), (32, 32, "V"), (64, 32, "A"), (96, 32, "A")], [(0, 32, "A"), (32, 32, "A"), (64, 32, "A"), (96, 32, "A")]],
+    "chunks": [[(0, 64), (64, 64)], [(0, 64), (64, 64)]],
+    "pxn": 32,
+    "passes": 6, "lead": 0.0,
+    "gr": 1.55, "pe": 0.5, "wlat": 6000.0, "slat": 2500.0,
+    "zha": [1, 1], "pda": [0, 0], "xsa": [1, 0], "msp": [0, 1], "blat": 12000.0, "sq": 5, "sqc": [(1, 1)],
+    "adp": [2, 2],
+    "bonus": {"CT": -20000.0, "TG": -20000.0},
+}
 
 SCRATCH = {
-    "XT": ("sbuf", [128, 8192], "bfloat16"), "PC": ("sbuf", [128, 2048], "float32"),
-    "NB0": ("sbuf", [128, 256], "bfloat16"), "NB1": ("sbuf", [128, 256], "bfloat16"),
-    "EALL": ("sbuf", [128, 2048], "bfloat16"), "RALL": ("sbuf", [128, 2048], "bfloat16"), "RESET": ("sbuf", [128, 2048], "bfloat16"),
-    "BO": ("sbuf", [128, 128], "bfloat16"), "IDM": ("sbuf", [128, 128], "bfloat16"), "NID": ("sbuf", [128, 128], "bfloat16"),
-    "ONES": ("sbuf", [128, 256], "bfloat16"), "DIAG": ("sbuf", [128, 256], "bfloat16"), "WALL": ("sbuf", [128, 2048], "float16"),
-    "ACT": ("sbuf", [128, 16], "float32"), "KF": ("sbuf", [128, 16], "float32"), "T1": ("sbuf", [128, 16], "bfloat16"), "T2": ("sbuf", [128, 32], "bfloat16"),
-    "NV": ("sbuf", [128, 128], "float32"), "SEL": ("sbuf", [128, 128], "bfloat16"),
-    "IO1": ("sbuf", [128, 2048], "bfloat16"), "IO2": ("sbuf", [128, 128], "bfloat16"), "IO3": ("sbuf", [128, 256], "bfloat16"),
-    "IO4": ("sbuf", [128, 128], "bfloat16"), "IO5": ("sbuf", [128, 128], "int32"), "RL1": ("sbuf", [128, 128], "int32"),
-    "RL2": ("sbuf", [128, 128], "int32"), "RLU": ("sbuf", [128, 128], "uint16"), "K0": ("sbuf", [128, 16], "int32"),
-    "KT": ("sbuf", [128, 16], "int32"), "KM": ("sbuf", [128, 16], "int32"), "K32": ("sbuf", [128, 16], "int32"),
+    "XT": ("sbuf", [128, 8192], "bfloat16"), "RP": ("sbuf", [128, NH * RW], "bfloat16"), "GE": ("sbuf", [128, 16 * K], "bfloat16"),
+    "W0": ("sbuf", [128, 32 * L], "int32"), "W1": ("sbuf", [128, 32 * L], "int32"), "ED": ("dram", [RO * NH, 128, L], "int32"),
+    "PC0": ("sbuf", [128, INV + K], "float32"), "PC1": ("sbuf", [128, INV + K], "float32"),
+    "EB": ("sbuf", [128, 144], "bfloat16"), "WB": ("sbuf", [128, 144], "float16"), "RESET": ("sbuf", [128, 1152], "bfloat16"),
+    "EH": ("sbuf", [128, 144], "bfloat16"), "D8": ("sbuf", [128, 128], "bfloat16"),
+    "BO": ("sbuf", [128, 128], "bfloat16"), "TRI": ("sbuf", [128, 128], "bfloat16"), "IDM": ("sbuf", [128, 128], "bfloat16"),
+    "NID": ("sbuf", [128, 128], "bfloat16"), "ID2": ("sbuf", [128, 128], "bfloat16"), "ONF": ("sbuf", [128, 128], "float32"),
+    "SEL": ("sbuf", [128, 128], "bfloat16"), "IO2": ("sbuf", [128, 128], "bfloat16"), "IO4": ("sbuf", [128, 144], "bfloat16"),
+    "K0": ("sbuf", [128, 16], "int32"), "KT": ("sbuf", [128, 16], "float32"), "KF": ("sbuf", [128, 16], "float32"),
+    "K32": ("sbuf", [128, 16], "int32"), "KK": ("sbuf", [128, 16], "bfloat16"),
     "PI": ("sbuf", [128, 8], "int32"), "PF": ("sbuf", [128, 24], "float32"), "F4": ("sbuf", [128, 16], "float32"),
     "Z0": ("sbuf", [128, 16], "float32"), "PWS": ("sbuf", [128, 16], "float32"), "PWM": ("sbuf", [128, 16], "float32"),
     "PW": ("sbuf", [128, 1], "float32"), "WI": ("sbuf", [128, 8], "int32"), "WF": ("sbuf", [128, 8], "float32"),
-    "LNI": ("sbuf", [128, 256], "int32"), "LNB": ("sbuf", [128, 256], "bfloat16"), "PCM": ("sbuf", [128, 256], "bfloat16"),
+    "LNI": ("sbuf", [128, 256], "int32"), "LNB": ("sbuf", [128, 256], "bfloat16"), "PCM": ("sbuf", [128, 256], "float32"),
     "STI": ("sbuf", [128, 256], "int32"), "BAI": ("sbuf", [128, 256], "int32"), "COI": ("sbuf", [128, 256], "int32"),
-    "HD": ("sbuf", [128, 16], "bfloat16"), "AR": ("sbuf", [128, 1], "float32"), "AC": ("sbuf", [128, 1], "float32"),
-    "FI": ("sbuf", [128, 256], "int32"), "FJ": ("sbuf", [128, 256], "int32"), "FC": ("sbuf", [128, 256], "float32"),
-    "FN": ("sbuf", [128, 256], "int32"), "FM": ("sbuf", [128, 256], "int32"), "FL": ("sbuf", [128, 256], "float32"),
-    "ER": ("dram", [8, 32, 256], "float32"), "YSF": ("sbuf", [128, 256], "float32"),
-    "RP": ("sbuf", [128, 8192], "bfloat16"),
-    "GE": ("sbuf", [128, 4096], "bfloat16"), "WR": ("sbuf", [128, 4096], "float32"), "HP": ("sbuf", [128, 256], "bfloat16"),
-    "ZH": ("sbuf", [128, 256], "bfloat16"), "DA": ("sbuf", [128, 512], "float32"), "DB": ("sbuf", [128, 512], "float32"),
-    "SM": ("sbuf", [128, 512], "int32"), "SF": ("sbuf", [128, 32], "float32"), "LU": ("sbuf", [128, 128], "uint16"),
-    "ME": ("sbuf", [128, 256], "bfloat16"), "YE": ("sbuf", [128, 256], "bfloat16"), "XS": ("sbuf", [128, 256], "int32"),
-    "XD": ("sbuf", [128, 256], "int32"), "AB": ("sbuf", [128, 256], "float32"), "AD": ("sbuf", [128, 256], "float32"),
-    "QQ": ("sbuf", [128, 256], "int32"), "SI": ("sbuf", [128, 256], "int32"), "S8": ("sbuf", [128, 256], "float32"),
-    "MD": ("sbuf", [128, 256], "bfloat16"), "ML": ("sbuf", [128, 256], "bfloat16"), "PL": ("sbuf", [128, 256], "float32"),
-    "pz": ("psum", [128, 512], "float32"), "pva": ("psum", [128, 512], "float32"), "pvb": ("psum", [128, 512], "float32"),
-    "pu": ("psum", [128, 512], "float32"), "pm": ("psum", [128, 512], "float32"), "pr0": ("psum", [128, 512], "float32"),
-    "pr1": ("psum", [128, 512], "float32"), "pr2": ("psum", [128, 512], "float32"),
+    "PL": ("sbuf", [128, 256], "float32"), "S0": ("sbuf", [128, 256], "int32"),
+    "ACT": ("sbuf", [128, 16], "float32"), "AR": ("sbuf", [128, 1], "float32"), "AC": ("sbuf", [128, 1], "float32"),
+    "HP": ("sbuf", [128, K], "bfloat16"), "ZH": ("sbuf", [128, K], "bfloat16"), "MY": ("sbuf", [128, 2 * K], "bfloat16"),
+    "SF": ("sbuf", [128, 16], "float32"), "DB": ("sbuf", [128, 32], "float32"), "HN": ("sbuf", [128, 16], "float32"),
+    "HB": ("sbuf", [128, 16], "bfloat16"), "YQ": ("sbuf", [128, 16], "float32"), "XX": ("sbuf", [128, 16], "float32"),
+    "PA": ("sbuf", [128, 32], "float32"), "SM": ("sbuf", [128, 256], "int32"), "LU": ("sbuf", [128, 128], "uint16"),
+    "XS": ("sbuf", [128, K], "int32"), "XD": ("sbuf", [128, K], "int32"), "AB": ("sbuf", [128, K], "float32"),
+    "SG": ("sbuf", [128, K], "bfloat16"), "Q1": ("sbuf", [128, K], "float32"), "Q2": ("sbuf", [128, K], "int32"),
+    "FC": ("sbuf", [128, K], "float32"), "FL": ("sbuf", [128, K], "float32"), "YSF": ("sbuf", [128, K], "float32"),
+    "NBO": ("sbuf", [128, 128], "bfloat16"), "DN": ("sbuf", [128, 128], "bfloat16"), "XG": ("sbuf", [128, K], "bfloat16"),
+    "SN": ("sbuf", [128, K], "bfloat16"),
+    "SU": ("sbuf", [128, RO * K], "uint16"), "SZ": ("sbuf", [128, RO * K], "bfloat16"),
+    "OU": ("sbuf", [128, 2 * K], "uint16"), "OZ": ("sbuf", [128, 2 * K], "bfloat16"), "OF": ("sbuf", [128, 2 * K], "int32"),
 }
+for _n in ("pz0", "pz1", "pv0", "pv1", "pu0", "pu1", "pm", "px"):
+    SCRATCH[_n] = ("psum", [128, 512], "float32")
 for _d in range(4):
-    SCRATCH["BB%d" % _d] = ("sbuf", [128, 256], "float32")
-for _n, _ty in (("U", "uint16"), ("Z", "bfloat16"), ("H", "bfloat16"), ("L", "bfloat16")):
-    SCRATCH["S" + _n] = ("sbuf", [128, RO * 256], _ty)
-    SCRATCH["O" + _n] = ("sbuf", [128, 2 * 256], _ty)
+    SCRATCH["BB%d" % _d] = ("sbuf", [128, K], "float32")
 
-SEMAPHORES = ["cV", "cA", "cT", "cG", "loc"] + ["lo%d" % i for i in range(20)] + ["dm%d" % i for i in range(24)] + ["bs%d" % d for d in (1, 2, 3)] + \
-             ["ar%d%d%s" % (t, c, s) for t in range(1, RO) for c in range(CH) for s in "ab"]
+SEMAPHORES = ["cV", "cA", "cT", "cG", "loc"] + ["lo%d" % i for i in range(20)] + ["dm%d" % i for i in range(32)] + ["bs%d" % d for d in (1, 2, 3)] + \
+             ["ar%d%d%s" % (t, c, s) for t in range(1, RO) for c in range(NH) for s in "ab"]
 
 ORDER = {}
-BONUS = {"IO": -2000.0, "HP": 8000.0, "XS": -20000.0, "OL": -8000.0, "pa": -2000.0, "SU": -2000.0, "pr": -20000.0, "NB": -20000.0, "pm": 8000.0,
-         "uv": -8000.0, "e": -20000.0, "HI": 2000.0, "XT": -20000.0, "pz": -20000.0}
 CYC = 0.83 * 1.2
-G_R = 1.55
 
 
-def make_order(ops, deps, log=None):
+def place(ops, pred, key):
     n = len(ops)
     succ = [[] for _ in range(n)]
     for i in range(n):
-        for j in deps[i]:
-            succ[j].append(i)
-    prio = [0.0] * n
-    for i in range(n - 1, -1, -1):
-        op = ops[i]
-        prio[i] = op["cost"] + max([op["lat"] + prio[x] for x in succ[i]] + [0.0])
-    for i in range(n):
-        prio[i] += max([BONUS.get(w.split(":")[0].rstrip("0123456789"), 0.0) for w in ops[i]["w"]] + [-9e9]) if ops[i]["w"] else 0.0
-    left = [len(deps[i]) for i in range(n)]
+        for j, lat in pred[i]:
+            succ[j].append((i, lat))
+    left = [len(pred[i]) for i in range(n)]
     est = [0.0] * n
-    qs = ["V", "A", "T", "S", "G"]
-    ready = {q: [] for q in qs}
+    start = [0.0] * n
+    busy = {}
+    ready = [i for i in range(n) if left[i] == 0]
+    while ready:
+        i = min(ready, key=lambda x: (key[x], x))
+        ready.remove(i)
+        c, t = ops[i]["cost"], est[i]
+        line = busy.setdefault(ops[i]["q"], [])
+        x = len(line)
+        while x > 0 and line[x - 1][1] > t:
+            x -= 1
+        while x < len(line) and line[x][0] < t + c:
+            t = max(t, line[x][1])
+            x += 1
+        line.insert(x, (t, t + c))
+        start[i] = t
+        for y, lat in succ[i]:
+            est[y] = max(est[y], t + c + lat)
+            left[y] -= 1
+            if left[y] == 0:
+                ready.append(y)
+    return start
+
+
+def make_order(ops, deps):
+    n = len(ops)
+    fwd = [[(j, ops[j]["lat"] if (w or ops[j]["q"] != ops[i]["q"]) else 0.0) for j, w in deps[i].items()] for i in range(n)]
+    bwd = [[] for _ in range(n)]
     for i in range(n):
-        if left[i] == 0:
-            ready[ops[i]["q"]].append(i)
-    qt = {q: 0.0 for q in qs}
-    order = []
-    while len(order) < n:
-        best = None
-        for q in qs:
-            if not ready[q]:
-                continue
-            m0 = max(qt[q], min([est[i] for i in ready[q]]))
-            if best is None or m0 < best[0]:
-                best = (m0, q)
-        m0, q = best
-        i = max([x for x in ready[q] if est[x] <= m0 + DELTA], key=lambda x: (prio[x], -x))
-        st = max(qt[q], est[i])
-        ready[q].remove(i)
-        qt[q] = st + ops[i]["cost"]
-        order.append(i)
-        if log is not None:
-            log.append((i, st))
-        for x in succ[i]:
-            cross = ops[x]["q"] != q or deps[x][i]
-            est[x] = max(est[x], qt[q] + (ops[i]["lat"] if cross else 0.0))
-            left[x] -= 1
-            if left[x] == 0:
-                ready[ops[x]["q"]].append(x)
-    return order, max(qt.values())
+        for j, lat in fwd[i]:
+            bwd[j].append((i, lat))
+    tail = [0.0] * n
+    for i in range(n - 1, -1, -1):
+        tail[i] = ops[i]["cost"] + max([lat + tail[x] for x, lat in bwd[i]] + [ops[i]["lat"]])
+    key, best = [-tail[i] - ops[i]["bonus"] for i in range(n)], None
+    for _ in range(P["passes"]):
+        st = place(ops, fwd, key)
+        end = max(st[i] + ops[i]["cost"] + ops[i]["lat"] for i in range(n))
+        if best is None or end < best[0]:
+            best = (end, st)
+        back = place(ops, bwd, [-(st[i] + ops[i]["cost"]) for i in range(n)])
+        key = [-(back[i] + ops[i]["cost"]) for i in range(n)]
+    ORDER["plan"], ORDER["ops"] = best, ops
+    return sorted(range(n), key=lambda i: (best[1][i], i))
 
 
 def rank_program(g, core, T, topo):
@@ -114,37 +126,34 @@ def rank_program(g, core, T, topo):
     n_ranks = len(T.cores)
     ops = []
     eng = {"V": g.vector, "A": g.scalar, "T": g.tensor, "S": g.sync, "G": g}
+    G_R = P["gr"]
+    now = [0.0, -1]
 
-    def add(q, fns, reads, writes, cost, lat=60.0, kind="c", sem=None, amount=0, banks=()):
+    def add(q, fns, reads, writes, cost, lat=60.0, kind="c", sem=None, amount=0):
+        banks = sorted(set(k.split(":")[0] for k in list(reads) + list(writes) if k.startswith("p")))
         ops.append({"q": q, "fns": fns if isinstance(fns, list) else [fns], "r": list(reads), "w": list(writes), "cost": cost,
-                    "lat": lat, "kind": kind, "sem": sem, "amount": amount, "banks": list(banks)})
+                    "lat": lat, "kind": kind, "sem": sem, "amount": amount, "banks": banks, "bonus": now[0], "t": now[1]})
 
     def vc(n, rate=1.0):
         return max(64.0, n * rate) * CYC
 
-    def isps(keys):
-        return sorted(set(k.split(":")[0] for k in keys if k.startswith("p")))
+    def V(fn, reads, writes, n=16, rate=1.0):
+        add("V", fn, reads, writes, vc(n, rate) + (60.0 if rate in (G_R, 3.8) else 0.0))
 
-    def V(fn, reads, writes, n, rate=1.0):
-        add("V", fn, reads, writes, vc(n, rate), banks=isps(list(reads) + list(writes)))
+    def A(fn, reads, writes, n=16, rate=1.0, extra=0.0):
+        add("A", fn, reads, writes, vc(n, rate) + extra + (75.0 if rate == G_R else 0.0))
 
-    def A(fn, reads, writes, n, rate=1.0, extra=0.0):
-        add("A", fn, reads, writes, vc(n, rate) + extra, banks=isps(list(reads) + list(writes)))
-
-    def P(fns, reads, writes, cyc):
-        add("T", fns, reads, writes, cyc * 0.8, banks=isps(list(reads) + list(writes)))
+    def PE(fns, reads, writes, cyc):
+        add("T", fns, reads, writes, cyc * P["pe"])
 
     def G(fn, reads, writes, n):
-        add("G", fn, reads, writes, 130 + 2 * n * CYC)
+        add("G", fn, reads, writes, 150 + 2 * n * CYC)
 
     ndma = [0]
 
-    def D(q, fn, reads, writes, lat=2500.0):
-        add(q, fn, reads, writes, 60.0, lat, "d", "dm%d" % ndma[0], 16)
-        ndma[0] += 1
-
-    def DS(fns, reads, writes, lat):
-        add("S", fns, reads, writes, 60.0 * len(fns), lat, "d", "dm%d" % ndma[0], 16 * len(fns))
+    def D(q, fns, reads, writes, lat=2500.0):
+        fns = fns if isinstance(fns, list) else [fns]
+        add(q, fns, reads, writes, 60.0 * len(fns), lat, "d", "dm%d" % ndma[0], 16 * len(fns))
         ndma[0] += 1
 
     v, s, te = g.vector, g.scalar, g.tensor
@@ -163,8 +172,8 @@ def rank_program(g, core, T, topo):
     def scan(o, d0, d1, op1, ini=0.0):
         return lambda: v.tensor_tensor_scan(out=o, data0=d0, data1=d1, initial=ini, op0=OP.mult, op1=op1)
 
-    def act(o, a, f, bias=0.0):
-        return lambda: s.activation(out=o, in_=a, func=f, bias=bias)
+    def act(o, a, f, bias=0.0, scale=1.0):
+        return lambda: s.activation(out=o, in_=a, func=f, bias=bias, scale=scale)
 
     def mm(o, lh, rh, st, sp):
         return lambda: te.matmul(out=o, lhsT=lh, rhs=rh, start=st, stop=sp)
@@ -180,74 +189,79 @@ def rank_program(g, core, T, topo):
     def dma(q, o, a):
         return lambda: eng[q].dma_start(out=o, in_=a)
 
-    V(ms(T.PF[:, 9:10], 0.5), [], ["PF9"], 1)
-    V(ms(T.PF[:, 10:11], 64.0), [], ["PF10"], 1)
-    V(ms(T.PF[:, 11:12], 8.5), [], ["PF11"], 1)
-    V(ms(T.PF[:, 12:13], 2040.0 - 0.4375), [], ["PF12"], 1)
-    for t in range(RO):
-        V(ms(T.PF[:, 16 + t:17 + t], 8192.0 * (t + 2)), [], ["PF%d" % (16 + t)], 1)
-
-    D("S", dma("S", T.XT[:], T.xt[:]), [], ["XT"], 9000.0)
     D("A", dma("A", T.STI[:], T.stk[:]), [], ["STI"])
-    D("A", dma("A", T.SZ[:, 0:256], T.z[:]), [], ["ZZ0:0", "ZZ0:1"])
-    D("S", dma("S", T.WI[:, 0:1], T.w[:]), [], ["WI"])
-    D("S", dma("S", T.BAI[:], T.bas[:]), [], ["BAI"])
-    D("A", dma("A", T.LNI[0:8, :], T.ln[:]), [], ["LNI"])
-    D("S", dma("S", T.COI[:], T.con[:]), [], ["COI"])
+    D("A", dma("A", T.SZ[:, 0:K], T.z[:]), [], ["ZZ0:0", "ZZ0:1"])
+    D("S", dma("S", T.XT[:], T.xt[:]), [], ["XT", "XL"], 9000.0)
+    D("S", dma("S", T.WI[:, 0:1], T.w[:]), [], ["WI"], 9000.0)
+    D("S", dma("S", T.BAI[:], T.bas[:]), [], ["BAI"], 9000.0)
+    D("S", dma("S", T.LNI[0:8, :], T.ln[:]), [], ["LNI"], 9000.0)
+    D("S", dma("S", T.COI[:], T.con[:]), [], ["COI"], 9000.0)
 
+    V(ms(T.PF[:, 10:11], math.exp(5.0)), [], ["PF10"])
+    V(ms(T.PF[:, 11:12], 149.23), [], ["PF11"])
+    V(ms(T.PF[:, 12:13], 2040.0 - 0.4375), [], ["PF12"])
     G(io(T.PI[:, 0:1], [[0, 1]], 1, False), [], ["PI0"], 1)
-    V(ts(T.PI[:, 1:2], T.PI[:, 0:1], 15, OP.bitwise_and), ["PI0"], ["PI1"], 1)
-    V(ts(T.PI[:, 2:3], T.PI[:, 0:1], 112, OP.bitwise_and), ["PI0"], ["PI2"], 1)
-    V(cp(T.PF[:, 0:3], T.PI[:, 0:3]), ["PI0", "PI1", "PI2"], ["PF0"], 3)
+    V(ts(T.PI[:, 1:2], T.PI[:, 0:1], 15, OP.bitwise_and), ["PI0"], ["PI1"])
+    V(ts(T.PI[:, 2:3], T.PI[:, 0:1], 112, OP.bitwise_and), ["PI0"], ["PI2"])
+    V(cp(T.PF[:, 0:3], T.PI[:, 0:3]), ["PI0", "PI1", "PI2"], ["PF0"])
     pf, pmf, p16 = T.PF[:, 0:1], T.PF[:, 1:2], T.PF[:, 2:3]
-    V(ts(T.PF[:, 3:4], pmf, -1.0, OP.mult, 16.0, OP.add), ["PF0"], ["PF3"], 1)
-    V(ts(T.PF[:, 4:5], pmf, -1.0, OP.mult, 15.0, OP.add), ["PF0"], ["PF4"], 1)
-    V(ts(T.PF[:, 5:6], pf, 16.0, OP.mult), ["PF0"], ["PF5"], 1)
-    V(ts(T.PF[:, 6:7], pmf, 256.0, OP.mult), ["PF0"], ["PF6"], 1)
-    V(ts(T.PF[:, 7:8], pmf, 15.5 - 4 * SIGNQ, OP.is_gt, -7.5, OP.mult), ["PF0"], ["PF7"], 1)
-    V(ts(T.PF[:, 8:9], T.PF[:, 7:8], 8.5, OP.add), ["PF7"], ["PF8"], 1)
-    G(io(T.IO4[:], [[1, 128]], 0), [], ["IO4"], 128)
-    G(io(T.RL1[:], [[1, 16], [0, 8]], 1, False), [], ["RL1"], 128)
-    G(io(T.IO5[:], [[0, 16], [16, 8]], 0, False), [], ["IO5"], 128)
-    G(io(T.IO3[:], [[0, 16], [1, 16]], 0), [], ["IO3"], 256)
-    G(io(T.IO1[:], [[-1, 16], [1, 128]], 0), [], ["IO1"], 2048)
+    V(ts(T.PF[:, 3:4], p16, 16.0, OP.add), ["PF0"], ["PF3"])
+    V(ts(T.PF[:, 4:5], pmf, -1.0, OP.mult, 15.0, OP.add), ["PF0"], ["PF4"])
+    V(ts(T.PF[:, 5:6], pf, 16.0, OP.mult), ["PF0"], ["PF5"])
+    V(ts(T.PF[:, 6:7], pmf, 0.5, OP.is_gt), ["PF0"], ["PF6"])
+    G(io(T.IO4[:], [[1, 144]], 0), [], ["IO4"], 144)
     G(io(T.IO2[:], [[16, 8], [0, 16]], 0), [], ["IO2"], 128)
     G(io(T.K0[:], [[16, 16]], 0, False), [], ["K0"], 16)
-    G(io(T.NV[:], [[8192, 8], [256, 16]], 0, True, -256), [], ["NV"], 128)
-    V(ms(T.NV[:, 0:128:16], 0.0), [], ["NV"], 8)
-    V(ts(T.IDM[:], T.IO4[:], pf, OP.is_equal), ["IO4", "PF0"], ["IDM"], 128, .5)
-    V(ts(T.NID[:], T.IDM[:], -1.0, OP.mult), ["IDM"], ["NID"], 128, .5)
     V(cp(T.SU[:, 0:K], T.STI[:]), ["STI"], ["SU0:0", "SU0:1"], K)
-    V(cp(T.SH[:, 0:K], T.STI[:]), ["STI"], ["HI0:0", "HI0:1"], K)
-    V(tt(T.SL[:, 0:K], T.STI[:], T.SH[:, 0:K], OP.subtract), ["STI", "HI0:0", "HI0:1"], ["LO0:0", "LO0:1"], K, 2)
-    V(ts(T.RL2[:], T.RL1[:], 15, OP.bitwise_and), ["RL1"], ["RL2"], 128)
-    V(tt(T.RL1[:], T.RL2[:], T.IO5[:], OP.add), ["RL2", "IO5"], ["RL1"], 128, 2)
-    V(cp(T.RLU[:], T.RL1[:]), ["RL1"], ["RLU"], 128)
-    A(act(T.RALL[:], T.IDM[:, 0:128].indirect(T.RLU[:, 0:128]), AF.Copy), ["IDM", "RLU"], ["RALL"], 2048, G_R)
-    V(ts(T.EALL[:], T.IO1[:], p16, OP.is_equal), ["IO1", "PF0"], ["EALL"], 2048, .5)
-    V(ms(T.RESET[:], 1.0), [], ["RESET"], 2048, .5)
-    V(ms(T.RESET[:, 0:2048:16], 0.0), [], ["RESET"], 128, .5)
-    V(ts(T.DIAG[:], T.IO3[:], pmf, OP.is_equal), ["IO3", "PF0"], ["DIAG"], 256, .5)
-    V(ts(T.T1[:], T.IO4[:, 0:16], pmf, OP.is_gt), ["IO4", "PF0"], ["T1"], 16)
-    V(ts(T.T2[:], T.IO4[:, 0:32], T.PF[:, 3:4], OP.is_ge), ["IO4", "PF3"], ["T2"], 32)
-    V(ms(T.T2[:, 16:32], 0.0), [], ["T2"], 16)
+    V(ts(T.S0[:], T.STI[:], -1.0, OP.mult, float(CM), OP.add), ["STI"], ["S0"], K)
+    for h in range(NH):
+        D("S", dma("S", T.ED[h], T.S0[:, h * L:(h + 1) * L]), ["S0"], ["ED0:%d" % h])
+    V(ts(T.IDM[:], T.IO4[:, 0:128], pf, OP.is_equal), ["IO4", "PF0"], ["IDM"], 128, .5)
+    V(ts(T.NID[:], T.IDM[:], -1.0, OP.mult), ["IDM"], ["NID"], 128, .5)
+    V(ts(T.ID2[:], T.IDM[:], 2.0, OP.mult), ["IDM"], ["ID2"], 128, .5)
+    V(ts(T.EB[:], T.IO4[:], T.PF[:, 3:4], OP.is_equal), ["IO4", "PF3"], ["EB"], 144, .5)
+
+    def toward(M, i):
+        return M[:, 16 - i:144 - i]
+
+    V(ms(T.RESET[:, 512:], 1.0), [], ["RESET"], 640, .5)
+    V(ms(T.RESET[:, 512:1024:16], 0.0), [], ["RESET"], 64, .5)
+    SQ = P["sq"]
+    if P["sqc"]:
+        V(ms(T.PF[:, 9:10], 0.5), [], ["PF9"])
+        V(ts(T.EH[:], T.EB[:], 0.5, OP.mult), ["EB"], ["EH"], 144, .5)
+        V(ts(T.PF[:, 7:8], pmf, 15.5 - SQ, OP.is_gt, 8.0, OP.mult), ["PF0"], ["PF7"])
+        V(ts(T.D8[:], T.IDM[:], T.PF[:, 7:8], OP.mult), ["IDM", "PF7"], ["D8"], 128, .5)
+    for h in range(NH):
+        V(ms(T.RP[:, h * RW + 16 * L:h * RW + DP], 0.0), [], ["GAP%d" % h], DP - 16 * L, .5)
     V(ts(T.BO[:], T.IO2[:], p16, OP.is_equal), ["IO2", "PF0"], ["BO"], 128, .5)
-    V(ms(T.ONES[:], 1.0), [], ["ONES"], 256, .5)
-    V(ts(T.KT[:], T.K0[:], pmf, OP.add), ["K0", "PF0"], ["KT"], 16)
-    V(ts(T.KM[:], T.KT[:], 16.0, OP.mult, 4095.0, OP.add), ["KT"], ["KM"], 16)
-    V(ts(T.K32[:], T.KT[:], 32.0, OP.mult), ["KT"], ["K32"], 16)
-    V(ts(T.KF[:], T.KT[:], -16.0 * math.log(4.0), OP.mult, -(4095.0 + 19.0) * math.log(4.0), OP.add), ["KT"], ["KF"], 16)
-    V(ms(T.F4[:], 4.0), [], ["F4"], 16)
-    V(ms(T.Z0[:], 0.0), [], ["Z0"], 16)
-    V(scan(T.PWS[:], T.F4[:], T.Z0[:], OP.add, 64.0), ["F4", "Z0"], ["PWS"], 16)
-    V(ms(T.PWS[:, 15:16], 0.0), [], ["PWS"], 1)
-    V(ts(T.PWM[:], T.IO4[:, 0:16], T.PF[:, 4:5], OP.is_equal), ["IO4", "PF4"], ["PWM"], 16)
-    V(tt(T.PWM[:], T.PWM[:], T.PWS[:], OP.mult), ["PWM", "PWS"], ["PWM"], 16)
-    V(lambda: v.tensor_reduce(out=T.PW[:], in_=T.PWM[:], axis=AxisListType.X, op=OP.add), ["PWM"], ["PW"], 16)
-    V(cp(T.WF[:, 0:1], T.WI[:, 0:1]), ["WI"], ["WF"], 1)
-    V(ts(T.WALL[:], T.EALL[:], T.WF[:, 0:1], OP.mult), ["EALL", "WF"], ["WALL"], 2048, .5)
-    V(ms(T.AC[:], -8.4375), [], ["AC"], 1)
-    V(ts(T.BB0[:], T.BAI[:], 8192.0, OP.add), ["BAI"], ["BB0"], 256)
+    V(ts(T.TRI[:], T.IO4[:, 0:128], pf, OP.is_ge, 512.0, OP.mult), ["IO4", "PF0"], ["TRI"], 128, .5)
+    V(tt(T.TRI[:], T.TRI[:], T.BO[:], OP.mult), ["TRI", "BO"], ["TRI"], 128, 2)
+    V(ms(T.ONF[:], 1.0), [], ["ONF"], 128)
+    V(ts(T.KT[:], T.K0[:], pmf, OP.add), ["K0", "PF0"], ["KT"])
+    V(ts(T.KF[:, 0:8], T.KT[:, 0:8], 16.0, OP.mult, DP + 20.47, OP.add), ["KT"], ["KF"])
+    V(ts(T.K32[:], T.KT[:], 256.0, OP.mult), ["KT"], ["K32"])
+    if any(P["zha"]):
+        V(ts(T.NBO[:], T.BO[:], -1.0, OP.mult), ["BO"], ["NBO"], 128, .5)
+    V(ts(T.DN[:], T.IDM[:], -PV, OP.mult), ["IDM"], ["DN"], 128, .5)
+    A(act(T.PF[:, 13:14], T.PF[:, 10:11], AF.Ln), ["PF10"], ["PF13"], 1, 1.0, 1500.0)
+    V(ts(T.PF[:, 14:15], T.PF[:, 13:14], 0.5, OP.add), ["PF13"], ["PF14"])
+    V(ts(T.KK[:, 0:8], T.KT[:, 0:8], 2.0 / L, OP.mult), ["KT"], ["KK"])
+    V(ms(T.F4[:], math.e), [], ["F4"])
+    V(ms(T.Z0[:], 0.0), [], ["Z0"])
+    V(scan(T.PWS[:], T.F4[:], T.Z0[:], OP.add, math.exp(5.0)), ["F4", "Z0"], ["PWS"])
+    V(ms(T.PWS[:, 15:16], 0.0), [], ["PWS"])
+    V(ts(T.PWM[:], T.IO4[:, 0:16], T.PF[:, 4:5], OP.is_equal), ["IO4", "PF4"], ["PWM"])
+    V(tt(T.PWM[:], T.PWM[:], T.PWS[:], OP.mult), ["PWM", "PWS"], ["PWM"])
+    V(lambda: v.tensor_reduce(out=T.PW[:], in_=T.PWM[:], axis=AxisListType.X, op=OP.add), ["PWM"], ["PW"])
+    V(cp(T.WF[:, 0:1], T.WI[:, 0:1]), ["WI"], ["WF"])
+    V(ts(T.WB[:], T.EB[:], T.WF[:, 0:1], OP.mult), ["EB", "WF"], ["WB"], 144, .5)
+    V(ms(T.AC[:], -8.4375), [], ["AC"])
+    for x in range(2, 31, 4):
+        y = min(x + 4, 31)
+        V(ms(T.W0[:, x * L:y * L], int(PV)), [], ["WM0:%d" % x], (y - x) * L)
+    G(io(T.W1[:, 2 * L:31 * L], [[0, 29 * L]], 0, False, int(PV)), ["IO4", "IO2", "K0", "PI0"], ["WM1:2"], 29 * L)
+    V(ts(T.BB0[:], T.BAI[:], -1.0, OP.mult, 2.0 * CM + 1.0, OP.add), ["BAI"], ["BB0"], K)
 
     def remote(pairs, dst, sem, lsem):
         es = topo.engines(core, dst)
@@ -262,178 +276,188 @@ def rank_program(g, core, T, topo):
     n_eng = len(topo.engines(core, T.cores[(rank + 1) % n_ranks]))
     for d in (1, 2, 3):
         dst = T.cores[(rank + d) % n_ranks]
-        add("G", remote([(T["BB%d" % d][:], T.BB0[:])], dst, "bs%d" % d, "loc"), ["BB0"], ["BB%d" % d], 1000.0, 4000.0, "r", "bs%d" % d, n_eng)
-    V(cp(T.LNB[0:8, :], T.LNI[0:8, :]), ["LNI"], ["LNB"], 256)
-    V(ts(T.SEL[0:8, :], T.IO2[0:8, :], T.PF[0:8, 5:6], OP.is_equal, 256.0, OP.mult), ["IO2", "PF5"], ["SEL"], 128)
-    P([mm(T.pm[:, 0:256], T.SEL[0:8, :], T.LNB[0:8, :], True, True)], ["SEL", "LNB"], ["pm:0"], 256)
-    V(ts(T.NB0[:], T.pm[:, 0:256], 7936.0, OP.add), ["pm:0"], ["NB0"], 256)
-    V(ts(T.PCM[:], T.pm[:, 0:256], T.PF[:, 6:7], OP.is_gt), ["pm:0", "PF6"], ["PCM"], 256)
-    V(ms(T.PC[:, 0:256], 0.0), [], ["PC0"], 256)
-    V(ts(T.PL[:], T.COI[:], 8192.0, OP.add), ["COI"], ["PL"], 256)
-    V(tt(T.PC[:, 256:512], T.PL[:], T.PCM[:], OP.mult), ["PL", "PCM"], ["PC1"], 256, 2)
-    V(cp(T.pm[:, 256:512], T.PL[:]), ["PL"], ["pm:c"], 256)
-    CT = T.pm[:, 256:512]
+        add("G", remote([(T["BB%d" % d][:], T.BB0[:])], dst, "bs%d" % d, "loc"), ["BB0"], ["BB%d" % d], 1000.0, P["blat"], "r", "bs%d" % d, n_eng)
+    V(cp(T.LNB[0:8, :], T.LNI[0:8, :]), ["LNI"], ["LNB"], K)
+    V(ts(T.SEL[0:8, :], T.IO2[0:8, :], T.PF[0:8, 5:6], OP.is_equal), ["IO2", "PF5"], ["SEL"], 128)
+    PE([mm(T.pm[:, 0:K], T.SEL[0:8, :], T.LNB[0:8, :], True, True)], ["SEL", "LNB"], ["pm:0"], K)
+    V(ts(T.pm[:, 0:K], T.pm[:, 0:K], pmf, OP.is_le, 0.5, OP.subtract), ["pm:0", "PF0"], ["pm:0"], K)
+    V(ts(T.PL[:], T.COI[:], 2.0, OP.mult, 2.0 * (PV - CM), OP.add), ["COI"], ["PL"], K)
+    V(tt(T.PC0[:, 0:K], T.pm[:, 0:K], T.PL[:], OP.mult), ["PL", "pm:0"], ["PC0"], K)
+    for x in range(2):
+        V(ms(T["PC%d" % x][:, K:INV], PV), [], ["NO%d" % x])
 
-    rotn = [0]
     nloc = [0]
     nxt = T.cores[(rank + 1) % n_ranks]
-    SM, LU, DA, DB, RP, GE = T.SM, T.LU, T.DA, T.DB, T.RP, T.GE
-    pvs = [T.pva, T.pvb]
+    SM, LU, RP, GE = T.SM, T.LU, T.RP, T.GE
+    PXN = P["pxn"]
 
-    def sm(x, w=16):
-        return SM[:, x * 16:x * 16 + w]
-
-    def bank():
-        rotn[0] += 1
-        return "pr%d" % (rotn[0] % 3)
-
-    def send(pairs, t, c, part, reads, writes):
-        sem, ls = "ar%d%d%s" % (t, c, part), "lo%d" % nloc[0]
+    def send(pairs, t, h, part, reads, writes):
+        sem, ls = "ar%d%d%s" % (t, h, part), "lo%d" % nloc[0]
         nloc[0] += 1
-        add("G", remote(pairs, nxt, sem, ls), reads, writes, 1000.0, 2300.0, "r", sem, n_eng)
+        add("G", remote(pairs, nxt, sem, ls), reads, writes, 1000.0, P["slat"] - 1000.0, "r", sem, n_eng)
         ops[-1]["lsem"] = ls
 
     for t in range(RO):
         last = t == RO - 1
         par = t % 2
-        NB, NN, nb, nn = T["NB%d" % par], T["NB%d" % (1 - par)], "NB%d" % par, "NB%d" % (1 - par)
+        now[1] = t
+        PC, PN, pc, pn = T["PC%d" % par], T["PC%d" % (1 - par)], "PC%d" % par, "PC%d" % (1 - par)
         BB, bbk = T["BB%d" % (t % 4)], "BB%d" % (t % 4)
-        r0, o0 = t * K, par * K
-        su, zz, hi, lo = [["%s%d:%d" % (x, t, c) for c in range(CH)] for x in ("SU", "ZZ", "HI", "LO")]
-        ZA = T.SZ[:, r0:r0 + K]
-        for c in range(CH):
-            P([mm(T.pz[:, c * L:c * L + L], T.IDM[:], T.SZ[:, r0 + c * L:r0 + c * L + L], True, True)], ["IDM", zz[c]], ["pz:z%d" % c], L)
-        for p0, pn, pq in PIECES:
-            a, rk = r0 + p0, ["R%d" % (x // 16) for x in range(p0, p0 + pn, 16)]
-            rd = ["XT", su[p0 // L]]
-            if pq == "A":
-                A(act(RP[:, 16 * p0:16 * (p0 + pn)], T.XT[:].indirect(T.SU[:, a:a + pn]), AF.Copy), rd, rk, pn * 16, G_R, 65.0)
+        for h in range(NH):
+            for p0, n, pq in P["pieces"][h]:
+                a, o = t * K + h * L + p0, RP[:, h * RW + 16 * p0:h * RW + 16 * (p0 + n)]
+                rd, rk = ["XT", "SU%d:%d" % (t, h)], ["R%d:%d" % (h, x // 16) for x in range(p0, p0 + n, 16)]
+                if pq == "A":
+                    A(act(o, T.XT[:].indirect(T.SU[:, a:a + n]), AF.Copy), rd, rk + ["oA"], n * 16, G_R)
+                else:
+                    V(cp(o, T.XT[:].indirect(T.SU[:, a:a + n])), rd, rk, n * 16, G_R)
+        for h in range(NH):
+            r0, o0, c = t * K + h * L, par * K + h * L, slice(h * L, (h + 1) * L)
+            c8 = slice(8 * h, 8 * h + 8)
+            now[0] = P["lead"] * (1 - h)
+            zz, Z = "ZZ%d:%d" % (t, h), T.SZ[:, r0:r0 + L]
+            pz, pv, pu, kz, kv, ku = T["pz%d" % h], T["pv%d" % h], T["pu%d" % h], "pz%d" % h, "pv%d" % h, "pu%d" % h
+            W, wk = T["W%d" % h], "W%d" % h
+            R0 = h * RW
+
+            def k(x):
+                return "%s%d" % (x, h)
+
+            def sm(x):
+                return SM[:, x * 16 + 8 * h:x * 16 + 8 * h + 8]
+
+            src = T.ED[t * NH + h]
+            D("S", [dma("S", W[i:128:16, (15 - i) * L:(31 - i) * L], src) for i in range(16)] + [dma("S", W[:, 31 * L:32 * L], src)],
+              ["ED%d:%d" % (t, h), "XL"] + ["WM%d:%d" % (h, x) for x in range(2, 31, 4)], [wk], P["wlat"])
+            PE([mm(pz[:, 0:L], T.IDM[:], Z, True, True)], ["IDM", zz], [kz + ":z"], L)
+            for ci, (c0, cn) in enumerate(P["chunks"][h]):
+                Rk = ["R%d:%d" % (h, x // 16) for x in range(c0, c0 + cn, 16)]
+                g0 = 16 * (h * L + c0)
+                sq = SQ if (h, ci) in P["sqc"] else 0
+                if sq:
+                    fns = []
+                    for x in range(sq):
+                        ob = pu[:, x * cn:(x + 1) * cn]
+                        fns += [mm(ob, T.NID[:], T.SZ[:, r0 + c0:r0 + c0 + cn], True, False), mm(ob, T.IDM[:], RP[:, R0 + 16 * c0 + 16 - sq + x:R0 + 16 * (c0 + cn):16], False, True)]
+                    PE(fns, ["IDM", "NID", zz] + Rk, [ku + ":g"], 2 * sq * cn)
+                    A(act(GE[:, g0 + (16 - sq) * cn:g0 + 16 * cn], pu[:, 0:sq * cn], AF.Sign, T.PF[:, 9:10]), [ku + ":g", "PF9"],
+                      ["GE%d:%d:%d" % (h, i, ci) for i in range(16 - sq, 16)], sq * cn)
+                    PE([mm(pv[:, c0:c0 + cn], T.D8[:], T.RESET[:, 1024:1024 + cn], True, False)], ["D8", "RESET"], [kv + ":v"], cn)
+                for i in range(1, 16 - sq):
+                    V(tt(GE[:, g0 + i * cn:g0 + (i + 1) * cn], RP[:, R0 + 16 * c0 + i:R0 + 16 * (c0 + cn):16], pz[:, c0:c0 + cn], OP.is_ge),
+                      [kz + ":z"] + Rk, ["GE%d:%d:%d" % (h, i, ci)], cn)
+                for i in range(1, 16):
+                    PE([mm(pv[:, c0:c0 + cn], toward(T.EB if i < 16 - sq else T.EH, i), GE[:, g0 + i * cn:g0 + (i + 1) * cn], i == 1 and not sq, i == 15)],
+                       ["EB", "EH", "GE%d:%d:%d" % (h, i, ci)], [kv + ":v"], cn)
+                for x0 in range(c0, c0 + cn, PXN):
+                    V(scan(RP[:, R0 + DP + 16 * x0:R0 + DP + 16 * (x0 + PXN)], T.RESET[:, 512:512 + 16 * PXN], RP[:, R0 + 16 * x0:R0 + 16 * (x0 + PXN)], OP.max),
+                      ["R%d:%d" % (h, x // 16) for x in range(x0, x0 + PXN, 16)] + ["RESET"], ["PX%d:%d" % (h, x0)], 16 * PXN, .5)
+            allR = ["R%d:%d" % (h, x) for x in range(L // 16)] + ["PX%d:%d" % (h, x) for x in range(0, L, PXN)] + [k("GAP")]
+            HP = T.HP[:, c]
+            V(ts(HP, pv[:, 0:L], 8.5, OP.is_ge, T.PW[:], OP.mult), [kv + ":v", "PW"], [k("HP")], L)
+            PE([mm(pv[:, 3 * L:3 * L + 8], toward(T.EB, i), T.HP[:, h * L + i:(h + 1) * L:16], i == 0, i == 15) for i in range(16)], ["EB", k("HP")], [kv + ":l"], 16 * 64)
+            SF, DM, DY = T.SF[:, c8], T.DB[:, 16 * h:16 * h + 8], T.DB[:, 16 * h + 8:16 * h + 16]
+            A(act(SF, pv[:, 3 * L:3 * L + 8], AF.Ln, T.PF[:, 10:11]), [kv + ":l", "PF10"], [k("SF")])
+            if P["zha"][h]:
+                PE([mm(pv[:, L:2 * L], T.IDM[:], Z, True, False), mm(pv[:, L:2 * L], T.NBO[:], HP, False, True)], ["IDM", "NBO", zz, k("HP")], [kv + ":s"], 2 * L)
             else:
-                V(cp(RP[:, 16 * p0:16 * (p0 + pn)], T.XT[:].indirect(T.SU[:, a:a + pn])), rd, rk, pn * 16, G_R)
-        for c, (c0, cn, sq) in enumerate(CHUNKS):
-            h = c0 // L
-            Z = T.SZ[:, r0 + c0:r0 + c0 + cn]
-            Rk = ["R%d" % (x // 16) for x in range(c0, c0 + cn, 16)]
-            vrows, srows = list(range(1, 16 - 4 * sq)), list(range(16 - 4 * sq, 16))
-            for qd in range(sq):
-                bk = bank()
-                i0 = 16 - 4 * (qd + 1)
-                fns = []
-                for i in range(4):
-                    ob = T[bk][:, i * cn:(i + 1) * cn]
-                    fns += [mm(ob, T.IDM[:], RP[:, 16 * c0 + i0 + i:16 * (c0 + cn):16], True, False), mm(ob, T.NID[:], Z, False, True)]
-                P(fns, ["IDM", "NID", zz[h]] + Rk, [bk + ":s"], 8 * cn)
-                A(act(GE[:, 16 * c0 + i0 * cn:16 * c0 + (i0 + 4) * cn], T[bk][:, 0:4 * cn], AF.Sign, T.PF[:, 9:10]), [bk + ":s", "PF9"],
-                  ["GE%d:%d" % (i, c) for i in range(i0, i0 + 4)], 4 * cn)
-            for i in vrows:
-                V(tt(GE[:, 16 * c0 + i * cn:16 * c0 + (i + 1) * cn], RP[:, 16 * c0 + i:16 * (c0 + cn):16], T.pz[:, c0:c0 + cn], OP.is_ge),
-                  ["pz:z%d" % h] + Rk, ["GE%d:%d" % (i, c)], cn)
-            pv, kv = pvs[h], ("pva", "pvb")[h]
-            seq = vrows + srows
-            for x, i in enumerate(seq):
-                P([mm(pv[:, c0 - h * L:c0 - h * L + cn], T.EALL[:, i * 128:(i + 1) * 128], GE[:, 16 * c0 + i * cn:16 * c0 + (i + 1) * cn], x == 0, x == len(seq) - 1)],
-                  ["EALL", "GE%d:%d" % (i, c)], [kv + ":v"], cn)
-            for x0 in range(c0, c0 + cn, PXN):
-                V(scan(RP[:, 4096 + 16 * x0:4096 + 16 * (x0 + PXN)], T.RESET[:, 0:16 * PXN], RP[:, 16 * x0:16 * (x0 + PXN)], OP.max),
-                  ["R%d" % (x // 16) for x in range(x0, x0 + PXN, 16)] + ["RESET"], ["PX:%d" % x0], 16 * PXN, .5)
-            if c0 + cn == L or c0 + cn == K:
-                V(ts(T.HP[:, h * L:h * L + L], pv[:, 0:L], T.PF[:, 8:9] if sq else T.PF[:, 11:12], OP.is_ge, T.PW[:], OP.mult), [kv + ":v", "PW", "PF8", "PF11"], ["HP%d" % h], L)
-        allR = ["R%d" % x for x in range(16)] + ["PX:%d" % x for x in range(0, K, PXN)]
-        P([mm(T.pva[:, 3 * L:3 * L + 16], T.EALL[:, i * 128:(i + 1) * 128], T.HP[:, i:K:16], i == 0, i == 15) for i in range(16)],
-          ["EALL", "HP0", "HP1"], ["pva:l"], 16 * 64)
-        A(act(T.SF[:, 0:16], T.pva[:, 3 * L:3 * L + 16], AF.Ln, T.PF[:, 10:11]), ["pva:l", "PF10"], ["SF"], 16)
-        P([mm(T.pvb[:, L:L + K], T.BO[:], T.HP[:], True, True)], ["BO", "HP0", "HP1"], ["pvb:s"], K)
-        V(tt(T.ZH[:], ZA, T.pvb[:, L:L + K], OP.min), zz + ["pvb:s"], ["ZH"], K)
-        V(ts(sm(0), T.SF[:, 0:16], -1.0 / math.log(4.0), OP.mult, 19.0, OP.add), ["SF"], ["h"], 16)
-        V(tt(sm(2), sm(0), T.KM[:], OP.add), ["h", "KM"], ["lm"], 16)
-        V(tt(DB[:, 0:16], T.SF[:, 0:16], T.KF[:], OP.add), ["SF", "KF"], ["SFx"], 16)
-        V(ts(LU[:, 0:16], DB[:, 0:16], -1.0 / math.log(4.0), OP.mult, 0.25, OP.add), ["SFx"], ["LU0"], 16)
-        V(ts(sm(1), sm(0), 15.5, OP.is_lt, -4095.0, OP.mult), ["h"], ["e"], 16)
-        V(tt(sm(3), sm(2), sm(1), OP.add), ["lm", "e"], ["ly"], 16)
-        V(cp(LU[:, 16:32], sm(3)), ["ly"], ["LUy"], 16)
-        A(act(T.ME[:], RP[:].indirect(LU[:, 0:16]), AF.Copy), allR + ["LU0"], ["M"], K, G_R, 65.0)
-        A(act(T.YE[:], RP[:].indirect(LU[:, 16:32]), AF.Copy), allR + ["LUy"], ["Y"], K, G_R, 65.0)
-        P([mm(T.pu[:, 0:16], T.BO[:], T.ONES[:, 0:16], True, False)], ["BO", "ONES"], ["pu:u"], 64)
-        P([mm(T.pu[:, 0:16], T.WALL[:, i * 128:(i + 1) * 128], T.ME[:, i:K:16], False, i == 15) for i in range(16)], ["WALL", "M"], ["pu:u"], 16 * 64)
-        P([mm(T.pva[:, 400:416], T.EALL[:, i * 128:(i + 1) * 128], T.YE[:, i:K:16], i == 0, i == 15) for i in range(16)], ["EALL", "Y"], ["pva:y"], 16 * 64)
-        V(cp(sm(4), T.pu[:, 0:16]), ["pu:u"], ["uv"], 16)
-        V(ts(sm(6), sm(4), 4095, OP.bitwise_and), ["uv"], ["uvm"], 16)
-        V(cp(sm(5), T.pva[:, 400:416]), ["pva:y"], ["vy"], 16)
-        u, vv = sm(6), sm(5)
-        V(tt(T.SF[:, 16:32], u, u, OP.mult), ["uvm"], ["yq"], 16)
-        V(ts(sm(9), T.SF[:, 16:32], 1.0 / 32.0, OP.mult, T.AC[:], OP.add), ["yq", "AC"], ["jf"], 16)
-        V(ts(sm(8), u, 16.0, OP.add), ["uvm"], ["u32"], 16)
-        V(ts(sm(11), sm(8), 31, OP.bitwise_and), ["u32"], ["a31"], 16)
-        V(ts(sm(12), sm(9), 255, OP.bitwise_and), ["jf"], ["j"], 16)
-        V(tt(sm(13), sm(11), T.K32[:], OP.add), ["a31", "K32"], ["a"], 16)
-        V(cp(LU[:, 32:64], sm(12, 32)), ["j", "a"], ["LU1"], 32)
-        V(tt(T.MD[:], NB[:].indirect(LU[:, 32:48]), T.DIAG[:, 0:K], OP.mult), [nb, "LU1", "DIAG"], ["MD"], K, G_R)
-        V(ts(T.HD[:], sm(0), 15.5, OP.is_lt), ["h"], ["HD"], 16)
-        V(ts(sm(17), sm(0), 256.0, OP.mult), ["h"], ["h256"], 16)
-        V(tt(sm(18), sm(17), T.KT[:], OP.add), ["h256", "KT"], ["d0"], 16)
-        V(ts(sm(14), vv, 3, OP.bitwise_and), ["vy"], ["v3"], 16)
-        V(tt(sm(16), sm(14), T.HD[:], OP.min), ["v3", "HD"], ["pa"], 16)
-        V(tt(sm(27), sm(0), sm(16), OP.mult), ["h", "pa"], ["cd"], 16)
-        V(scan(T.ML[:], T.RESET[:, 0:K], T.MD[:], OP.add), ["RESET", "MD"], ["ML"], K, .5)
-        V(tt(sm(20), T.ML[:, 15:K:16], sm(16), OP.mult), ["ML", "pa"], ["mc"], 16)
-        V(tt(sm(21), sm(18), sm(20), OP.subtract), ["d0", "mc"], ["d"], 16)
-        V(ts(sm(22), sm(20), 5, OP.arith_shift_right, 0x700, OP.bitwise_and), ["mc"], ["ver"], 16)
-        V(ts(sm(24), sm(21), 4095, OP.bitwise_and), ["d"], ["lr"], 16)
-        V(ts(sm(25), sm(21), 8, OP.arith_shift_right, 31, OP.bitwise_and), ["d"], ["ls"], 16)
-        V(tt(sm(26), sm(22), sm(12), OP.add), ["ver", "j"], ["lp"], 16)
-        V(cp(LU[:, 64:128], sm(24, 64)), ["lr", "ls", "lp", "cd"], ["LU2"], 64)
-        P([mm(T.pz[:, K:2 * K], T.IDM[:], T.YE[:], True, False), mm(T.pz[:, K:2 * K], T.NID[:], T.ZH[:], False, True)], ["IDM", "NID", "Y", "ZH"], ["pz:d"], 2 * K)
-        OZ, oz = T.OZ[:, o0:o0 + K], "OZ%d" % par
-        A(act(OZ, T.pz[:, K:2 * K], AF.Abs), ["pz:d"], [oz], K)
-        for qd in range(8 - NDP):
-            bk = bank()
-            for i in range(2):
-                r = qd * 2 + i
-                ob, lh = T[bk][:, i * K:(i + 1) * K], T.RALL[:, r * 128:(r + 1) * 128]
-                P([mm(ob, lh, T.SH[:, r0:r0 + K], True, False), mm(ob, lh, T.SL[:, r0:r0 + K], False, True)], ["RALL"] + hi + lo, [bk + ":%d" % i], 2 * K)
-            if qd == 0:
-                A(act(T.S8[:], T[bk][:, 0:K], AF.Identity, T.PF[:, 16 + t:17 + t]), [bk + ":0", "PF%d" % (16 + t)], ["S8"], K)
-            A(act(T.WR[:, qd * 512:(qd + 1) * 512], T[bk][:], AF.Copy), [bk + ":0", bk + ":1"], ["WR%d" % qd], 512)
-        if NDP:
-            DS([dma("S", T.ER[:, 0:16, :], T.WR[:, 0:K]), dma("S", T.ER[:, 16:32, :], T.WR[:, 0:K])], ["WR0"], ["ER"], 2300.0)
-            DS([dma("S", T.WR[:, r * K:(r + 1) * K], T.ER[:, r:r + 16, :]) for r in range(16 - 2 * NDP, 16)], ["ER"], ["WR%d" % x for x in range(8 - NDP, 8)], 2000.0 + 500.0 * 2 * NDP)
-        V(tt(T.AB[:], T.T2[:].indirect(LU[:, 80:96]), BB[:], OP.mult), ["T2", bbk, "LU2"], ["AB"], K, G_R)
-        V(tt(T.AD[:], T.PC[:, 0:K * (t + 2)].indirect(LU[:, 96:112]), T.AB[:], OP.max), ["PC%d" % x for x in range(t + 2)] + ["AB", "LU2"], ["AD"], K, G_R)
-        V(tt(T.QQ[:], T.WR[:].indirect(LU[:, 64:80]), T.AD[:], OP.max), ["WR%d" % x for x in range(8)] + ["AD", "LU2"], ["Q"], K, G_R)
-        V(ts(T.SI[:], T.QQ[:], 8191, OP.bitwise_and), ["Q"], ["SI"], K)
-        if last:
-            V(cp(T.YSF[:], T.SI[:]), ["SI"], ["YSF"], K)
-            D("S", dma("S", T.ys[:], T.YSF[:]), ["YSF"], [])
-            D("S", dma("S", T.yz[:], OZ), [oz], [])
-        else:
-            ou = "OU%d" % par
-            V(cp(T.OU[:, o0:o0 + K], T.SI[:]), ["SI"], [ou], K)
-            send([(T.SU[:, r0 + K:r0 + 2 * K], T.OU[:, o0:o0 + K]), (T.SZ[:, r0 + K:r0 + 2 * K], OZ)], t + 1, 0, "a", [ou, oz],
-                 [x % (t + 1) for x in ("SU%d:0", "SU%d:1", "ZZ%d:0", "ZZ%d:1")])
-            oc, nc, px = slice(o0, o0 + K), slice(r0 + K, r0 + 2 * K), T.pva[:, L:L + K]
-            oh, ol = "OH%d" % par, "OL%d" % par
-            V(cp(px, T.SI[:]), ["SI"], ["pva:x"], K)
-            A(act(T.OH[:, oc], px, AF.Copy), ["pva:x"], [oh], K)
-            V(tt(T.OL[:, oc], px, T.OH[:, oc], OP.subtract), ["pva:x", oh], [ol], K)
-            send([(T.SH[:, nc], T.OH[:, oc]), (T.SL[:, nc], T.OL[:, oc])], t + 1, 0, "b", [oh, ol], [x % (t + 1) for x in ("HI%d:0", "HI%d:1", "LO%d:0", "LO%d:1")])
-            V(tt(T.XS[:], T.XT[:].indirect(LU[:, 48:64]), T.ME[:], OP.add), ["XT", "LU1", "M"], ["XS"], K, G_R)
-            V(ts(T.XD[:], T.XS[:], 1, OP.arith_shift_right), ["XS"], ["XD"], K)
-            V(cp(T.XT[:].indirect(LU[:, 48:64]), T.XD[:]), ["XD", "LU1"], ["XT"], K, 4)
-            P([mm(T.pm[:, 0:16], T.ONES[:, 0:128], T.HD[:], True, True)], ["ONES", "HD"], ["pm:a"], 64)
-            A(lambda: s.activation(out=T.ACT[:], in_=T.pm[:, 0:16], func=AF.Copy, accum_out=T.AR[:]), ["pm:a"], ["AR"], 16, 1.0, 140.0)
-            A(lambda: s.activation(out=T.AC[:], in_=T.AR[:], func=AF.Identity, bias=T.PF[:, 12:13], scale=-1.0), ["AR", "PF12"], ["AC"], 1)
-        pk, PD = ("PL", T.PL[:]) if last else ("PC%d" % (t + 2), T.PC[:, K * (t + 2):K * (t + 3)])
-        V(tt(PD, T.T1[:].indirect(LU[:, 112:128]), T.S8[:], OP.mult), ["T1", "S8", "LU2"], [pk], K, G_R)
-        V(tt(CT, CT, PD, OP.max), ["pm:c", pk], ["pm:c"], K)
-        V(tt(NN[:], T.NV[:, 16 * (t + 2):16 * (t + 3)].indirect(LU[:, 112:128]), NB[:], OP.max), ["NV", "LU2", nb], [nn], K, G_R)
-    NF, nf = T["NB%d" % (RO % 2)], "NB%d" % (RO % 2)
-    V(cp(T.FI[:], CT), ["pm:c"], ["FI"], K)
-    V(ts(T.FJ[:], T.FI[:], 8191, OP.bitwise_and), ["FI"], ["FJ"], K)
-    V(cp(T.FC[:], T.FJ[:]), ["FJ"], ["FC"], K)
+                PE([mm(pv[:, L:2 * L], T.BO[:], HP, True, True)], ["BO", k("HP")], [kv + ":s"], L)
+            V(tt(DM, T.KF[:, 0:8], SF, OP.subtract), [k("SF"), "KF"], [k("DM")])
+            V(ts(T.HN[:, c8], SF, T.PF[:, 14:15], OP.is_gt, -HC, OP.mult), [k("SF"), "PF14"], [k("HN")])
+            V(tt(DY, DM, T.HN[:, c8], OP.add), [k("DM"), k("HN")], [k("DY")])
+            m0 = 2 * L * h
+            ME, YE = T.MY[:, m0:m0 + L], T.MY[:, m0 + L:m0 + 2 * L]
+            if P["msp"][h]:
+                V(cp(LU[:, 16 * h:16 * h + 8], DM), [k("DM")], [k("LM")])
+                V(cp(LU[:, 16 * h + 8:16 * h + 16], DY), [k("DY")], [k("LY")])
+                A(act(ME, RP[:, R0:R0 + RW].indirect(LU[:, 16 * h:16 * h + 8]), AF.Copy), allR + [k("LM")], [k("ME")], L, G_R)
+                A(act(YE, RP[:, R0:R0 + RW].indirect(LU[:, 16 * h + 8:16 * h + 16]), AF.Copy), allR + [k("LY")], [k("MY")], L, G_R)
+            else:
+                V(cp(LU[:, 16 * h:16 * h + 16], T.DB[:, 16 * h:16 * h + 16]), [k("DM"), k("DY")], [k("LM"), k("LY")])
+                A(act(T.MY[:, m0:m0 + 2 * L], RP[:, R0:R0 + RW].indirect(LU[:, 16 * h:16 * h + 16]), AF.Copy), allR + [k("LM"), k("LY")], [k("MY"), k("ME")], 2 * L, G_R)
+            A(act(T.HB[:, c8], SF, AF.Identity, T.PF[:, 11:12], -1.0), [k("SF"), "PF11"], [k("HB")])
+            if P["zha"][h]:
+                A(act(T.ZH[:, c], pv[:, L:2 * L], AF.Relu), [kv + ":s"], [k("ZH")], L)
+            else:
+                V(tt(T.ZH[:, c], Z, pv[:, L:2 * L], OP.min), [zz, kv + ":s"], [k("ZH")], L)
+            PE([mm(pu[:, 0:8], toward(T.WB, i), T.MY[:, m0 + i:m0 + L:16], i == 0, i == 15) for i in range(16)], ["WB", k("ME")], [ku + ":u"], 16 * 64)
+            PE([mm(pz[:, 400:408], toward(T.EB, i), T.MY[:, m0 + L + i:m0 + 2 * L:16], i == 0, i == 15) for i in range(16)], ["EB", k("MY")], [kz + ":y"], 16 * 64)
+            V(ts(sm(0), pu[:, 0:8], 16.0, OP.add), [ku + ":u"], [k("u0")])
+            PE([mm(pu[:, 16:24], T.IDM[:], T.KK[:, 0:8], True, False), mm(pu[:, 16:24], T.ID2[:], T.HB[:, c8], False, False)],
+               ["IDM", "KK", "ID2", k("HB")], [ku + ":m"], 128)
+            V(ts(sm(1), sm(0), 4095, OP.bitwise_and), [k("u0")], [k("u1")])
+            V(tt(T.YQ[:, c8], sm(1), sm(1), OP.mult), [k("u1")], [k("yq")])
+            x0, x1 = 160 + 16 * h, 192 + 16 * h
+            V(ts(SM[:, x0:x0 + 8], T.YQ[:, c8], 1.0 / 32.0, OP.mult, T.AC[:], OP.add), [k("yq"), "AC"], [k("jf")])
+            if last:
+                V(ts(SM[:, x1:x1 + 8], SM[:, x0:x0 + 8], 255, OP.bitwise_and), [k("jf")], [k("j")])
+            else:
+                V(ts(SM[:, x0 + 8:x0 + 16], sm(1), 8.0, OP.mult, 128.0, OP.add), [k("u1")], [k("a0")])
+                if P["msp"][h]:
+                    V(ts(SM[:, x1:x1 + 8], SM[:, x0:x0 + 8], 255, OP.bitwise_and), [k("jf")], [k("j")])
+                    V(ts(SM[:, x1 + 8:x1 + 16], SM[:, x0 + 8:x0 + 16], 255, OP.bitwise_and), [k("a0")], [k("a1")])
+                else:
+                    V(ts(SM[:, x1:x1 + 16], SM[:, x0:x0 + 16], 255, OP.bitwise_and), [k("jf"), k("a0")], [k("j"), k("a1")])
+            V(ts(sm(4), pz[:, 400:408], 1024.0, OP.mult, HC + 256.0, OP.add), [kz + ":y"], [k("y0")])
+            V(ts(sm(5), sm(4), 4095, OP.bitwise_and), [k("y0")], [k("y1")])
+            V(tt(T.XX[:, c8], sm(5), T.HN[:, c8], OP.add), [k("y1"), k("HN")], [k("XX")])
+            V(tt(sm(6), SM[:, x1:x1 + 8], T.XX[:, c8], OP.max), [k("j"), k("XX")], [k("jp")])
+            LJ, LR, LA = LU[:, 32 + 8 * h:40 + 8 * h], LU[:, 48 + 8 * h:56 + 8 * h], LU[:, 64 + 8 * h:72 + 8 * h]
+            V(ts(LJ, sm(6), 256.0, OP.min), [k("jp")], [k("LJ")])
+            pk = [pc, "NO%d" % par, k("LJ")]
+            A(act(T.SG[:, c], PC[:, 0:INV].indirect(LJ), AF.Sign, 0.0, T.PF[:, 6:7]), pk + ["PF6"], [k("SG")], L, G_R)
+            V(tt(T.Q1[:, c], PC[:, 0:INV].indirect(LJ), BB[:, c], OP.min), pk + [bbk], [k("QA")], L, G_R)
+            PE([mm(pu[:, 16:24], toward(T.EB, i), T.SG[:, h * L + i:(h + 1) * L:16], False, i == 15) for i in range(16)], ["EB", k("SG")], [ku + ":n", ku + ":m"], 16 * 64)
+            V(ts(LR, pu[:, 16:24], L / 2.0, OP.mult, (5.5 - 128.0) * L + 0.25, OP.add), [ku + ":m"], [k("LR")])
+            if P["zha"][h]:
+                PE([mm(pz[:, L:2 * L], T.NID[:], Z, True, False), mm(pz[:, L:2 * L], T.IDM[:], YE, False, False), mm(pz[:, L:2 * L], T.IDM[:], T.ZH[:, c], False, True)],
+                   ["IDM", "NID", zz, k("MY"), k("ZH")], [kz + ":d"], 3 * L)
+            else:
+                PE([mm(pz[:, L:2 * L], T.IDM[:], YE, True, False), mm(pz[:, L:2 * L], T.NID[:], T.ZH[:, c], False, True)], ["IDM", "NID", k("MY"), k("ZH")], [kz + ":d"], 2 * L)
+            OZ, oz = T.OZ[:, o0:o0 + L], "OZ%d:%d" % (par, h)
+            A(act(OZ, pz[:, L:2 * L], AF.Abs), [kz + ":d"], [oz], L)
+            V(tt(T.Q2[:, c], W[:, 2 * L:32 * L].indirect(LR), T.Q1[:, c], OP.min), [wk, k("QA"), k("LR")], [k("QB")], L, G_R)
+            OF, of = T.OF[:, o0:o0 + L], "OF%d:%d" % (par, h)
+            V(ts(OF, T.Q2[:, c], CM, OP.bitwise_and), [k("QB")], [of], L)
+            if last:
+                V(ts(T.YSF[:, c], OF, -1.0, OP.mult, float(CM), OP.add), [of], [k("YSF")], L)
+                D("S", dma("S", T.ys[:, c], T.YSF[:, c]), [k("YSF")], [])
+                D("S", dma("S", T.yz[:, c], OZ), [oz], [])
+            else:
+                ou = "OU%d:%d" % (par, h)
+                V(ts(T.OU[:, o0:o0 + L], OF, -1.0, OP.mult, float(CM), OP.add), [of], [ou], L)
+                send([(T.SU[:, r0 + K:r0 + K + L], T.OU[:, o0:o0 + L]), (T.SZ[:, r0 + K:r0 + K + L], OZ)], t + 1, h, "a", [ou, oz],
+                     ["SU%d:%d" % (t + 1, h), "ZZ%d:%d" % (t + 1, h)])
+                send([(T.ED[(t + 1) * NH + h], OF)], t + 1, h, "b", [of], ["ED%d:%d" % (t + 1, h)])
+                V(tt(sm(9), SM[:, x1 + 8:x1 + 16], T.K32[:, c8], OP.add), [k("a1"), "K32"], [k("a2")])
+                V(ts(LA, sm(9), 0.125, OP.mult), [k("a2")], [k("LA")])
+                if P["xsa"][h]:
+                    A(act(T.XG[:, c], T.XT[:].indirect(LA), AF.Copy), ["XT", k("LA")], [k("XG")], L, G_R)
+                    PE([mm(T.pm[:, c], T.IDM[:], ME, True, False), mm(T.pm[:, c], T.IDM[:], T.XG[:, c], False, True)], ["IDM", k("ME"), k("XG")], [k("pm:x")], 2 * L)
+                    V(ts(T.XD[:, c], T.pm[:, c], 0.5, OP.mult, -0.25, OP.add), [k("pm:x")], [k("XD")], L)
+                else:
+                    V(tt(T.XS[:, c], T.XT[:].indirect(LA), ME, OP.add), ["XT", k("LA"), k("ME")], [k("XS")], L, G_R)
+                    V(ts(T.XD[:, c], T.XS[:, c], 1, OP.arith_shift_right), [k("XS")], [k("XD")], L)
+                V(cp(T.XT[:].indirect(LA), T.XD[:, c]), [k("XD"), k("LA")], [k("XW"), "XT"], L, 3.8)
+            PD, pd, pt = PC[:, INV + h * L:INV + (h + 1) * L], "PD%d:%d" % (par, h), pv[:, 2 * L:3 * L]
+            A(act(T.AB[:, c], PC[:, c], AF.Abs), [pc], [k("AB")], L)
+            PE([mm(pt, T.DN[:], T.RESET[:, 1024:1024 + L], True, False), mm(pt, T.TRI[:], HP, False, True)], ["DN", "RESET", "TRI", k("HP")], [kv + ":t"], 2 * L)
+            V(tt(pt, pt, W[:, 15 * L:16 * L], OP.add), [kv + ":t", wk], [k("PT"), kv + ":t"], L)
+            V(tt(PD, pt, T.AB[:, c], OP.min), [kv + ":t", k("AB")], [pd], L)
+        V(ts(T.PA[:, 0:16], T.XX[:], 0.0, OP.is_lt, float(INV), OP.mult), ["XX0", "XX1"], ["PA"])
+        V(tt(T.PA[:, 16:32], T.PA[:, 0:16], T.KT[:], OP.add), ["PA", "KT"], ["PB"])
+        V(cp(LU[:, 80:96], T.PA[:, 16:32]), ["PB"], ["LG"])
+        A(act(PN[:, 0:K], PC[:].indirect(LU[:, 80:96]), AF.Copy), [pc, "NO%d" % par, "PD%d:0" % par, "PD%d:1" % par, "LG"], [pn], K, G_R)
+        if not last:
+            PE([mm(T.px[:, 2 * L:2 * L + 16], T.ONF[:], T.HN[:], True, True)], ["ONF", "HN0", "HN1"], ["px:a"], 256)
+            A(lambda: s.activation(out=T.ACT[:], in_=T.px[:, 2 * L:2 * L + 16], func=AF.Copy, accum_out=T.AR[:]), ["px:a"], ["AR"], 16, 1.0, 140.0)
+            A(act(T.AC[:], T.AR[:], AF.Identity, T.PF[:, 12:13], 1.0 / HC), ["AR", "PF12"], ["AC"])
+    A(act(T.AB[:], T["PC%d" % (RO % 2)][:, 0:K], AF.Abs), ["PC%d" % (RO % 2)], ["AB0", "AB1"], K)
+    V(ts(T.FC[:], T.AB[:], CM - PV, OP.add), ["AB0", "AB1"], ["FC"], K)
     D("S", dma("S", T.yc[:], T.FC[:]), ["FC"], [])
-    V(cp(T.FN[:], NF[:]), [nf], ["FN"], K)
-    V(ts(T.FM[:], T.FN[:], 8, OP.arith_shift_right, 31, OP.bitwise_and), ["FN"], ["FM"], K)
-    V(ts(T.FL[:], T.FM[:], 1.0, OP.add), ["FM"], ["FL"], K)
+    A(act(T.SN[:], T["PC%d" % (RO % 2)][:, 0:K], AF.Sign), ["PC%d" % (RO % 2)], ["SN"], K)
+    PE([mm(T.px[:, K:2 * K], T.BO[:], T.SN[:], True, True)], ["BO", "SN"], ["px:n"], K)
+    V(ts(T.FL[:], T.px[:, K:2 * K], -0.5, OP.mult, 8.0, OP.add), ["px:n"], ["FL"], K)
     D("S", dma("S", T.yn[:], T.FL[0:128:16, :]), ["FL"], [])
 
     lastw, readers, lastb = {}, {}, {}
@@ -451,9 +475,8 @@ def rank_program(g, core, T, topo):
                 dep(i, lastw[r], True)
             readers.setdefault(r, []).append(i)
         for w in op["w"]:
-            acc = op["q"] == "T" and w.startswith("pv")
             if w in lastw:
-                dep(i, lastw[w], not (acc and ops[lastw[w]]["q"] == "T"))
+                dep(i, lastw[w], not (op["q"] == "T" and ops[lastw[w]]["q"] == "T") and not w.startswith("o"))
             for j in readers.get(w, []):
                 dep(i, j, True)
             lastw[w] = i
@@ -464,7 +487,7 @@ def rank_program(g, core, T, topo):
             lastb[b] = i
 
     if "order" not in ORDER:
-        ORDER["order"] = make_order(ops, deps)[0]
+        ORDER["order"] = make_order(ops, deps)
     order = ORDER["order"]
 
     CN = {"V": "cV", "A": "cA", "T": "cT", "G": "cG"}

@@ -13,12 +13,13 @@ HC = float(DP - 1)
 INV = 272
 TAG = 16384.0
 P = {
-    "pieces": [[(0, 32, "A"), (32, 32, "V"), (64, 32, "A"), (96, 32, "A")], [(0, 32, "A"), (32, 32, "A"), (64, 32, "A"), (96, 32, "A")]],
+    "pieces": [[(0, 32, "A"), (32, 32, "V"), (64, 32, "A"), (96, 32, "A")], [(0, 32, "A"), (32, 32, "A"), (64, 32, "A"), (96, 32, "V")]],
+    "ends": [[(0, 32, "A"), (32, 32, "V"), (64, 32, "A"), (96, 32, "A")], [(0, 32, "A"), (32, 32, "A"), (64, 32, "A"), (96, 32, "V")]], "endt": [5],
     "chunks": [[(0, 64), (64, 64)], [(0, 64), (64, 64)]],
     "pxn": 32,
-    "passes": 6, "lead": 0.0,
-    "gr": 1.55, "pe": 0.5, "wlat": 6000.0, "slat": 2500.0,
-    "zha": [1, 1], "pda": [0, 0], "xsa": [1, 0], "msp": [0, 1], "blat": 12000.0, "sq": 5, "sqc": [(1, 1)],
+    "passes": 500, "seed": 4, "zsep": 0,
+    "cyc": 0.93, "hop": 110.0, "gr": 1.55, "pe": 0.55, "wlat": 6000.0, "slat": 3000.0, "pb": 8,
+    "zha": [1, 1], "xsa": [1, 1], "msp": [1, 1], "blat": 12000.0, "sq": 5, "sqc": [(1, 1)],
     "adp": [2, 2],
     "bonus": {"CT": -20000.0, "TG": -20000.0},
 }
@@ -26,7 +27,7 @@ P = {
 SCRATCH = {
     "XT": ("sbuf", [128, 8192], "bfloat16"), "RP": ("sbuf", [128, NH * RW], "bfloat16"), "GE": ("sbuf", [128, 16 * K], "bfloat16"),
     "W0": ("sbuf", [128, 32 * L], "int32"), "W1": ("sbuf", [128, 32 * L], "int32"), "ED": ("dram", [RO * NH, 128, L], "int32"),
-    "PC0": ("sbuf", [128, INV + K], "float32"), "PC1": ("sbuf", [128, INV + K], "float32"),
+    "PC0": ("sbuf", [128, 3 * K + 16], "float32"), "PC1": ("sbuf", [128, 3 * K + 16], "float32"),
     "EB": ("sbuf", [128, 144], "bfloat16"), "WB": ("sbuf", [128, 144], "float16"), "RESET": ("sbuf", [128, 1152], "bfloat16"),
     "EH": ("sbuf", [128, 144], "bfloat16"), "D8": ("sbuf", [128, 128], "bfloat16"),
     "BO": ("sbuf", [128, 128], "bfloat16"), "TRI": ("sbuf", [128, 128], "bfloat16"), "IDM": ("sbuf", [128, 128], "bfloat16"),
@@ -44,14 +45,14 @@ SCRATCH = {
     "HP": ("sbuf", [128, K], "bfloat16"), "ZH": ("sbuf", [128, K], "bfloat16"), "MY": ("sbuf", [128, 2 * K], "bfloat16"),
     "SF": ("sbuf", [128, 16], "float32"), "DB": ("sbuf", [128, 32], "float32"), "HN": ("sbuf", [128, 16], "float32"),
     "HB": ("sbuf", [128, 16], "bfloat16"), "YQ": ("sbuf", [128, 16], "float32"), "XX": ("sbuf", [128, 16], "float32"),
-    "PA": ("sbuf", [128, 32], "float32"), "SM": ("sbuf", [128, 256], "int32"), "LU": ("sbuf", [128, 128], "uint16"),
+    "PA": ("sbuf", [128, 16], "bfloat16"), "AQ": ("sbuf", [128, 1], "bfloat16"), "SM": ("sbuf", [128, 256], "int32"), "LU": ("sbuf", [128, 128], "uint16"),
     "XS": ("sbuf", [128, K], "int32"), "XD": ("sbuf", [128, K], "int32"), "AB": ("sbuf", [128, K], "float32"),
     "SG": ("sbuf", [128, K], "bfloat16"), "Q1": ("sbuf", [128, K], "float32"), "Q2": ("sbuf", [128, K], "int32"),
     "FC": ("sbuf", [128, K], "float32"), "FL": ("sbuf", [128, K], "float32"), "YSF": ("sbuf", [128, K], "float32"),
     "NBO": ("sbuf", [128, 128], "bfloat16"), "DN": ("sbuf", [128, 128], "bfloat16"), "XG": ("sbuf", [128, K], "bfloat16"),
     "SN": ("sbuf", [128, K], "bfloat16"),
-    "SU": ("sbuf", [128, RO * K], "uint16"), "SZ": ("sbuf", [128, RO * K], "bfloat16"),
-    "OU": ("sbuf", [128, 2 * K], "uint16"), "OZ": ("sbuf", [128, 2 * K], "bfloat16"), "OF": ("sbuf", [128, 2 * K], "int32"),
+    "SU": ("sbuf", [128, RO * K], "uint16"), "SZ": ("sbuf", [128, 2 * RO * K], "bfloat16"),
+    "OU": ("sbuf", [128, 2 * K], "uint16"), "OZ": ("sbuf", [128, 4 * K], "bfloat16"), "OF": ("sbuf", [128, 2 * K], "int32"),
 }
 for _n in ("pz0", "pz1", "pv0", "pv1", "pu0", "pu1", "pm", "px"):
     SCRATCH[_n] = ("psum", [128, 512], "float32")
@@ -62,7 +63,19 @@ SEMAPHORES = ["cV", "cA", "cT", "cG", "loc"] + ["lo%d" % i for i in range(20)] +
              ["ar%d%d%s" % (t, c, s) for t in range(1, RO) for c in range(NH) for s in "ab"]
 
 ORDER = {}
-CYC = 0.83 * 1.2
+
+
+CASES = [
+    (1.04, 1.55, 3.8, 0.52, 60.0, 2500.0, 1.0), (0.91, 1.55, 3.8, 0.46, 130.0, 2500.0, 1.0), (0.91, 1.55, 3.8, 0.46, 60.0, 4000.0, 1.0),
+    (0.91, 1.55, 3.8, 0.75, 60.0, 2500.0, 1.0), (1.2, 2.0, 5.5, 0.61, 100.0, 2500.0, 1.1)]
+
+
+def step_name(reads, writes):
+    w = writes[0] if writes else reads[0]
+    if w[:2] in ("OZ", "OF", "OU", "PD", "SU", "ED", "PC"):
+        return w[:2] + w[3:]
+    ge = [x.split(":") for x in [w] + list(reads) if x.startswith("GE")]
+    return w[:3] + ge[0][2] + str(int(ge[0][1]) // 6) if ge else w
 
 
 def place(ops, pred, key):
@@ -99,7 +112,7 @@ def place(ops, pred, key):
 
 def make_order(ops, deps):
     n = len(ops)
-    fwd = [[(j, ops[j]["lat"] if (w or ops[j]["q"] != ops[i]["q"]) else 0.0) for j, w in deps[i].items()] for i in range(n)]
+    fwd = [[(j, ops[j]["lat"] if w else 0.0) for j, w in deps[i].items()] for i in range(n)]
     bwd = [[] for _ in range(n)]
     for i in range(n):
         for j, lat in fwd[i]:
@@ -107,14 +120,45 @@ def make_order(ops, deps):
     tail = [0.0] * n
     for i in range(n - 1, -1, -1):
         tail[i] = ops[i]["cost"] + max([lat + tail[x] for x, lat in bwd[i]] + [ops[i]["lat"]])
-    key, best = [-tail[i] - ops[i]["bonus"] for i in range(n)], None
-    for _ in range(P["passes"]):
+    cost = [op["cost"] for op in ops]
+    cases = []
+    for cyc, gather, scatter, pe, hop, write, weight in CASES:
+        by = {P["gr"]: 0.2 + 0.8 * gather / P["gr"], 3.8: 0.1 + 0.9 * scatter / 3.8}
+        cs = [op["cost"] * (cyc / P["cyc"] * by.get(op["rate"], 1.0) if op["rate"] else pe / P["pe"] if op["q"] == "T" else 1.0) for op in ops]
+        ed = [[(x, hop if lat == P["hop"] else lat + (write - P["slat"] if ops[i]["kind"] == "r" and lat else 0.0)) for x, lat in bwd[i]] for i in range(n)]
+        cases.append((cs, ed, weight))
+
+    def length(st):
+        seq, total = sorted(range(n), key=lambda i: (st[i], i)), 0.0
+        for cs, ed, weight in cases:
+            est, free = [0.0] * n, {}
+            for i in seq:
+                e = max(est[i], free.get(ops[i]["q"], 0.0)) + cs[i]
+                free[ops[i]["q"]] = e
+                for x, lat in ed[i]:
+                    if est[x] < e + lat:
+                        est[x] = e + lat
+                est[i] = e + ops[i]["lat"]
+            total += weight * max(est)
+        return total
+
+    kinds = sorted(set(op["name"] for op in ops))
+    state = [P["seed"]]
+
+    def draw():
+        state[0] = (state[0] * 6364136223846793005 + 1442695040888963407) % 2 ** 64
+        return (state[0] >> 11) / 2.0 ** 53
+
+    best, key = None, [-x for x in tail]
+    for it in range(P["passes"]):
         st = place(ops, fwd, key)
-        end = max(st[i] + ops[i]["cost"] + ops[i]["lat"] for i in range(n))
-        if best is None or end < best[0]:
-            best = (end, st)
-        back = place(ops, bwd, [-(st[i] + ops[i]["cost"]) for i in range(n)])
-        key = [-(back[i] + ops[i]["cost"]) for i in range(n)]
+        back = place(ops, bwd, [-(st[i] + cost[i]) for i in range(n)])
+        for x in (st, place(ops, fwd, [-(back[i] + cost[i]) for i in range(n)])):
+            e = length(x)
+            if best is None or e <= best[0]:
+                best = (e, x)
+        shift = {kinds[int(draw() * len(kinds))]: 3000.0 * (draw() + draw() + draw() - 1.5) for _ in range((0, 1, 2, 3, 6)[min(it, 1 + int(4 * draw()))])}
+        key = [best[1][i] + shift.get(ops[i]["name"], 0.0) for i in range(n)]
     ORDER["plan"], ORDER["ops"] = best, ops
     return sorted(range(n), key=lambda i: (best[1][i], i))
 
@@ -129,22 +173,29 @@ def rank_program(g, core, T, topo):
     G_R = P["gr"]
     now = [0.0, -1]
 
-    def add(q, fns, reads, writes, cost, lat=60.0, kind="c", sem=None, amount=0):
+    CYC = P["cyc"]
+
+    def add(q, fns, reads, writes, cost, lat=P["hop"], kind="c", sem=None, amount=0):
         banks = sorted(set(k.split(":")[0] for k in list(reads) + list(writes) if k.startswith("p")))
         ops.append({"q": q, "fns": fns if isinstance(fns, list) else [fns], "r": list(reads), "w": list(writes), "cost": cost,
-                    "lat": lat, "kind": kind, "sem": sem, "amount": amount, "banks": banks, "bonus": now[0], "t": now[1]})
+                    "lat": lat, "kind": kind, "sem": sem, "amount": amount, "banks": banks, "rate": None, "t": now[1],
+                    "name": q + step_name(reads, writes)})
 
     def vc(n, rate=1.0):
         return max(64.0, n * rate) * CYC
 
     def V(fn, reads, writes, n=16, rate=1.0):
         add("V", fn, reads, writes, vc(n, rate) + (60.0 if rate in (G_R, 3.8) else 0.0))
+        ops[-1]["rate"] = rate
 
     def A(fn, reads, writes, n=16, rate=1.0, extra=0.0):
         add("A", fn, reads, writes, vc(n, rate) + extra + (75.0 if rate == G_R else 0.0))
+        ops[-1]["rate"] = rate
 
     def PE(fns, reads, writes, cyc):
-        add("T", fns, reads, writes, cyc * P["pe"])
+        pb = P["pb"]
+        for x in range(0, len(fns), pb):
+            add("T", fns[x:x + pb], reads, writes, cyc * P["pe"] * len(fns[x:x + pb]) / len(fns))
 
     def G(fn, reads, writes, n):
         add("G", fn, reads, writes, 150 + 2 * n * CYC)
@@ -190,7 +241,7 @@ def rank_program(g, core, T, topo):
         return lambda: eng[q].dma_start(out=o, in_=a)
 
     D("A", dma("A", T.STI[:], T.stk[:]), [], ["STI"])
-    D("A", dma("A", T.SZ[:, 0:K], T.z[:]), [], ["ZZ0:0", "ZZ0:1"])
+    D("A", [dma("A", T.SZ[:, h * K:h * K + L], T.z[:, h * L:(h + 1) * L]) for h in range(NH)], [], ["ZZ0:0", "ZZ0:1"])
     D("S", dma("S", T.XT[:], T.xt[:]), [], ["XT", "XL"], 9000.0)
     D("S", dma("S", T.WI[:, 0:1], T.w[:]), [], ["WI"], 9000.0)
     D("S", dma("S", T.BAI[:], T.bas[:]), [], ["BAI"], 9000.0)
@@ -199,7 +250,8 @@ def rank_program(g, core, T, topo):
 
     V(ms(T.PF[:, 10:11], math.exp(5.0)), [], ["PF10"])
     V(ms(T.PF[:, 11:12], 149.23), [], ["PF11"])
-    V(ms(T.PF[:, 12:13], 2040.0 - 0.4375), [], ["PF12"])
+    V(ms(T.PF[:, 12:13], 2040.25 + 129 * K), [], ["PF12"])
+    V(ms(T.PF[:, 15:16], -0.499), [], ["PF15"])
     G(io(T.PI[:, 0:1], [[0, 1]], 1, False), [], ["PI0"], 1)
     V(ts(T.PI[:, 1:2], T.PI[:, 0:1], 15, OP.bitwise_and), ["PI0"], ["PI1"])
     V(ts(T.PI[:, 2:3], T.PI[:, 0:1], 112, OP.bitwise_and), ["PI0"], ["PI2"])
@@ -240,13 +292,13 @@ def rank_program(g, core, T, topo):
     V(ms(T.ONF[:], 1.0), [], ["ONF"], 128)
     V(ts(T.KT[:], T.K0[:], pmf, OP.add), ["K0", "PF0"], ["KT"])
     V(ts(T.KF[:, 0:8], T.KT[:, 0:8], 16.0, OP.mult, DP + 20.47, OP.add), ["KT"], ["KF"])
-    V(ts(T.K32[:], T.KT[:], 256.0, OP.mult), ["KT"], ["K32"])
+    V(ts(T.K32[:], T.KT[:], 32.0, OP.mult), ["KT"], ["K32"])
     if any(P["zha"]):
         V(ts(T.NBO[:], T.BO[:], -1.0, OP.mult), ["BO"], ["NBO"], 128, .5)
     V(ts(T.DN[:], T.IDM[:], -PV, OP.mult), ["IDM"], ["DN"], 128, .5)
     A(act(T.PF[:, 13:14], T.PF[:, 10:11], AF.Ln), ["PF10"], ["PF13"], 1, 1.0, 1500.0)
     V(ts(T.PF[:, 14:15], T.PF[:, 13:14], 0.5, OP.add), ["PF13"], ["PF14"])
-    V(ts(T.KK[:, 0:8], T.KT[:, 0:8], 2.0 / L, OP.mult), ["KT"], ["KK"])
+    V(ts(T.KK[:], T.KT[:], 2.0 / L, OP.mult), ["KT"], ["KK"])
     V(ms(T.F4[:], math.e), [], ["F4"])
     V(ms(T.Z0[:], 0.0), [], ["Z0"])
     V(scan(T.PWS[:], T.F4[:], T.Z0[:], OP.add, math.exp(5.0)), ["F4", "Z0"], ["PWS"])
@@ -256,7 +308,9 @@ def rank_program(g, core, T, topo):
     V(lambda: v.tensor_reduce(out=T.PW[:], in_=T.PWM[:], axis=AxisListType.X, op=OP.add), ["PWM"], ["PW"])
     V(cp(T.WF[:, 0:1], T.WI[:, 0:1]), ["WI"], ["WF"])
     V(ts(T.WB[:], T.EB[:], T.WF[:, 0:1], OP.mult), ["EB", "WF"], ["WB"], 144, .5)
-    V(ms(T.AC[:], -8.4375), [], ["AC"])
+    V(ms(T.AC[:], K - 8.0), [], ["AC"])
+    for x in range(2 * NH * P["zsep"]):
+        V(ms(T.OZ[:, x * K + L:(x + 1) * K], 0.0), [], ["OZ"], L, .5)
     for x in range(2, 31, 4):
         y = min(x + 4, 31)
         V(ms(T.W0[:, x * L:y * L], int(PV)), [], ["WM0:%d" % x], (y - x) * L)
@@ -276,15 +330,16 @@ def rank_program(g, core, T, topo):
     n_eng = len(topo.engines(core, T.cores[(rank + 1) % n_ranks]))
     for d in (1, 2, 3):
         dst = T.cores[(rank + d) % n_ranks]
-        add("G", remote([(T["BB%d" % d][:], T.BB0[:])], dst, "bs%d" % d, "loc"), ["BB0"], ["BB%d" % d], 1000.0, P["blat"], "r", "bs%d" % d, n_eng)
+        add("G", remote([(T["BB%d" % d][:], T.BB0[:])], dst, "bs%d" % d, "loc"), ["BB0"], ["BB%d" % d, "oB"], 1000.0, P["blat"], "r", "bs%d" % d, n_eng)
     V(cp(T.LNB[0:8, :], T.LNI[0:8, :]), ["LNI"], ["LNB"], K)
     V(ts(T.SEL[0:8, :], T.IO2[0:8, :], T.PF[0:8, 5:6], OP.is_equal), ["IO2", "PF5"], ["SEL"], 128)
     PE([mm(T.pm[:, 0:K], T.SEL[0:8, :], T.LNB[0:8, :], True, True)], ["SEL", "LNB"], ["pm:0"], K)
     V(ts(T.pm[:, 0:K], T.pm[:, 0:K], pmf, OP.is_le, 0.5, OP.subtract), ["pm:0", "PF0"], ["pm:0"], K)
     V(ts(T.PL[:], T.COI[:], 2.0, OP.mult, 2.0 * (PV - CM), OP.add), ["COI"], ["PL"], K)
-    V(tt(T.PC0[:, 0:K], T.pm[:, 0:K], T.PL[:], OP.mult), ["PL", "pm:0"], ["PC0"], K)
+    V(tt(T.PC0[:, K:2 * K], T.pm[:, 0:K], T.PL[:], OP.mult), ["PL", "pm:0"], ["PC0"], K)
+    A(act(T.PC0[:, 2 * K:3 * K], T.PC0[:, K:2 * K], AF.Copy), ["PC0"], ["PC0b"], K)
     for x in range(2):
-        V(ms(T["PC%d" % x][:, K:INV], PV), [], ["NO%d" % x])
+        V(ms(T["PC%d" % x][:, 3 * K:], PV), [], ["NO%d" % x])
 
     nloc = [0]
     nxt = T.cores[(rank + 1) % n_ranks]
@@ -304,7 +359,7 @@ def rank_program(g, core, T, topo):
         PC, PN, pc, pn = T["PC%d" % par], T["PC%d" % (1 - par)], "PC%d" % par, "PC%d" % (1 - par)
         BB, bbk = T["BB%d" % (t % 4)], "BB%d" % (t % 4)
         for h in range(NH):
-            for p0, n, pq in P["pieces"][h]:
+            for p0, n, pq in P["ends" if t in P["endt"] else "pieces"][h]:
                 a, o = t * K + h * L + p0, RP[:, h * RW + 16 * p0:h * RW + 16 * (p0 + n)]
                 rd, rk = ["XT", "SU%d:%d" % (t, h)], ["R%d:%d" % (h, x // 16) for x in range(p0, p0 + n, 16)]
                 if pq == "A":
@@ -314,8 +369,7 @@ def rank_program(g, core, T, topo):
         for h in range(NH):
             r0, o0, c = t * K + h * L, par * K + h * L, slice(h * L, (h + 1) * L)
             c8 = slice(8 * h, 8 * h + 8)
-            now[0] = P["lead"] * (1 - h)
-            zz, Z = "ZZ%d:%d" % (t, h), T.SZ[:, r0:r0 + L]
+            zz, Z = "ZZ%d:%d" % (t, h), T.SZ[:, 2 * r0:2 * r0 + L]
             pz, pv, pu, kz, kv, ku = T["pz%d" % h], T["pv%d" % h], T["pu%d" % h], "pz%d" % h, "pv%d" % h, "pu%d" % h
             W, wk = T["W%d" % h], "W%d" % h
             R0 = h * RW
@@ -338,7 +392,7 @@ def rank_program(g, core, T, topo):
                     fns = []
                     for x in range(sq):
                         ob = pu[:, x * cn:(x + 1) * cn]
-                        fns += [mm(ob, T.NID[:], T.SZ[:, r0 + c0:r0 + c0 + cn], True, False), mm(ob, T.IDM[:], RP[:, R0 + 16 * c0 + 16 - sq + x:R0 + 16 * (c0 + cn):16], False, True)]
+                        fns += [mm(ob, T.NID[:], T.SZ[:, 2 * r0 + c0:2 * r0 + c0 + cn], True, False), mm(ob, T.IDM[:], RP[:, R0 + 16 * c0 + 16 - sq + x:R0 + 16 * (c0 + cn):16], False, True)]
                     PE(fns, ["IDM", "NID", zz] + Rk, [ku + ":g"], 2 * sq * cn)
                     A(act(GE[:, g0 + (16 - sq) * cn:g0 + 16 * cn], pu[:, 0:sq * cn], AF.Sign, T.PF[:, 9:10]), [ku + ":g", "PF9"],
                       ["GE%d:%d:%d" % (h, i, ci) for i in range(16 - sq, 16)], sq * cn)
@@ -357,7 +411,7 @@ def rank_program(g, core, T, topo):
             V(ts(HP, pv[:, 0:L], 8.5, OP.is_ge, T.PW[:], OP.mult), [kv + ":v", "PW"], [k("HP")], L)
             PE([mm(pv[:, 3 * L:3 * L + 8], toward(T.EB, i), T.HP[:, h * L + i:(h + 1) * L:16], i == 0, i == 15) for i in range(16)], ["EB", k("HP")], [kv + ":l"], 16 * 64)
             SF, DM, DY = T.SF[:, c8], T.DB[:, 16 * h:16 * h + 8], T.DB[:, 16 * h + 8:16 * h + 16]
-            A(act(SF, pv[:, 3 * L:3 * L + 8], AF.Ln, T.PF[:, 10:11]), [kv + ":l", "PF10"], [k("SF")])
+            A(act(SF, pv[:, 3 * L:3 * L + 8], AF.Ln, T.PF[:, 10:11]), [kv + ":l", "PF10"], [k("SF")] + (["oB"] if t == 0 and h == 1 else []))
             if P["zha"][h]:
                 PE([mm(pv[:, L:2 * L], T.IDM[:], Z, True, False), mm(pv[:, L:2 * L], T.NBO[:], HP, False, True)], ["IDM", "NBO", zz, k("HP")], [kv + ":s"], 2 * L)
             else:
@@ -383,30 +437,23 @@ def rank_program(g, core, T, topo):
             PE([mm(pu[:, 0:8], toward(T.WB, i), T.MY[:, m0 + i:m0 + L:16], i == 0, i == 15) for i in range(16)], ["WB", k("ME")], [ku + ":u"], 16 * 64)
             PE([mm(pz[:, 400:408], toward(T.EB, i), T.MY[:, m0 + L + i:m0 + 2 * L:16], i == 0, i == 15) for i in range(16)], ["EB", k("MY")], [kz + ":y"], 16 * 64)
             V(ts(sm(0), pu[:, 0:8], 16.0, OP.add), [ku + ":u"], [k("u0")])
+            if not last:
+                V(cp(sm(7), pu[:, 0:8]), [ku + ":u"], [k("a0")])
+                V(ts(sm(8), sm(7), 31, OP.bitwise_and), [k("a0")], [k("a1")])
             PE([mm(pu[:, 16:24], T.IDM[:], T.KK[:, 0:8], True, False), mm(pu[:, 16:24], T.ID2[:], T.HB[:, c8], False, False)],
                ["IDM", "KK", "ID2", k("HB")], [ku + ":m"], 128)
             V(ts(sm(1), sm(0), 4095, OP.bitwise_and), [k("u0")], [k("u1")])
-            V(tt(T.YQ[:, c8], sm(1), sm(1), OP.mult), [k("u1")], [k("yq")])
-            x0, x1 = 160 + 16 * h, 192 + 16 * h
-            V(ts(SM[:, x0:x0 + 8], T.YQ[:, c8], 1.0 / 32.0, OP.mult, T.AC[:], OP.add), [k("yq"), "AC"], [k("jf")])
-            if last:
-                V(ts(SM[:, x1:x1 + 8], SM[:, x0:x0 + 8], 255, OP.bitwise_and), [k("jf")], [k("j")])
-            else:
-                V(ts(SM[:, x0 + 8:x0 + 16], sm(1), 8.0, OP.mult, 128.0, OP.add), [k("u1")], [k("a0")])
-                if P["msp"][h]:
-                    V(ts(SM[:, x1:x1 + 8], SM[:, x0:x0 + 8], 255, OP.bitwise_and), [k("jf")], [k("j")])
-                    V(ts(SM[:, x1 + 8:x1 + 16], SM[:, x0 + 8:x0 + 16], 255, OP.bitwise_and), [k("a0")], [k("a1")])
-                else:
-                    V(ts(SM[:, x1:x1 + 16], SM[:, x0:x0 + 16], 255, OP.bitwise_and), [k("jf"), k("a0")], [k("j"), k("a1")])
-            V(ts(sm(4), pz[:, 400:408], 1024.0, OP.mult, HC + 256.0, OP.add), [kz + ":y"], [k("y0")])
+            V(tt(sm(2), sm(1), sm(1), OP.mult), [k("u1")], [k("yq")])
+            V(ts(sm(3), sm(2), 5, OP.arith_shift_right, 255, OP.bitwise_and), [k("yq")], [k("j")])
+            V(ts(sm(4), pz[:, 400:408], 1024.0, OP.mult, HC + 2 * K, OP.add), [kz + ":y"], [k("y0")])
             V(ts(sm(5), sm(4), 4095, OP.bitwise_and), [k("y0")], [k("y1")])
             V(tt(T.XX[:, c8], sm(5), T.HN[:, c8], OP.add), [k("y1"), k("HN")], [k("XX")])
-            V(tt(sm(6), SM[:, x1:x1 + 8], T.XX[:, c8], OP.max), [k("j"), k("XX")], [k("jp")])
+            V(tt(sm(6), sm(3), T.XX[:, c8], OP.max), [k("j"), k("XX")], [k("jp")])
             LJ, LR, LA = LU[:, 32 + 8 * h:40 + 8 * h], LU[:, 48 + 8 * h:56 + 8 * h], LU[:, 64 + 8 * h:72 + 8 * h]
-            V(ts(LJ, sm(6), 256.0, OP.min), [k("jp")], [k("LJ")])
-            pk = [pc, "NO%d" % par, k("LJ")]
-            A(act(T.SG[:, c], PC[:, 0:INV].indirect(LJ), AF.Sign, 0.0, T.PF[:, 6:7]), pk + ["PF6"], [k("SG")], L, G_R)
-            V(tt(T.Q1[:, c], PC[:, 0:INV].indirect(LJ), BB[:, c], OP.min), pk + [bbk], [k("QA")], L, G_R)
+            V(ts(LJ, sm(6), T.AC[:], OP.add, 2.0 * K, OP.min), [k("jp"), "AC"], [k("LJ")])
+            pk = [pc, pc + "b", "NO%d" % par, k("LJ")]
+            A(act(T.SG[:, c], PC[:, K:].indirect(LJ), AF.Sign, 0.0, T.PF[:, 6:7]), pk + ["PF6"], [k("SG")], L, G_R)
+            V(tt(T.Q1[:, c], PC[:, K:].indirect(LJ), BB[:, c], OP.min), pk + [bbk], [k("QA")], L, G_R)
             PE([mm(pu[:, 16:24], toward(T.EB, i), T.SG[:, h * L + i:(h + 1) * L:16], False, i == 15) for i in range(16)], ["EB", k("SG")], [ku + ":n", ku + ":m"], 16 * 64)
             V(ts(LR, pu[:, 16:24], L / 2.0, OP.mult, (5.5 - 128.0) * L + 0.25, OP.add), [ku + ":m"], [k("LR")])
             if P["zha"][h]:
@@ -414,7 +461,7 @@ def rank_program(g, core, T, topo):
                    ["IDM", "NID", zz, k("MY"), k("ZH")], [kz + ":d"], 3 * L)
             else:
                 PE([mm(pz[:, L:2 * L], T.IDM[:], YE, True, False), mm(pz[:, L:2 * L], T.NID[:], T.ZH[:, c], False, True)], ["IDM", "NID", k("MY"), k("ZH")], [kz + ":d"], 2 * L)
-            OZ, oz = T.OZ[:, o0:o0 + L], "OZ%d:%d" % (par, h)
+            OZ, oz = T.OZ[:, 2 * o0:2 * o0 + L], "OZ%d:%d" % (par, h)
             A(act(OZ, pz[:, L:2 * L], AF.Abs), [kz + ":d"], [oz], L)
             V(tt(T.Q2[:, c], W[:, 2 * L:32 * L].indirect(LR), T.Q1[:, c], OP.min), [wk, k("QA"), k("LR")], [k("QB")], L, G_R)
             OF, of = T.OF[:, o0:o0 + L], "OF%d:%d" % (par, h)
@@ -426,11 +473,17 @@ def rank_program(g, core, T, topo):
             else:
                 ou = "OU%d:%d" % (par, h)
                 V(ts(T.OU[:, o0:o0 + L], OF, -1.0, OP.mult, float(CM), OP.add), [of], [ou], L)
-                send([(T.SU[:, r0 + K:r0 + K + L], T.OU[:, o0:o0 + L]), (T.SZ[:, r0 + K:r0 + K + L], OZ)], t + 1, h, "a", [ou, oz],
-                     ["SU%d:%d" % (t + 1, h), "ZZ%d:%d" % (t + 1, h)])
-                send([(T.ED[(t + 1) * NH + h], OF)], t + 1, h, "b", [of], ["ED%d:%d" % (t + 1, h)])
-                V(tt(sm(9), SM[:, x1 + 8:x1 + 16], T.K32[:, c8], OP.add), [k("a1"), "K32"], [k("a2")])
-                V(ts(LA, sm(9), 0.125, OP.mult), [k("a2")], [k("LA")])
+                if P["zsep"]:
+                    send([(T.SU[:, r0 + K:r0 + K + L], T.OU[:, o0:o0 + L])], t + 1, h, "a", [ou], ["SU%d:%d" % (t + 1, h), "oG"])
+                    ops[-1]["lat"] -= 300.0
+                    send([(T.SZ[:, 2 * (r0 + K):2 * (r0 + K + L)], T.OZ[:, 2 * o0:2 * (o0 + L)]), (T.ED[(t + 1) * NH + h], OF)], t + 1, h, "b", [of, oz, "OZ"],
+                         ["ED%d:%d" % (t + 1, h), "ZZ%d:%d" % (t + 1, h), "oG"])
+                else:
+                    send([(T.SU[:, r0 + K:r0 + K + L], T.OU[:, o0:o0 + L]), (T.SZ[:, 2 * (r0 + K):2 * (r0 + K) + L], OZ)], t + 1, h, "a", [ou, oz],
+                         ["SU%d:%d" % (t + 1, h), "ZZ%d:%d" % (t + 1, h), "oG"])
+                    send([(T.ED[(t + 1) * NH + h], OF)], t + 1, h, "b", [of], ["ED%d:%d" % (t + 1, h), "oG"])
+                V(tt(sm(9), sm(8), T.K32[:, c8], OP.add), [k("a1"), "K32"], [k("a2")])
+                V(cp(LA, sm(9)), [k("a2")], [k("LA")])
                 if P["xsa"][h]:
                     A(act(T.XG[:, c], T.XT[:].indirect(LA), AF.Copy), ["XT", k("LA")], [k("XG")], L, G_R)
                     PE([mm(T.pm[:, c], T.IDM[:], ME, True, False), mm(T.pm[:, c], T.IDM[:], T.XG[:, c], False, True)], ["IDM", k("ME"), k("XG")], [k("pm:x")], 2 * L)
@@ -439,23 +492,26 @@ def rank_program(g, core, T, topo):
                     V(tt(T.XS[:, c], T.XT[:].indirect(LA), ME, OP.add), ["XT", k("LA"), k("ME")], [k("XS")], L, G_R)
                     V(ts(T.XD[:, c], T.XS[:, c], 1, OP.arith_shift_right), [k("XS")], [k("XD")], L)
                 V(cp(T.XT[:].indirect(LA), T.XD[:, c]), [k("XD"), k("LA")], [k("XW"), "XT"], L, 3.8)
-            PD, pd, pt = PC[:, INV + h * L:INV + (h + 1) * L], "PD%d:%d" % (par, h), pv[:, 2 * L:3 * L]
-            A(act(T.AB[:, c], PC[:, c], AF.Abs), [pc], [k("AB")], L)
+            PD, pd, pt = PC[:, c], "PD%d:%d" % (par, h), pv[:, 2 * L:3 * L]
+            A(act(T.AB[:, c], PC[:, K + h * L:K + (h + 1) * L], AF.Abs), [pc], [k("AB")], L)
             PE([mm(pt, T.DN[:], T.RESET[:, 1024:1024 + L], True, False), mm(pt, T.TRI[:], HP, False, True)], ["DN", "RESET", "TRI", k("HP")], [kv + ":t"], 2 * L)
             V(tt(pt, pt, W[:, 15 * L:16 * L], OP.add), [kv + ":t", wk], [k("PT"), kv + ":t"], L)
             V(tt(PD, pt, T.AB[:, c], OP.min), [kv + ":t", k("AB")], [pd], L)
-        V(ts(T.PA[:, 0:16], T.XX[:], 0.0, OP.is_lt, float(INV), OP.mult), ["XX0", "XX1"], ["PA"])
-        V(tt(T.PA[:, 16:32], T.PA[:, 0:16], T.KT[:], OP.add), ["PA", "KT"], ["PB"])
-        V(cp(LU[:, 80:96], T.PA[:, 16:32]), ["PB"], ["LG"])
-        A(act(PN[:, 0:K], PC[:].indirect(LU[:, 80:96]), AF.Copy), [pc, "NO%d" % par, "PD%d:0" % par, "PD%d:1" % par, "LG"], [pn], K, G_R)
+        A(act(T.PA[:], T.XX[:], AF.Sign), ["XX0", "XX1"], ["PA"])
+        PE([mm(T.px[:, 0:16], T.IDM[:], T.KK[:, 0:16], True, False), mm(T.px[:, 0:16], T.ID2[:], T.PA[:], False, True)], ["IDM", "ID2", "KK", "PA"], ["px:g"], 128)
+        V(ts(LU[:, 80:96], T.px[:, 0:16], L / 2.0, OP.mult, L + 0.25, OP.add), ["px:g"], ["LG"])
+        A(act(PN[:, K:2 * K], PC[:, 0:2 * K].indirect(LU[:, 80:96]), AF.Copy), [pc, "PD%d:0" % par, "PD%d:1" % par, "LG"], [pn], K, G_R)
         if not last:
+            A(act(PN[:, 2 * K:3 * K], PN[:, K:2 * K], AF.Copy), [pn], [pn + "b"], K)
             PE([mm(T.px[:, 2 * L:2 * L + 16], T.ONF[:], T.HN[:], True, True)], ["ONF", "HN0", "HN1"], ["px:a"], 256)
-            A(lambda: s.activation(out=T.ACT[:], in_=T.px[:, 2 * L:2 * L + 16], func=AF.Copy, accum_out=T.AR[:]), ["px:a"], ["AR"], 16, 1.0, 140.0)
-            A(act(T.AC[:], T.AR[:], AF.Identity, T.PF[:, 12:13], 1.0 / HC), ["AR", "PF12"], ["AC"])
-    A(act(T.AB[:], T["PC%d" % (RO % 2)][:, 0:K], AF.Abs), ["PC%d" % (RO % 2)], ["AB0", "AB1"], K)
+            A(lambda: s.activation(out=T.ACT[:], in_=T.px[:, 2 * L:2 * L + 16], func=AF.Copy, accum_out=T.AR[:]), ["px:a"], ["AR", "A0"], 16, 1.0, 140.0)
+            A(act(T.ACT[:, 0:1], T.AR[:], AF.Identity, T.PF[:, 12:13], 1.0 / HC), ["AR", "PF12"], ["A0"])
+            A(act(T.AQ[:], T.ACT[:, 0:1], AF.Identity, T.PF[:, 15:16], 1.0 / K), ["A0", "PF15"], ["A1"])
+            A(act(T.AC[:], T.AQ[:], AF.Identity, T.ACT[:, 0:1], -float(K)), ["A0", "A1"], ["AC"])
+    A(act(T.AB[:], T["PC%d" % (RO % 2)][:, K:2 * K], AF.Abs), ["PC%d" % (RO % 2)], ["AB0", "AB1"], K)
     V(ts(T.FC[:], T.AB[:], CM - PV, OP.add), ["AB0", "AB1"], ["FC"], K)
     D("S", dma("S", T.yc[:], T.FC[:]), ["FC"], [])
-    A(act(T.SN[:], T["PC%d" % (RO % 2)][:, 0:K], AF.Sign), ["PC%d" % (RO % 2)], ["SN"], K)
+    A(act(T.SN[:], T["PC%d" % (RO % 2)][:, K:2 * K], AF.Sign), ["PC%d" % (RO % 2)], ["SN"], K)
     PE([mm(T.px[:, K:2 * K], T.BO[:], T.SN[:], True, True)], ["BO", "SN"], ["px:n"], K)
     V(ts(T.FL[:], T.px[:, K:2 * K], -0.5, OP.mult, 8.0, OP.add), ["px:n"], ["FL"], K)
     D("S", dma("S", T.yn[:], T.FL[0:128:16, :]), ["FL"], [])

import math
from concourse.bass import DstId, RemoteDMATransfer
from concourse.mybir import AluOpType as OP, AxisListType, ActivationFunctionType as AF

RO = 6
NH, L = 2, 128
K = NH * L
CM = 16383
PV = 65536.0
DP = 3088
RW = DP + 16 * L
HC = float(DP - 1)
INV = 272
TAG = 16384.0
P = {
    "pieces": [[(0, 32, "A"), (32, 32, "V"), (64, 32, "A"), (96, 32, "A")], [(0, 32, "A"), (32, 32, "A"), (64, 32, "A"), (96, 32, "V")]],
    "ends": [[(0, 32, "A"), (32, 32, "V"), (64, 32, "A"), (96, 32, "A")], [(0, 32, "A"), (32, 32, "A"), (64, 32, "A"), (96, 32, "V")]], "endt": [5],
    "chunks": [[(0, 64), (64, 64)], [(0, 64), (64, 64)]],
    "pxn": 32,
    "passes": 500, "seed": 4, "zsep": 0,
    "cyc": 0.93, "hop": 110.0, "gr": 1.55, "pe": 0.55, "wlat": 6000.0, "slat": 3000.0, "pb": 8,
    "zha": [1, 1], "xsa": [1, 1], "msp": [1, 1], "blat": 12000.0, "sq": 5, "sqc": [(1, 1)],
    "adp": [2, 2],
    "bonus": {"CT": -20000.0, "TG": -20000.0},
}

SCRATCH = {
    "XT": ("sbuf", [128, 8192], "bfloat16"), "RP": ("sbuf", [128, NH * RW], "bfloat16"), "GE": ("sbuf", [128, 16 * K], "bfloat16"),
    "W0": ("sbuf", [128, 32 * L], "int32"), "W1": ("sbuf", [128, 32 * L], "int32"), "ED": ("dram", [RO * NH, 128, L], "int32"),
    "PC0": ("sbuf", [128, 3 * K + 16], "float32"), "PC1": ("sbuf", [128, 3 * K + 16], "float32"),
    "EB": ("sbuf", [128, 144], "bfloat16"), "WB": ("sbuf", [128, 144], "float16"), "RESET": ("sbuf", [128, 1152], "bfloat16"),
    "EH": ("sbuf", [128, 144], "bfloat16"), "D8": ("sbuf", [128, 128], "bfloat16"),
    "BO": ("sbuf", [128, 128], "bfloat16"), "TRI": ("sbuf", [128, 128], "bfloat16"), "IDM": ("sbuf", [128, 128], "bfloat16"),
    "NID": ("sbuf", [128, 128], "bfloat16"), "ID2": ("sbuf", [128, 128], "bfloat16"), "ONF": ("sbuf", [128, 128], "float32"),
    "SEL": ("sbuf", [128, 128], "bfloat16"), "IO2": ("sbuf", [128, 128], "bfloat16"), "IO4": ("sbuf", [128, 144], "bfloat16"),
    "K0": ("sbuf", [128, 16], "int32"), "KT": ("sbuf", [128, 16], "float32"), "KF": ("sbuf", [128, 16], "float32"),
    "K32": ("sbuf", [128, 16], "int32"), "KK": ("sbuf", [128, 16], "bfloat16"),
    "PI": ("sbuf", [128, 8], "int32"), "PF": ("sbuf", [128, 24], "float32"), "F4": ("sbuf", [128, 16], "float32"),
    "Z0": ("sbuf", [128, 16], "float32"), "PWS": ("sbuf", [128, 16], "float32"), "PWM": ("sbuf", [128, 16], "float32"),
    "PW": ("sbuf", [128, 1], "float32"), "WI": ("sbuf", [128, 8], "int32"), "WF": ("sbuf", [128, 8], "float32"),
    "LNI": ("sbuf", [128, 256], "int32"), "LNB": ("sbuf", [128, 256], "bfloat16"), "PCM": ("sbuf", [128, 256], "float32"),
    "STI": ("sbuf", [128, 256], "int32"), "BAI": ("sbuf", [128, 256], "int32"), "COI": ("sbuf", [128, 256], "int32"),
    "PL": ("sbuf", [128, 256], "float32"), "S0": ("sbuf", [128, 256], "int32"),
    "ACT": ("sbuf", [128, 16], "float32"), "AR": ("sbuf", [128, 1], "float32"), "AC": ("sbuf", [128, 1], "float32"),
    "HP": ("sbuf", [128, K], "bfloat16"), "ZH": ("sbuf", [128, K], "bfloat16"), "MY": ("sbuf", [128, 2 * K], "bfloat16"),
    "SF": ("sbuf", [128, 16], "float32"), "DB": ("sbuf", [128, 32], "float32"), "HN": ("sbuf", [128, 16], "float32"),
    "HB": ("sbuf", [128, 16], "bfloat16"), "YQ": ("sbuf", [128, 16], "float32"), "XX": ("sbuf", [128, 16], "float32"),
    "PA": ("sbuf", [128, 16], "bfloat16"), "AQ": ("sbuf", [128, 1], "bfloat16"), "SM": ("sbuf", [128, 256], "int32"), "LU": ("sbuf", [128, 128], "uint16"),
    "XS": ("sbuf", [128, K], "int32"), "XD": ("sbuf", [128, K], "int32"), "AB": ("sbuf", [128, K], "float32"),
    "SG": ("sbuf", [128, K], "bfloat16"), "Q1": ("sbuf", [128, K], "float32"), "Q2": ("sbuf", [128, K], "int32"),
    "FC": ("sbuf", [128, K], "float32"), "FL": ("sbuf", [128, K], "float32"), "YSF": ("sbuf", [128, K], "float32"),
    "NBO": ("sbuf", [128, 128], "bfloat16"), "DN": ("sbuf", [128, 128], "bfloat16"), "XG": ("sbuf", [128, K], "bfloat16"),
    "SN": ("sbuf", [128, K], "bfloat16"),
    "SU": ("sbuf", [128, RO * K], "uint16"), "SZ": ("sbuf", [128, 2 * RO * K], "bfloat16"),
    "OU": ("sbuf", [128, 2 * K], "uint16"), "OZ": ("sbuf", [128, 4 * K], "bfloat16"), "OF": ("sbuf", [128, 2 * K], "int32"),
}
for _n in ("pz0", "pz1", "pv0", "pv1", "pu0", "pu1", "pm", "px"):
    SCRATCH[_n] = ("psum", [128, 512], "float32")
for _d in range(4):
    SCRATCH["BB%d" % _d] = ("sbuf", [128, K], "float32")

SEMAPHORES = ["cV", "cA", "cT", "cG", "loc"] + ["lo%d" % i for i in range(20)] + ["dm%d" % i for i in range(32)] + ["bs%d" % d for d in (1, 2, 3)] + \
             ["ar%d%d%s" % (t, c, s) for t in range(1, RO) for c in range(NH) for s in "ab"]

ORDER = {}


CASES = [
    (1.04, 1.55, 3.8, 0.52, 60.0, 2500.0, 1.0), (0.91, 1.55, 3.8, 0.46, 130.0, 2500.0, 1.0), (0.91, 1.55, 3.8, 0.46, 60.0, 4000.0, 1.0),
    (0.91, 1.55, 3.8, 0.75, 60.0, 2500.0, 1.0), (1.2, 2.0, 5.5, 0.61, 100.0, 2500.0, 1.1)]


def step_name(reads, writes):
    w = writes[0] if writes else reads[0]
    if w[:2] in ("OZ", "OF", "OU", "PD", "SU", "ED", "PC"):
        return w[:2] + w[3:]
    ge = [x.split(":") for x in [w] + list(reads) if x.startswith("GE")]
    return w[:3] + ge[0][2] + str(int(ge[0][1]) // 6) if ge else w


def place(ops, pred, key):
    n = len(ops)
    succ = [[] for _ in range(n)]
    for i in range(n):
        for j, lat in pred[i]:
            succ[j].append((i, lat))
    left = [len(pred[i]) for i in range(n)]
    est = [0.0] * n
    start = [0.0] * n
    busy = {}
    ready = [i for i in range(n) if left[i] == 0]
    while ready:
        i = min(ready, key=lambda x: (key[x], x))
        ready.remove(i)
        c, t = ops[i]["cost"], est[i]
        line = busy.setdefault(ops[i]["q"], [])
        x = len(line)
        while x > 0 and line[x - 1][1] > t:
            x -= 1
        while x < len(line) and line[x][0] < t + c:
            t = max(t, line[x][1])
            x += 1
        line.insert(x, (t, t + c))
        start[i] = t
        for y, lat in succ[i]:
            est[y] = max(est[y], t + c + lat)
            left[y] -= 1
            if left[y] == 0:
                ready.append(y)
    return start


def make_order(ops, deps):
    n = len(ops)
    fwd = [[(j, ops[j]["lat"] if w else 0.0) for j, w in deps[i].items()] for i in range(n)]
    bwd = [[] for _ in range(n)]
    for i in range(n):
        for j, lat in fwd[i]:
            bwd[j].append((i, lat))
    tail = [0.0] * n
    for i in range(n - 1, -1, -1):
        tail[i] = ops[i]["cost"] + max([lat + tail[x] for x, lat in bwd[i]] + [ops[i]["lat"]])
    cost = [op["cost"] for op in ops]
    cases = []
    for cyc, gather, scatter, pe, hop, write, weight in CASES:
        by = {P["gr"]: 0.2 + 0.8 * gather / P["gr"], 3.8: 0.1 + 0.9 * scatter / 3.8}
        cs = [op["cost"] * (cyc / P["cyc"] * by.get(op["rate"], 1.0) if op["rate"] else pe / P["pe"] if op["q"] == "T" else 1.0) for op in ops]
        ed = [[(x, hop if lat == P["hop"] else lat + (write - P["slat"] if ops[i]["kind"] == "r" and lat else 0.0)) for x, lat in bwd[i]] for i in range(n)]
        cases.append((cs, ed, weight))

    def length(st):
        seq, total = sorted(range(n), key=lambda i: (st[i], i)), 0.0
        for cs, ed, weight in cases:
            est, free = [0.0] * n, {}
            for i in seq:
                e = max(est[i], free.get(ops[i]["q"], 0.0)) + cs[i]
                free[ops[i]["q"]] = e
                for x, lat in ed[i]:
                    if est[x] < e + lat:
                        est[x] = e + lat
                est[i] = e + ops[i]["lat"]
            total += weight * max(est)
        return total

    kinds = sorted(set(op["name"] for op in ops))
    state = [P["seed"]]

    def draw():
        state[0] = (state[0] * 6364136223846793005 + 1442695040888963407) % 2 ** 64
        return (state[0] >> 11) / 2.0 ** 53

    best, key = None, [-x for x in tail]
    for it in range(P["passes"]):
        st = place(ops, fwd, key)
        back = place(ops, bwd, [-(st[i] + cost[i]) for i in range(n)])
        for x in (st, place(ops, fwd, [-(back[i] + cost[i]) for i in range(n)])):
            e = length(x)
            if best is None or e <= best[0]:
                best = (e, x)
        shift = {kinds[int(draw() * len(kinds))]: 3000.0 * (draw() + draw() + draw() - 1.5) for _ in range((0, 1, 2, 3, 6)[min(it, 1 + int(4 * draw()))])}
        key = [best[1][i] + shift.get(ops[i]["name"], 0.0) for i in range(n)]
    ORDER["plan"], ORDER["ops"] = best, ops
    return sorted(range(n), key=lambda i: (best[1][i], i))


def rank_program(g, core, T, topo):
    rank = T.rank_of(core)
    if rank is None:
        return
    n_ranks = len(T.cores)
    ops = []
    eng = {"V": g.vector, "A": g.scalar, "T": g.tensor, "S": g.sync, "G": g}
    G_R = P["gr"]
    now = [0.0, -1]

    CYC = P["cyc"]

    def add(q, fns, reads, writes, cost, lat=P["hop"], kind="c", sem=None, amount=0):
        banks = sorted(set(k.split(":")[0] for k in list(reads) + list(writes) if k.startswith("p")))
        ops.append({"q": q, "fns": fns if isinstance(fns, list) else [fns], "r": list(reads), "w": list(writes), "cost": cost,
                    "lat": lat, "kind": kind, "sem": sem, "amount": amount, "banks": banks, "rate": None, "t": now[1],
                    "name": q + step_name(reads, writes)})

    def vc(n, rate=1.0):
        return max(64.0, n * rate) * CYC

    def V(fn, reads, writes, n=16, rate=1.0):
        add("V", fn, reads, writes, vc(n, rate) + (60.0 if rate in (G_R, 3.8) else 0.0))
        ops[-1]["rate"] = rate

    def A(fn, reads, writes, n=16, rate=1.0, extra=0.0):
        add("A", fn, reads, writes, vc(n, rate) + extra + (75.0 if rate == G_R else 0.0))
        ops[-1]["rate"] = rate

    def PE(fns, reads, writes, cyc):
        pb = P["pb"]
        for x in range(0, len(fns), pb):
            add("T", fns[x:x + pb], reads, writes, cyc * P["pe"] * len(fns[x:x + pb]) / len(fns))

    def G(fn, reads, writes, n):
        add("G", fn, reads, writes, 150 + 2 * n * CYC)

    ndma = [0]

    def D(q, fns, reads, writes, lat=2500.0):
        fns = fns if isinstance(fns, list) else [fns]
        add(q, fns, reads, writes, 60.0 * len(fns), lat, "d", "dm%d" % ndma[0], 16 * len(fns))
        ndma[0] += 1

    v, s, te = g.vector, g.scalar, g.tensor

    def tt(o, a, b, op):
        return lambda: v.tensor_tensor(out=o, in0=a, in1=b, op=op)

    def ts(o, a, s1, op0, s2=None, op1=None):
        if op1 is None:
            return lambda: v.tensor_scalar(out=o, in0=a, scalar1=s1, scalar2=None, op0=op0)
        return lambda: v.tensor_scalar(out=o, in0=a, scalar1=s1, scalar2=s2, op0=op0, op1=op1)

    def cp(o, a):
        return lambda: v.tensor_copy(out=o, in_=a)

    def scan(o, d0, d1, op1, ini=0.0):
        return lambda: v.tensor_tensor_scan(out=o, data0=d0, data1=d1, initial=ini, op0=OP.mult, op1=op1)

    def act(o, a, f, bias=0.0, scale=1.0):
        return lambda: s.activation(out=o, in_=a, func=f, bias=bias, scale=scale)

    def mm(o, lh, rh, st, sp):
        return lambda: te.matmul(out=o, lhsT=lh, rhs=rh, start=st, stop=sp)

    def ms(o, x):
        return lambda: v.memset(o, x)

    def io(o, pat, ch, flag=True, base=0):
        if flag:
            return lambda: g.iota(o, pattern=pat, base=base, channel_multiplier=ch, allow_small_or_imprecise_dtypes=True)
        return lambda: g.iota(o, pattern=pat, base=base, channel_multiplier=ch)

    def dma(q, o, a):
        return lambda: eng[q].dma_start(out=o, in_=a)

    D("A", dma("A", T.STI[:], T.stk[:]), [], ["STI"])
    D("A", [dma("A", T.SZ[:, h * K:h * K + L], T.z[:, h * L:(h + 1) * L]) for h in range(NH)], [], ["ZZ0:0", "ZZ0:1"])
    D("S", dma("S", T.XT[:], T.xt[:]), [], ["XT", "XL"], 9000.0)
    D("S", dma("S", T.WI[:, 0:1], T.w[:]), [], ["WI"], 9000.0)
    D("S", dma("S", T.BAI[:], T.bas[:]), [], ["BAI"], 9000.0)
    D("S", dma("S", T.LNI[0:8, :], T.ln[:]), [], ["LNI"], 9000.0)
    D("S", dma("S", T.COI[:], T.con[:]), [], ["COI"], 9000.0)

    V(ms(T.PF[:, 10:11], math.exp(5.0)), [], ["PF10"])
    V(ms(T.PF[:, 11:12], 149.23), [], ["PF11"])
    V(ms(T.PF[:, 12:13], 2040.25 + 129 * K), [], ["PF12"])
    V(ms(T.PF[:, 15:16], -0.499), [], ["PF15"])
    G(io(T.PI[:, 0:1], [[0, 1]], 1, False), [], ["PI0"], 1)
    V(ts(T.PI[:, 1:2], T.PI[:, 0:1], 15, OP.bitwise_and), ["PI0"], ["PI1"])
    V(ts(T.PI[:, 2:3], T.PI[:, 0:1], 112, OP.bitwise_and), ["PI0"], ["PI2"])
    V(cp(T.PF[:, 0:3], T.PI[:, 0:3]), ["PI0", "PI1", "PI2"], ["PF0"])
    pf, pmf, p16 = T.PF[:, 0:1], T.PF[:, 1:2], T.PF[:, 2:3]
    V(ts(T.PF[:, 3:4], p16, 16.0, OP.add), ["PF0"], ["PF3"])
    V(ts(T.PF[:, 4:5], pmf, -1.0, OP.mult, 15.0, OP.add), ["PF0"], ["PF4"])
    V(ts(T.PF[:, 5:6], pf, 16.0, OP.mult), ["PF0"], ["PF5"])
    V(ts(T.PF[:, 6:7], pmf, 0.5, OP.is_gt), ["PF0"], ["PF6"])
    G(io(T.IO4[:], [[1, 144]], 0), [], ["IO4"], 144)
    G(io(T.IO2[:], [[16, 8], [0, 16]], 0), [], ["IO2"], 128)
    G(io(T.K0[:], [[16, 16]], 0, False), [], ["K0"], 16)
    V(cp(T.SU[:, 0:K], T.STI[:]), ["STI"], ["SU0:0", "SU0:1"], K)
    V(ts(T.S0[:], T.STI[:], -1.0, OP.mult, float(CM), OP.add), ["STI"], ["S0"], K)
    for h in range(NH):
        D("S", dma("S", T.ED[h], T.S0[:, h * L:(h + 1) * L]), ["S0"], ["ED0:%d" % h])
    V(ts(T.IDM[:], T.IO4[:, 0:128], pf, OP.is_equal), ["IO4", "PF0"], ["IDM"], 128, .5)
    V(ts(T.NID[:], T.IDM[:], -1.0, OP.mult), ["IDM"], ["NID"], 128, .5)
    V(ts(T.ID2[:], T.IDM[:], 2.0, OP.mult), ["IDM"], ["ID2"], 128, .5)
    V(ts(T.EB[:], T.IO4[:], T.PF[:, 3:4], OP.is_equal), ["IO4", "PF3"], ["EB"], 144, .5)

    def toward(M, i):
        return M[:, 16 - i:144 - i]

    V(ms(T.RESET[:, 512:], 1.0), [], ["RESET"], 640, .5)
    V(ms(T.RESET[:, 512:1024:16], 0.0), [], ["RESET"], 64, .5)
    SQ = P["sq"]
    if P["sqc"]:
        V(ms(T.PF[:, 9:10], 0.5), [], ["PF9"])
        V(ts(T.EH[:], T.EB[:], 0.5, OP.mult), ["EB"], ["EH"], 144, .5)
        V(ts(T.PF[:, 7:8], pmf, 15.5 - SQ, OP.is_gt, 8.0, OP.mult), ["PF0"], ["PF7"])
        V(ts(T.D8[:], T.IDM[:], T.PF[:, 7:8], OP.mult), ["IDM", "PF7"], ["D8"], 128, .5)
    for h in range(NH):
        V(ms(T.RP[:, h * RW + 16 * L:h * RW + DP], 0.0), [], ["GAP%d" % h], DP - 16 * L, .5)
    V(ts(T.BO[:], T.IO2[:], p16, OP.is_equal), ["IO2", "PF0"], ["BO"], 128, .5)
    V(ts(T.TRI[:], T.IO4[:, 0:128], pf, OP.is_ge, 512.0, OP.mult), ["IO4", "PF0"], ["TRI"], 128, .5)
    V(tt(T.TRI[:], T.TRI[:], T.BO[:], OP.mult), ["TRI", "BO"], ["TRI"], 128, 2)
    V(ms(T.ONF[:], 1.0), [], ["ONF"], 128)
    V(ts(T.KT[:], T.K0[:], pmf, OP.add), ["K0", "PF0"], ["KT"])
    V(ts(T.KF[:, 0:8], T.KT[:, 0:8], 16.0, OP.mult, DP + 20.47, OP.add), ["KT"], ["KF"])
    V(ts(T.K32[:], T.KT[:], 32.0, OP.mult), ["KT"], ["K32"])
    if any(P["zha"]):
        V(ts(T.NBO[:], T.BO[:], -1.0, OP.mult), ["BO"], ["NBO"], 128, .5)
    V(ts(T.DN[:], T.IDM[:], -PV, OP.mult), ["IDM"], ["DN"], 128, .5)
    A(act(T.PF[:, 13:14], T.PF[:, 10:11], AF.Ln), ["PF10"], ["PF13"], 1, 1.0, 1500.0)
    V(ts(T.PF[:, 14:15], T.PF[:, 13:14], 0.5, OP.add), ["PF13"], ["PF14"])
    V(ts(T.KK[:], T.KT[:], 2.0 / L, OP.mult), ["KT"], ["KK"])
    V(ms(T.F4[:], math.e), [], ["F4"])
    V(ms(T.Z0[:], 0.0), [], ["Z0"])
    V(scan(T.PWS[:], T.F4[:], T.Z0[:], OP.add, math.exp(5.0)), ["F4", "Z0"], ["PWS"])
    V(ms(T.PWS[:, 15:16], 0.0), [], ["PWS"])
    V(ts(T.PWM[:], T.IO4[:, 0:16], T.PF[:, 4:5], OP.is_equal), ["IO4", "PF4"], ["PWM"])
    V(tt(T.PWM[:], T.PWM[:], T.PWS[:], OP.mult), ["PWM", "PWS"], ["PWM"])
    V(lambda: v.tensor_reduce(out=T.PW[:], in_=T.PWM[:], axis=AxisListType.X, op=OP.add), ["PWM"], ["PW"])
    V(cp(T.WF[:, 0:1], T.WI[:, 0:1]), ["WI"], ["WF"])
    V(ts(T.WB[:], T.EB[:], T.WF[:, 0:1], OP.mult), ["EB", "WF"], ["WB"], 144, .5)
    V(ms(T.AC[:], K - 8.0), [], ["AC"])
    for x in range(2 * NH * P["zsep"]):
        V(ms(T.OZ[:, x * K + L:(x + 1) * K], 0.0), [], ["OZ"], L, .5)
    for x in range(2, 31, 4):
        y = min(x + 4, 31)
        V(ms(T.W0[:, x * L:y * L], int(PV)), [], ["WM0:%d" % x], (y - x) * L)
    G(io(T.W1[:, 2 * L:31 * L], [[0, 29 * L]], 0, False, int(PV)), ["IO4", "IO2", "K0", "PI0"], ["WM1:2"], 29 * L)
    V(ts(T.BB0[:], T.BAI[:], -1.0, OP.mult, 2.0 * CM + 1.0, OP.add), ["BAI"], ["BB0"], K)

    def remote(pairs, dst, sem, lsem):
        es = topo.engines(core, dst)
        per = len(es) // len(pairs)
        rid, pid, _ = topo.addr(dst)
        tr = []
        for i, (o, a) in enumerate(pairs):
            m = sum(1 << e for e in es[i * per:(i + 1) * per])
            tr.append(RemoteDMATransfer(dst_ids=[DstId(rid=rid, pnc=pid)], dma_engine_mask=m, remote_sem=T.sem[sem], srcs=[a], dsts=[o], alu_op=0))
        return lambda: g.remote_dma_fused(tr, local_sem=T.sem[lsem])

    n_eng = len(topo.engines(core, T.cores[(rank + 1) % n_ranks]))
    for d in (1, 2, 3):
        dst = T.cores[(rank + d) % n_ranks]
        add("G", remote([(T["BB%d" % d][:], T.BB0[:])], dst, "bs%d" % d, "loc"), ["BB0"], ["BB%d" % d, "oB"], 1000.0, P["blat"], "r", "bs%d" % d, n_eng)
    V(cp(T.LNB[0:8, :], T.LNI[0:8, :]), ["LNI"], ["LNB"], K)
    V(ts(T.SEL[0:8, :], T.IO2[0:8, :], T.PF[0:8, 5:6], OP.is_equal), ["IO2", "PF5"], ["SEL"], 128)
    PE([mm(T.pm[:, 0:K], T.SEL[0:8, :], T.LNB[0:8, :], True, True)], ["SEL", "LNB"], ["pm:0"], K)
    V(ts(T.pm[:, 0:K], T.pm[:, 0:K], pmf, OP.is_le, 0.5, OP.subtract), ["pm:0", "PF0"], ["pm:0"], K)
    V(ts(T.PL[:], T.COI[:], 2.0, OP.mult, 2.0 * (PV - CM), OP.add), ["COI"], ["PL"], K)
    V(tt(T.PC0[:, K:2 * K], T.pm[:, 0:K], T.PL[:], OP.mult), ["PL", "pm:0"], ["PC0"], K)
    A(act(T.PC0[:, 2 * K:3 * K], T.PC0[:, K:2 * K], AF.Copy), ["PC0"], ["PC0b"], K)
    for x in range(2):
        V(ms(T["PC%d" % x][:, 3 * K:], PV), [], ["NO%d" % x])

    nloc = [0]
    nxt = T.cores[(rank + 1) % n_ranks]
    SM, LU, RP, GE = T.SM, T.LU, T.RP, T.GE
    PXN = P["pxn"]

    def send(pairs, t, h, part, reads, writes):
        sem, ls = "ar%d%d%s" % (t, h, part), "lo%d" % nloc[0]
        nloc[0] += 1
        add("G", remote(pairs, nxt, sem, ls), reads, writes, 1000.0, P["slat"] - 1000.0, "r", sem, n_eng)
        ops[-1]["lsem"] = ls

    for t in range(RO):
        last = t == RO - 1
        par = t % 2
        now[1] = t
        PC, PN, pc, pn = T["PC%d" % par], T["PC%d" % (1 - par)], "PC%d" % par, "PC%d" % (1 - par)
        BB, bbk = T["BB%d" % (t % 4)], "BB%d" % (t % 4)
        for h in range(NH):
            for p0, n, pq in P["ends" if t in P["endt"] else "pieces"][h]:
                a, o = t * K + h * L + p0, RP[:, h * RW + 16 * p0:h * RW + 16 * (p0 + n)]
                rd, rk = ["XT", "SU%d:%d" % (t, h)], ["R%d:%d" % (h, x // 16) for x in range(p0, p0 + n, 16)]
                if pq == "A":
                    A(act(o, T.XT[:].indirect(T.SU[:, a:a + n]), AF.Copy), rd, rk + ["oA"], n * 16, G_R)
                else:
                    V(cp(o, T.XT[:].indirect(T.SU[:, a:a + n])), rd, rk, n * 16, G_R)
        for h in range(NH):
            r0, o0, c = t * K + h * L, par * K + h * L, slice(h * L, (h + 1) * L)
            c8 = slice(8 * h, 8 * h + 8)
            zz, Z = "ZZ%d:%d" % (t, h), T.SZ[:, 2 * r0:2 * r0 + L]
            pz, pv, pu, kz, kv, ku = T["pz%d" % h], T["pv%d" % h], T["pu%d" % h], "pz%d" % h, "pv%d" % h, "pu%d" % h
            W, wk = T["W%d" % h], "W%d" % h
            R0 = h * RW

            def k(x):
                return "%s%d" % (x, h)

            def sm(x):
                return SM[:, x * 16 + 8 * h:x * 16 + 8 * h + 8]

            src = T.ED[t * NH + h]
            D("S", [dma("S", W[i:128:16, (15 - i) * L:(31 - i) * L], src) for i in range(16)] + [dma("S", W[:, 31 * L:32 * L], src)],
              ["ED%d:%d" % (t, h), "XL"] + ["WM%d:%d" % (h, x) for x in range(2, 31, 4)], [wk], P["wlat"])
            PE([mm(pz[:, 0:L], T.IDM[:], Z, True, True)], ["IDM", zz], [kz + ":z"], L)
            for ci, (c0, cn) in enumerate(P["chunks"][h]):
                Rk = ["R%d:%d" % (h, x // 16) for x in range(c0, c0 + cn, 16)]
                g0 = 16 * (h * L + c0)
                sq = SQ if (h, ci) in P["sqc"] else 0
                if sq:
                    fns = []
                    for x in range(sq):
                        ob = pu[:, x * cn:(x + 1) * cn]
                        fns += [mm(ob, T.NID[:], T.SZ[:, 2 * r0 + c0:2 * r0 + c0 + cn], True, False), mm(ob, T.IDM[:], RP[:, R0 + 16 * c0 + 16 - sq + x:R0 + 16 * (c0 + cn):16], False, True)]
                    PE(fns, ["IDM", "NID", zz] + Rk, [ku + ":g"], 2 * sq * cn)
                    A(act(GE[:, g0 + (16 - sq) * cn:g0 + 16 * cn], pu[:, 0:sq * cn], AF.Sign, T.PF[:, 9:10]), [ku + ":g", "PF9"],
                      ["GE%d:%d:%d" % (h, i, ci) for i in range(16 - sq, 16)], sq * cn)
                    PE([mm(pv[:, c0:c0 + cn], T.D8[:], T.RESET[:, 1024:1024 + cn], True, False)], ["D8", "RESET"], [kv + ":v"], cn)
                for i in range(1, 16 - sq):
                    V(tt(GE[:, g0 + i * cn:g0 + (i + 1) * cn], RP[:, R0 + 16 * c0 + i:R0 + 16 * (c0 + cn):16], pz[:, c0:c0 + cn], OP.is_ge),
                      [kz + ":z"] + Rk, ["GE%d:%d:%d" % (h, i, ci)], cn)
                for i in range(1, 16):
                    PE([mm(pv[:, c0:c0 + cn], toward(T.EB if i < 16 - sq else T.EH, i), GE[:, g0 + i * cn:g0 + (i + 1) * cn], i == 1 and not sq, i == 15)],
                       ["EB", "EH", "GE%d:%d:%d" % (h, i, ci)], [kv + ":v"], cn)
                for x0 in range(c0, c0 + cn, PXN):
                    V(scan(RP[:, R0 + DP + 16 * x0:R0 + DP + 16 * (x0 + PXN)], T.RESET[:, 512:512 + 16 * PXN], RP[:, R0 + 16 * x0:R0 + 16 * (x0 + PXN)], OP.max),
                      ["R%d:%d" % (h, x // 16) for x in range(x0, x0 + PXN, 16)] + ["RESET"], ["PX%d:%d" % (h, x0)], 16 * PXN, .5)
            allR = ["R%d:%d" % (h, x) for x in range(L // 16)] + ["PX%d:%d" % (h, x) for x in range(0, L, PXN)] + [k("GAP")]
            HP = T.HP[:, c]
            V(ts(HP, pv[:, 0:L], 8.5, OP.is_ge, T.PW[:], OP.mult), [kv + ":v", "PW"], [k("HP")], L)
            PE([mm(pv[:, 3 * L:3 * L + 8], toward(T.EB, i), T.HP[:, h * L + i:(h + 1) * L:16], i == 0, i == 15) for i in range(16)], ["EB", k("HP")], [kv + ":l"], 16 * 64)
            SF, DM, DY = T.SF[:, c8], T.DB[:, 16 * h:16 * h + 8], T.DB[:, 16 * h + 8:16 * h + 16]
            A(act(SF, pv[:, 3 * L:3 * L + 8], AF.Ln, T.PF[:, 10:11]), [kv + ":l", "PF10"], [k("SF")] + (["oB"] if t == 0 and h == 1 else []))
            if P["zha"][h]:
                PE([mm(pv[:, L:2 * L], T.IDM[:], Z, True, False), mm(pv[:, L:2 * L], T.NBO[:], HP, False, True)], ["IDM", "NBO", zz, k("HP")], [kv + ":s"], 2 * L)
            else:
                PE([mm(pv[:, L:2 * L], T.BO[:], HP, True, True)], ["BO", k("HP")], [kv + ":s"], L)
            V(tt(DM, T.KF[:, 0:8], SF, OP.subtract), [k("SF"), "KF"], [k("DM")])
            V(ts(T.HN[:, c8], SF, T.PF[:, 14:15], OP.is_gt, -HC, OP.mult), [k("SF"), "PF14"], [k("HN")])
            V(tt(DY, DM, T.HN[:, c8], OP.add), [k("DM"), k("HN")], [k("DY")])
            m0 = 2 * L * h
            ME, YE = T.MY[:, m0:m0 + L], T.MY[:, m0 + L:m0 + 2 * L]
            if P["msp"][h]:
                V(cp(LU[:, 16 * h:16 * h + 8], DM), [k("DM")], [k("LM")])
                V(cp(LU[:, 16 * h + 8:16 * h + 16], DY), [k("DY")], [k("LY")])
                A(act(ME, RP[:, R0:R0 + RW].indirect(LU[:, 16 * h:16 * h + 8]), AF.Copy), allR + [k("LM")], [k("ME")], L, G_R)
                A(act(YE, RP[:, R0:R0 + RW].indirect(LU[:, 16 * h + 8:16 * h + 16]), AF.Copy), allR + [k("LY")], [k("MY")], L, G_R)
            else:
                V(cp(LU[:, 16 * h:16 * h + 16], T.DB[:, 16 * h:16 * h + 16]), [k("DM"), k("DY")], [k("LM"), k("LY")])
                A(act(T.MY[:, m0:m0 + 2 * L], RP[:, R0:R0 + RW].indirect(LU[:, 16 * h:16 * h + 16]), AF.Copy), allR + [k("LM"), k("LY")], [k("MY"), k("ME")], 2 * L, G_R)
            A(act(T.HB[:, c8], SF, AF.Identity, T.PF[:, 11:12], -1.0), [k("SF"), "PF11"], [k("HB")])
            if P["zha"][h]:
                A(act(T.ZH[:, c], pv[:, L:2 * L], AF.Relu), [kv + ":s"], [k("ZH")], L)
            else:
                V(tt(T.ZH[:, c], Z, pv[:, L:2 * L], OP.min), [zz, kv + ":s"], [k("ZH")], L)
            PE([mm(pu[:, 0:8], toward(T.WB, i), T.MY[:, m0 + i:m0 + L:16], i == 0, i == 15) for i in range(16)], ["WB", k("ME")], [ku + ":u"], 16 * 64)
            PE([mm(pz[:, 400:408], toward(T.EB, i), T.MY[:, m0 + L + i:m0 + 2 * L:16], i == 0, i == 15) for i in range(16)], ["EB", k("MY")], [kz + ":y"], 16 * 64)
            V(ts(sm(0), pu[:, 0:8], 16.0, OP.add), [ku + ":u"], [k("u0")])
            if not last:
                V(cp(sm(7), pu[:, 0:8]), [ku + ":u"], [k("a0")])
                V(ts(sm(8), sm(7), 31, OP.bitwise_and), [k("a0")], [k("a1")])
            PE([mm(pu[:, 16:24], T.IDM[:], T.KK[:, 0:8], True, False), mm(pu[:, 16:24], T.ID2[:], T.HB[:, c8], False, False)],
               ["IDM", "KK", "ID2", k("HB")], [ku + ":m"], 128)
            V(ts(sm(1), sm(0), 4095, OP.bitwise_and), [k("u0")], [k("u1")])
            V(tt(sm(2), sm(1), sm(1), OP.mult), [k("u1")], [k("yq")])
            V(ts(sm(3), sm(2), 5, OP.arith_shift_right, 255, OP.bitwise_and), [k("yq")], [k("j")])
            V(ts(sm(4), pz[:, 400:408], 1024.0, OP.mult, HC + 2 * K, OP.add), [kz + ":y"], [k("y0")])
            V(ts(sm(5), sm(4), 4095, OP.bitwise_and), [k("y0")], [k("y1")])
            V(tt(T.XX[:, c8], sm(5), T.HN[:, c8], OP.add), [k("y1"), k("HN")], [k("XX")])
            V(tt(sm(6), sm(3), T.XX[:, c8], OP.max), [k("j"), k("XX")], [k("jp")])
            LJ, LR, LA = LU[:, 32 + 8 * h:40 + 8 * h], LU[:, 48 + 8 * h:56 + 8 * h], LU[:, 64 + 8 * h:72 + 8 * h]
            V(ts(LJ, sm(6), T.AC[:], OP.add, 2.0 * K, OP.min), [k("jp"), "AC"], [k("LJ")])
            pk = [pc, pc + "b", "NO%d" % par, k("LJ")]
            A(act(T.SG[:, c], PC[:, K:].indirect(LJ), AF.Sign, 0.0, T.PF[:, 6:7]), pk + ["PF6"], [k("SG")], L, G_R)
            V(tt(T.Q1[:, c], PC[:, K:].indirect(LJ), BB[:, c], OP.min), pk + [bbk], [k("QA")], L, G_R)
            PE([mm(pu[:, 16:24], toward(T.EB, i), T.SG[:, h * L + i:(h + 1) * L:16], False, i == 15) for i in range(16)], ["EB", k("SG")], [ku + ":n", ku + ":m"], 16 * 64)
            V(ts(LR, pu[:, 16:24], L / 2.0, OP.mult, (5.5 - 128.0) * L + 0.25, OP.add), [ku + ":m"], [k("LR")])
            if P["zha"][h]:
                PE([mm(pz[:, L:2 * L], T.NID[:], Z, True, False), mm(pz[:, L:2 * L], T.IDM[:], YE, False, False), mm(pz[:, L:2 * L], T.IDM[:], T.ZH[:, c], False, True)],
                   ["IDM", "NID", zz, k("MY"), k("ZH")], [kz + ":d"], 3 * L)
            else:
                PE([mm(pz[:, L:2 * L], T.IDM[:], YE, True, False), mm(pz[:, L:2 * L], T.NID[:], T.ZH[:, c], False, True)], ["IDM", "NID", k("MY"), k("ZH")], [kz + ":d"], 2 * L)
            OZ, oz = T.OZ[:, 2 * o0:2 * o0 + L], "OZ%d:%d" % (par, h)
            A(act(OZ, pz[:, L:2 * L], AF.Abs), [kz + ":d"], [oz], L)
            V(tt(T.Q2[:, c], W[:, 2 * L:32 * L].indirect(LR), T.Q1[:, c], OP.min), [wk, k("QA"), k("LR")], [k("QB")], L, G_R)
            OF, of = T.OF[:, o0:o0 + L], "OF%d:%d" % (par, h)
            V(ts(OF, T.Q2[:, c], CM, OP.bitwise_and), [k("QB")], [of], L)
            if last:
                V(ts(T.YSF[:, c], OF, -1.0, OP.mult, float(CM), OP.add), [of], [k("YSF")], L)
                D("S", dma("S", T.ys[:, c], T.YSF[:, c]), [k("YSF")], [])
                D("S", dma("S", T.yz[:, c], OZ), [oz], [])
            else:
                ou = "OU%d:%d" % (par, h)
                V(ts(T.OU[:, o0:o0 + L], OF, -1.0, OP.mult, float(CM), OP.add), [of], [ou], L)
                if P["zsep"]:
                    send([(T.SU[:, r0 + K:r0 + K + L], T.OU[:, o0:o0 + L])], t + 1, h, "a", [ou], ["SU%d:%d" % (t + 1, h), "oG"])
                    ops[-1]["lat"] -= 300.0
                    send([(T.SZ[:, 2 * (r0 + K):2 * (r0 + K + L)], T.OZ[:, 2 * o0:2 * (o0 + L)]), (T.ED[(t + 1) * NH + h], OF)], t + 1, h, "b", [of, oz, "OZ"],
                         ["ED%d:%d" % (t + 1, h), "ZZ%d:%d" % (t + 1, h), "oG"])
                else:
                    send([(T.SU[:, r0 + K:r0 + K + L], T.OU[:, o0:o0 + L]), (T.SZ[:, 2 * (r0 + K):2 * (r0 + K) + L], OZ)], t + 1, h, "a", [ou, oz],
                         ["SU%d:%d" % (t + 1, h), "ZZ%d:%d" % (t + 1, h), "oG"])
                    send([(T.ED[(t + 1) * NH + h], OF)], t + 1, h, "b", [of], ["ED%d:%d" % (t + 1, h), "oG"])
                V(tt(sm(9), sm(8), T.K32[:, c8], OP.add), [k("a1"), "K32"], [k("a2")])
                V(cp(LA, sm(9)), [k("a2")], [k("LA")])
                if P["xsa"][h]:
                    A(act(T.XG[:, c], T.XT[:].indirect(LA), AF.Copy), ["XT", k("LA")], [k("XG")], L, G_R)
                    PE([mm(T.pm[:, c], T.IDM[:], ME, True, False), mm(T.pm[:, c], T.IDM[:], T.XG[:, c], False, True)], ["IDM", k("ME"), k("XG")], [k("pm:x")], 2 * L)
                    V(ts(T.XD[:, c], T.pm[:, c], 0.5, OP.mult, -0.25, OP.add), [k("pm:x")], [k("XD")], L)
                else:
                    V(tt(T.XS[:, c], T.XT[:].indirect(LA), ME, OP.add), ["XT", k("LA"), k("ME")], [k("XS")], L, G_R)
                    V(ts(T.XD[:, c], T.XS[:, c], 1, OP.arith_shift_right), [k("XS")], [k("XD")], L)
                V(cp(T.XT[:].indirect(LA), T.XD[:, c]), [k("XD"), k("LA")], [k("XW"), "XT"], L, 3.8)
            PD, pd, pt = PC[:, c], "PD%d:%d" % (par, h), pv[:, 2 * L:3 * L]
            A(act(T.AB[:, c], PC[:, K + h * L:K + (h + 1) * L], AF.Abs), [pc], [k("AB")], L)
            PE([mm(pt, T.DN[:], T.RESET[:, 1024:1024 + L], True, False), mm(pt, T.TRI[:], HP, False, True)], ["DN", "RESET", "TRI", k("HP")], [kv + ":t"], 2 * L)
            V(tt(pt, pt, W[:, 15 * L:16 * L], OP.add), [kv + ":t", wk], [k("PT"), kv + ":t"], L)
            V(tt(PD, pt, T.AB[:, c], OP.min), [kv + ":t", k("AB")], [pd], L)
        A(act(T.PA[:], T.XX[:], AF.Sign), ["XX0", "XX1"], ["PA"])
        PE([mm(T.px[:, 0:16], T.IDM[:], T.KK[:, 0:16], True, False), mm(T.px[:, 0:16], T.ID2[:], T.PA[:], False, True)], ["IDM", "ID2", "KK", "PA"], ["px:g"], 128)
        V(ts(LU[:, 80:96], T.px[:, 0:16], L / 2.0, OP.mult, L + 0.25, OP.add), ["px:g"], ["LG"])
        A(act(PN[:, K:2 * K], PC[:, 0:2 * K].indirect(LU[:, 80:96]), AF.Copy), [pc, "PD%d:0" % par, "PD%d:1" % par, "LG"], [pn], K, G_R)
        if not last:
            A(act(PN[:, 2 * K:3 * K], PN[:, K:2 * K], AF.Copy), [pn], [pn + "b"], K)
            PE([mm(T.px[:, 2 * L:2 * L + 16], T.ONF[:], T.HN[:], True, True)], ["ONF", "HN0", "HN1"], ["px:a"], 256)
            A(lambda: s.activation(out=T.ACT[:], in_=T.px[:, 2 * L:2 * L + 16], func=AF.Copy, accum_out=T.AR[:]), ["px:a"], ["AR", "A0"], 16, 1.0, 140.0)
            A(act(T.ACT[:, 0:1], T.AR[:], AF.Identity, T.PF[:, 12:13], 1.0 / HC), ["AR", "PF12"], ["A0"])
            A(act(T.AQ[:], T.ACT[:, 0:1], AF.Identity, T.PF[:, 15:16], 1.0 / K), ["A0", "PF15"], ["A1"])
            A(act(T.AC[:], T.AQ[:], AF.Identity, T.ACT[:, 0:1], -float(K)), ["A0", "A1"], ["AC"])
    A(act(T.AB[:], T["PC%d" % (RO % 2)][:, K:2 * K], AF.Abs), ["PC%d" % (RO % 2)], ["AB0", "AB1"], K)
    V(ts(T.FC[:], T.AB[:], CM - PV, OP.add), ["AB0", "AB1"], ["FC"], K)
    D("S", dma("S", T.yc[:], T.FC[:]), ["FC"], [])
    A(act(T.SN[:], T["PC%d" % (RO % 2)][:, K:2 * K], AF.Sign), ["PC%d" % (RO % 2)], ["SN"], K)
    PE([mm(T.px[:, K:2 * K], T.BO[:], T.SN[:], True, True)], ["BO", "SN"], ["px:n"], K)
    V(ts(T.FL[:], T.px[:, K:2 * K], -0.5, OP.mult, 8.0, OP.add), ["px:n"], ["FL"], K)
    D("S", dma("S", T.yn[:], T.FL[0:128:16, :]), ["FL"], [])

    lastw, readers, lastb = {}, {}, {}
    N = len(ops)
    deps = [dict() for _ in range(N)]

    def dep(i, j, wait):
        if i != j:
            deps[i][j] = deps[i].get(j, False) or wait

    for i in range(N):
        op = ops[i]
        for r in op["r"]:
            if r in lastw:
                dep(i, lastw[r], True)
            readers.setdefault(r, []).append(i)
        for w in op["w"]:
            if w in lastw:
                dep(i, lastw[w], not (op["q"] == "T" and ops[lastw[w]]["q"] == "T") and not w.startswith("o"))
            for j in readers.get(w, []):
                dep(i, j, True)
            lastw[w] = i
            readers[w] = []
        for b in op["banks"]:
            if b in lastb:
                dep(i, lastb[b], ops[lastb[b]]["q"] != op["q"])
            lastb[b] = i

    if "order" not in ORDER:
        ORDER["order"] = make_order(ops, deps)
    order = ORDER["order"]

    CN = {"V": "cV", "A": "cA", "T": "cT", "G": "cG"}
    count = {q: 0 for q in CN}
    known = {q: {} for q in eng}
    done, clock = {}, {}
    locsum = 0
    for i in order:
        op = ops[i]
        q = op["q"]
        need = {}
        for j, wait in deps[i].items():
            if not wait:
                continue
            oj = ops[j]
            if oj["kind"] == "r" and not any(w in op["r"] or w in op["w"] for w in oj["w"]):
                sem, val, cl = oj["lsem"], oj["amount"], {}
            else:
                sem, val = done[j]
                cl = clock[j] if oj["kind"] != "r" else {}
            if known[q].get(sem, 0) >= val:
                continue
            if sem not in need or need[sem][0] < val:
                need[sem] = (val, cl)
        for sem in sorted(need):
            val, cl = need[sem]
            if any(o2 != sem and need[o2][1].get(sem, 0) >= val and not (cl.get(o2, 0) >= need[o2][0]) for o2 in need):
                continue
            eng[q].wait_ge(T.sem[sem], int(val))
        for sem in need:
            val, cl = need[sem]
            known[q][sem] = max(known[q].get(sem, 0), val)
            for s2 in cl:
                known[q][s2] = max(known[q].get(s2, 0), cl[s2])
        for f in op["fns"]:
            ins = f()
            if op["kind"] == "c":
                ins.then_inc(T.sem[CN[q]], 1)
                count[q] += 1
            elif op["kind"] == "d":
                ins.then_inc(T.sem[op["sem"]], 16)
        if op["kind"] == "c":
            done[i] = (CN[q], count[q])
        else:
            done[i] = (op["sem"], op["amount"])
            if op["kind"] == "r" and "lsem" not in op:
                locsum += n_eng
        clock[i] = dict(known[q])
        clock[i][done[i][0]] = max(clock[i].get(done[i][0], 0), done[i][1])
    for q in CN:
        if count[q]:
            g.wait_ge(T.sem[CN[q]], count[q])
    g.wait_ge(T.sem.loc, locsum)
    for op in ops:
        if op["kind"] in ("d", "r") and known["G"].get(op["sem"], 0) < op["amount"]:
            g.wait_ge(T.sem[op["sem"]], op["amount"])
        if "lsem" in op and known["G"].get(op["lsem"], 0) < n_eng:
            g.wait_ge(T.sem[op["lsem"]], n_eng)
